import numpy as np
import ml_dtypes


def mxq(x, axis, fmt="e4m3"):
    dtype, down = {"e4m3": (ml_dtypes.float8_e4m3fn, 7), "e5m2": (ml_dtypes.float8_e5m2, 14)}[fmt]
    v = np.moveaxis(np.asarray(x, np.float32).astype(ml_dtypes.bfloat16).astype(np.float64), axis, -1)
    blocks = v.reshape(v.shape[:-1] + (-1, 32))
    amax = np.abs(blocks).max(-1, keepdims=True)
    byte = np.maximum(np.where(amax > 0, np.frexp(amax)[1] - 1 + 127, 0) - down, 1)
    scale = np.exp2(byte - 127.0)
    codes = (blocks / scale).astype(np.float32).astype(dtype).astype(np.float64)
    return np.moveaxis((codes * scale).reshape(v.shape), -1, axis)


WIDE = False


def mx_kscale(k):
    if not WIDE:
        return np.ones(k)
    levels = np.array([18, -18])
    if k % 512:
        return np.exp2(np.random.permutation(np.resize(levels, k // 32))).repeat(32)
    a = np.empty((k // 512, 16))
    for p in range(k // 512):
        a[p, :8] = np.random.permutation(np.resize(levels, 8))
        for g in range(8):
            far = levels[np.abs(levels - a[p, g]) >= 10]
            a[p, g + 8] = far[np.random.randint(len(far))]
    return np.exp2(a.ravel()).repeat(32)


def f64(x):
    return np.asarray(x).astype(np.float64)


def striped(idx):
    return np.tile(np.asarray(idx).reshape(-1, 16).T, (8, 1)).astype(np.uint16)


def unstriped(offs):
    return offs[:16].T.reshape(-1).astype(np.int64)


def sig(x):
    return 1.0 / (1.0 + np.exp(-x))


def setup_inputs():
    n = np.random.standard_normal
    uni = np.random.uniform
    order = np.random.permutation(2048)
    idx = order[:512]
    fan = order[512:1024]
    f_d = mx_kscale(512)
    f_i = np.ones(2048)
    f_i[idx] = mx_kscale(512)
    f_j = np.ones(2048)
    f_j[fan] = mx_kscale(512)
    return {
        "vT": (n((512, 2048)) * f_d[:, None] * f_i[None, :] * f_j[None, :]).astype(np.float32),
        "W": (n((512, 512)) / np.sqrt(512) / f_d[:, None]).astype(np.float32),
        "cf": np.tile(uni(0.75, 1.3, 512), (128, 1)).astype(np.float32),
        "tv": np.tile(uni(0.75, 1.3, 2048) / f_i / f_j, (128, 1)).astype(np.float32),
        "offs": striped(idx),
        "foffs": striped(fan),
    }


def reference(vT, W, cf, tv, offs, foffs):
    idx = unstriped(offs)
    fan = unstriped(foffs)
    va = f64(vT)[:, idx]
    vb = f64(vT)[:, fan]
    ta = f64(tv)[:1][:, idx]
    tb = f64(tv)[:1][:, fan]
    tac = ta.T
    tbc = tb.T
    q_W = mxq(f64(W), 0, "e4m3")
    sa = mxq(va, 0, "e4m3").T @ q_W
    ha = tac * sig(tac * f64(cf)[:1] * sa)
    sb = mxq(vb, 0, "e4m3").T @ q_W
    hb = tbc * sig(tbc * f64(cf)[:1] * sb)
    g1 = mxq(va, 1, "e4m3") @ mxq(ha, 0, "e4m3")
    g2 = mxq(vb, 1, "e4m3") @ mxq(hb, 0, "e4m3")
    out = f64(cf)[:1] * (g1 - g2)
    return out

@@ -1,0 +1,224 @@
+from contextlib import ExitStack
+
+import concourse.mybir as mybir
+from concourse.masks import make_identity
+
+F32 = mybir.dt.float32
+BF16 = mybir.dt.bfloat16
+U32 = mybir.dt.uint32
+U16 = mybir.dt.uint16
+U8 = mybir.dt.uint8
+FP8X4 = mybir.dt.float8_e4m3fn_x4
+MULT = mybir.AluOpType.mult
+COPY = mybir.ActivationFunctionType.Copy
+SIGMOID = mybir.ActivationFunctionType.Sigmoid
+
+P = 128
+PACK = 4
+D = 512
+F = 512
+SLOTS = 512
+T = 2048
+HALF = F // 2
+FLOPS = 4 * 2 * D * F * SLOTS
+SCALAR_PLANES = (0,)
+VECTOR_SCALES = ()
+
+
+def tile_attend_grbm_kernel(tc, vT, W, cf, tv, offs, foffs, out):
+    nc = tc.nc
+    with ExitStack() as ctx:
+        keep = ctx.enter_context(tc.tile_pool(name="keep", bufs=1))
+        ring = ctx.enter_context(tc.tile_pool(name="ring", bufs=2))
+        psum2 = ctx.enter_context(tc.psum_pool(name="psum2", bufs=2))
+        psum4 = ctx.enter_context(tc.psum_pool(name="psum4", bufs=4))
+
+        def quantise(name, grouped, width):
+            codes = keep.tile([P, width], U32, name=name + "_codes", align_bytes=64)
+            scales = keep.tile([P, width], U8, name=name + "_scales", align_bytes=64)
+            nc.vector.quantize_mx(out=codes[:].bitcast(FP8X4), scales=scales[:], in_=grouped)
+            return codes, scales
+
+        def weave(ap):
+            return ap.rearrange("p (c i t) -> p c t i", i=4, t=PACK)
+
+        def planar(ap):
+            return ap.rearrange("p (t c i) -> p c t i", i=4, t=PACK)
+
+        lists = []
+        for name, src in (("offs", offs), ("foffs", foffs)):
+            tile = keep.tile([P, SLOTS // 16], U16, name=name + "_sb")
+            nc.sync.dma_start(tile[:], src)
+            lists.append(tile)
+
+        tv_sb = keep.tile([P, T], F32, name="tv_sb")
+        nc.vector.memset(tv_sb[:], 0.0)
+        ident = keep.tile([P, P], F32, name="ident")
+        make_identity(nc, ident[:])
+        warm = keep.tile([P, 1], F32, name="warm")
+        nc.scalar.activation(warm[:], ident[:, 0:1], SIGMOID)
+
+        vT_planes = vT.rearrange("(p t) x -> t p x", t=PACK)
+        planes = []
+        for t in range(PACK):
+            plane = keep.tile([P, T], F32, name="plane%d" % t)
+            nc.sync.dma_start(plane[:], vT_planes[t])
+            planes.append(plane)
+            if t == 0:
+                nc.sync.dma_start(tv_sb[0:1, :], tv[0:1, :])
+        w_rows = W.rearrange("(p t) f -> p t f", t=PACK)
+        w_raw = []
+        cf_sb = keep.tile([P, F], F32, name="cf_sb")
+        for h in range(2):
+            raw = keep.tile([P, PACK, HALF], F32, name="w_raw%d" % h)
+            nc.sync.dma_start(raw[:], w_rows[:, :, h * HALF : (h + 1) * HALF])
+            w_raw.append(raw)
+            if h == 0:
+                nc.sync.dma_start(cf_sb[:], cf)
+
+        t_cols = []
+        t_signed = []
+        for s in range(2):
+            picked = keep.tile([P, SLOTS], F32, name="tv_picked%d" % s)
+            nc.vector.tensor_copy(picked[:], tv_sb[:].indirect(lists[s][:]))
+            bank = psum2.tile([P, PACK, P], F32, name="score")
+            for r in range(PACK):
+                nc.tensor.transpose(bank[:, r, :], picked[:, r::PACK], ident[:])
+            col = keep.tile([P, PACK], F32, name="t_col%d" % s)
+            nc.scalar.copy(col[:], bank[:, :, 0])
+            t_cols.append(col)
+            if s == 0:
+                t_signed.append(col)
+            else:
+                neg = keep.tile([P, PACK], F32, name="t_neg")
+                nc.scalar.activation(neg[:], bank[:, :, 0], COPY, scale=-1.0)
+                t_signed.append(neg)
+
+        gathered = [keep.tile([P, PACK * SLOTS], BF16, name="gathered%d" % s, align_bytes=64) for s in range(2)]
+        turned = [keep.tile([P, PACK * 2 * P], F32, name="turned%d" % s, align_bytes=64) for s in range(2)]
+        windows = {}
+
+        def gather(s, t):
+            dst = gathered[s][:, t * SLOTS : (t + 1) * SLOTS]
+            if t in SCALAR_PLANES:
+                if t not in windows:
+                    windows[t] = keep.tile([P, T], BF16, name="window%d" % t)
+                    nc.scalar.activation(windows[t][:], planes[t][:], COPY)
+                nc.scalar.activation(dst, windows[t][:].indirect(lists[s][:]), COPY)
+            else:
+                nc.vector.tensor_copy(dst, planes[t][:].indirect(lists[s][:]))
+
+        def turn(s, t):
+            words = gathered[s][:, t * SLOTS : (t + 1) * SLOTS].bitcast(F32)
+            bank = psum2.tile([P, 2, P], F32, name="turn")
+            for u in range(2):
+                nc.tensor.transpose(bank[:, u, :], words[:, u::2], ident[:])
+            dst = turned[s][:, t * 2 * P : (t + 1) * 2 * P].rearrange("p (x u) -> p x u", u=2)
+            nc.scalar.copy(dst, bank[:].rearrange("p u x -> p x u"))
+
+        def along_d(s):
+            grouped = keep.tile([P, PACK * SLOTS], BF16, name="x_grouped%d" % s, align_bytes=64)
+            nc.vector.tensor_copy(weave(grouped[:]), planar(gathered[s][:]))
+            return grouped
+
+        def w_group(h):
+            grouped = keep.tile([P, PACK * HALF], BF16, name="w_grouped%d" % h, align_bytes=64)
+            nc.scalar.copy(weave(grouped[:]), planar(w_raw[h][:].rearrange("p t f -> p (t f)")))
+            return grouped
+
+        for t in range(PACK - 1):
+            for s in range(2):
+                gather(s, t)
+            for s in range(2):
+                turn(s, t)
+        gather(0, PACK - 1)
+        xg0 = along_d(0)
+        wg0 = w_group(0)
+        cf_bank = psum2.tile([P, PACK, P], F32, name="score")
+        for j in range(PACK):
+            nc.tensor.transpose(cf_bank[:, j, :], cf_sb[:, j * P : (j + 1) * P], ident[:])
+        cf_col = keep.tile([P, PACK], F32, name="cf_col")
+        nc.scalar.copy(cf_col[:], cf_bank[:, :, 0])
+        w_q = [quantise("w0", wg0[:], HALF)]
+        x_q = [quantise("x0", xg0[:], SLOTS)]
+        wg1 = w_group(1)
+        gather(1, PACK - 1)
+        w_q.append(quantise("w1", wg1[:], HALF))
+        xg1 = along_d(1)
+
+        def hidden(s, j0, nj):
+            width = nj * P
+            per_bank = PACK // nj
+            banks = [psum4.tile([P, per_bank, width], F32, name="logit") for b in range(nj)]
+            for jj in range(nj):
+                j = j0 + jj
+                score = psum2.tile([P, SLOTS], F32, name="score")
+                cols = slice((j % 2) * P, (j % 2 + 1) * P)
+                nc.tensor.matmul_mx(
+                    out=score[:],
+                    lhsT=w_q[j // 2][0][:, cols].bitcast(FP8X4),
+                    lhsT_scale=w_q[j // 2][1][:, cols],
+                    rhs=x_q[s][0][:].bitcast(FP8X4),
+                    rhs_scale=x_q[s][1][:],
+                    start=True,
+                    stop=True,
+                )
+                scaled = ring.tile([P, PACK, P], F32, name="scaled")
+                dealt = score[:].rearrange("p (m r) -> p r m", r=PACK)
+                if (s, j) in VECTOR_SCALES:
+                    nc.vector.tensor_scalar(scaled[:], dealt, cf_col[:, j : j + 1], None, MULT)
+                else:
+                    nc.scalar.activation(scaled[:], dealt, COPY, scale=cf_col[:, j : j + 1])
+                for r in range(PACK):
+                    nc.tensor.transpose(
+                        banks[r // per_bank][:, r % per_bank, jj * P : (jj + 1) * P], scaled[:, r, :], ident[:]
+                    )
+            sig = ring.tile([P, PACK * width], F32, name="sig", bufs=3)
+            for r in range(PACK):
+                nc.scalar.activation(
+                    sig[:, r * width : (r + 1) * width],
+                    banks[r // per_bank][:, r % per_bank, :],
+                    SIGMOID,
+                    scale=t_cols[s][:, r : r + 1],
+                )
+            grouped = ring.tile([P, PACK * width], BF16, name="h_grouped", align_bytes=64)
+            factor = t_signed[s][:].rearrange("p (c t i) -> p c t i", c=1, i=1).to_broadcast([P, width // 4, PACK, 4])
+            nc.vector.tensor_tensor(weave(grouped[:]), planar(sig[:]), factor, MULT)
+            return grouped
+
+        h_a = []
+        hg = hidden(0, 0, 2)
+        x_q.append(quantise("x1", xg1[:], SLOTS))
+        turn(0, PACK - 1)
+        turn(1, PACK - 1)
+        h_a.append(quantise("ha0", hg[:], HALF))
+        y_q = [quantise("y%d" % s, turned[s][:].bitcast(BF16), D) for s in range(2)]
+        hg = hidden(0, 2, 2)
+        h_a.append(quantise("ha1", hg[:], HALF))
+
+        out_rows = out.rearrange("(p t) f -> p t f", t=PACK)
+        for j0, nj in ((0, 2), (2, 1), (3, 1)):
+            width = nj * P
+            hg = hidden(1, j0, nj)
+            h_b = quantise("hb%d" % j0, hg[:], width)
+            a_cols = slice((j0 % 2) * P, (j0 % 2) * P + width)
+            moving = [(h_a[j0 // 2][0][:, a_cols], h_a[j0 // 2][1][:, a_cols]), (h_b[0][:], h_b[1][:])]
+            fcols = slice(j0 * P, j0 * P + width)
+            for pair in range(2):
+                acc = psum2.tile([P, 2, width], F32, name="turn")
+                for e in range(2):
+                    t = 2 * pair + e
+                    for s in range(2):
+                        nc.tensor.matmul_mx(
+                            out=acc[:, e, :],
+                            lhsT=y_q[s][0][:, t * P : (t + 1) * P].bitcast(FP8X4),
+                            lhsT_scale=y_q[s][1][:, t * P : (t + 1) * P],
+                            rhs=moving[s][0].bitcast(FP8X4),
+                            rhs_scale=moving[s][1],
+                            start=(s == 0),
+                            stop=(s == 1),
+                        )
+                result = keep.tile([P, 2, width], F32, name="result%d%d" % (j0, pair))
+                scale = cf_sb[:, fcols].rearrange("p (e f) -> p e f", e=1).to_broadcast([P, 2, width])
+                nc.vector.tensor_tensor(result[:], acc[:], scale, MULT)
+                nc.sync.dma_start(out_rows[:, 2 * pair : 2 * pair + 2, fcols], result[:])

@@ -21,7 +21,6 @@ SLOTS = 512
 T = 2048
 HALF = F // 2
 FLOPS = 4 * 2 * D * F * SLOTS
-SCALAR_PLANES = (0,)
 VECTOR_SCALES = ()
 
 
@@ -45,14 +44,14 @@ def tile_attend_grbm_kernel(tc, vT, W, cf, tv, offs, foffs, out):
         def planar(ap):
             return ap.rearrange("p (t c i) -> p c t i", i=4, t=PACK)
 
+        tv_sb = keep.tile([P, T], F32, name="tv_sb")
+        nc.vector.memset(tv_sb[: P - 1, :], 0.0)
+        nc.sync.dma_start(tv_sb[P - 1 :, :], tv[0:1, :])
         lists = []
         for name, src in (("offs", offs), ("foffs", foffs)):
             tile = keep.tile([P, SLOTS // 16], U16, name=name + "_sb")
             nc.sync.dma_start(tile[:], src)
             lists.append(tile)
-
-        tv_sb = keep.tile([P, T], F32, name="tv_sb")
-        nc.vector.memset(tv_sb[:], 0.0)
         ident = keep.tile([P, P], F32, name="ident")
         make_identity(nc, ident[:])
         warm = keep.tile([P, 1], F32, name="warm")
@@ -64,8 +63,6 @@ def tile_attend_grbm_kernel(tc, vT, W, cf, tv, offs, foffs, out):
             plane = keep.tile([P, T], F32, name="plane%d" % t)
             nc.sync.dma_start(plane[:], vT_planes[t])
             planes.append(plane)
-            if t == 0:
-                nc.sync.dma_start(tv_sb[0:1, :], tv[0:1, :])
         w_rows = W.rearrange("(p t) f -> p t f", t=PACK)
         w_raw = []
         cf_sb = keep.tile([P, F], F32, name="cf_sb")
@@ -79,70 +76,76 @@ def tile_attend_grbm_kernel(tc, vT, W, cf, tv, offs, foffs, out):
         t_cols = []
         t_signed = []
         for s in range(2):
-            picked = keep.tile([P, SLOTS], F32, name="tv_picked%d" % s)
-            nc.vector.tensor_copy(picked[:], tv_sb[:].indirect(lists[s][:]))
+            tv_picked = keep.tile([P, SLOTS], F32, name="tv_picked%d" % s)
+            nc.vector.tensor_copy(tv_picked[:], tv_sb[:].indirect(lists[s][:]))
             bank = psum2.tile([P, PACK, P], F32, name="score")
             for r in range(PACK):
-                nc.tensor.transpose(bank[:, r, :], picked[:, r::PACK], ident[:])
+                nc.tensor.transpose(bank[:, r, :], tv_picked[:, r::PACK], ident[:])
             col = keep.tile([P, PACK], F32, name="t_col%d" % s)
-            nc.scalar.copy(col[:], bank[:, :, 0])
+            nc.scalar.copy(col[:], bank[:, :, P - 1])
             t_cols.append(col)
             if s == 0:
                 t_signed.append(col)
             else:
                 neg = keep.tile([P, PACK], F32, name="t_neg")
-                nc.scalar.activation(neg[:], bank[:, :, 0], COPY, scale=-1.0)
+                nc.scalar.activation(neg[:], bank[:, :, P - 1], COPY, scale=-1.0)
                 t_signed.append(neg)
 
-        gathered = [keep.tile([P, PACK * SLOTS], BF16, name="gathered%d" % s, align_bytes=64) for s in range(2)]
-        turned = [keep.tile([P, PACK * 2 * P], F32, name="turned%d" % s, align_bytes=64) for s in range(2)]
-        windows = {}
-
         def gather(s, t):
-            dst = gathered[s][:, t * SLOTS : (t + 1) * SLOTS]
-            if t in SCALAR_PLANES:
-                if t not in windows:
-                    windows[t] = keep.tile([P, T], BF16, name="window%d" % t)
-                    nc.scalar.activation(windows[t][:], planes[t][:], COPY)
-                nc.scalar.activation(dst, windows[t][:].indirect(lists[s][:]), COPY)
-            else:
-                nc.vector.tensor_copy(dst, planes[t][:].indirect(lists[s][:]))
+            nc.vector.tensor_copy(picked[s][:, t * SLOTS : (t + 1) * SLOTS], planes[t][:].indirect(lists[s][:]))
 
-        def turn(s, t):
-            words = gathered[s][:, t * SLOTS : (t + 1) * SLOTS].bitcast(F32)
-            bank = psum2.tile([P, 2, P], F32, name="turn")
-            for u in range(2):
-                nc.tensor.transpose(bank[:, u, :], words[:, u::2], ident[:])
-            dst = turned[s][:, t * 2 * P : (t + 1) * 2 * P].rearrange("p (x u) -> p x u", u=2)
-            nc.scalar.copy(dst, bank[:].rearrange("p u x -> p x u"))
+        turned = keep.tile([P, 2 * PACK * 2 * P], F32, name="turned", align_bytes=64)
+
+        def turn(items, dst):
+            bank = psum2.tile([P, 2, 2, P], F32, name="turn")
+            for e, (s, t) in enumerate(items):
+                words = picked[s][:, t * SLOTS : (t + 1) * SLOTS].bitcast(F32)
+                for u in range(2):
+                    nc.tensor.transpose(bank[:, e, u, :], words[:, u::2], ident[:])
+            nc.scalar.copy(dst, bank[:].rearrange("p e u x -> p e x u"))
+
+        def turn_planes(s, t0):
+            dst = turned[:].rearrange("p (s t x u) -> p s t x u", s=2, t=PACK, u=2)[:, s, t0 : t0 + 2]
+            turn(((s, t0), (s, t0 + 1)), dst)
+
+        def turn_lists(t):
+            dst = turned[:].rearrange("p (s t x u) -> p t s x u", s=2, t=PACK, u=2)[:, t]
+            turn(((0, t), (1, t)), dst)
 
         def along_d(s):
             grouped = keep.tile([P, PACK * SLOTS], BF16, name="x_grouped%d" % s, align_bytes=64)
-            nc.vector.tensor_copy(weave(grouped[:]), planar(gathered[s][:]))
+            nc.vector.tensor_copy(weave(grouped[:]), planar(picked[s][:, : PACK * SLOTS]))
             return grouped
 
-        def w_group(h):
-            grouped = keep.tile([P, PACK * HALF], BF16, name="w_grouped%d" % h, align_bytes=64)
-            nc.scalar.copy(weave(grouped[:]), planar(w_raw[h][:].rearrange("p t f -> p (t f)")))
-            return grouped
+        def w_group(h, grouped):
+            nc.scalar.copy(weave(grouped), planar(w_raw[h][:].rearrange("p t f -> p (t f)")))
 
-        for t in range(PACK - 1):
-            for s in range(2):
-                gather(s, t)
-            for s in range(2):
-                turn(s, t)
-        gather(0, PACK - 1)
+        picked = [keep.tile([P, (PACK + s) * SLOTS], BF16, name="picked%d" % s, align_bytes=64) for s in range(2)]
+        window = keep.tile([P, T], BF16, name="window")
+        nc.scalar.activation(window[:], planes[0][:], COPY)
+        nc.scalar.activation(picked[1][:, :SLOTS], window[:].indirect(lists[1][:]), COPY)
+        gather(0, 0)
+        gather(0, 1)
+        gather(1, 1)
+        turn_planes(0, 0)
+        turn_planes(1, 0)
+        gather(0, 2)
+        gather(1, 2)
+        turn_lists(2)
+        gather(0, 3)
         xg0 = along_d(0)
-        wg0 = w_group(0)
+        wg0 = picked[1][:, (PACK - 1) * SLOTS :]
+        w_group(0, wg0)
         cf_bank = psum2.tile([P, PACK, P], F32, name="score")
         for j in range(PACK):
             nc.tensor.transpose(cf_bank[:, j, :], cf_sb[:, j * P : (j + 1) * P], ident[:])
         cf_col = keep.tile([P, PACK], F32, name="cf_col")
         nc.scalar.copy(cf_col[:], cf_bank[:, :, 0])
-        w_q = [quantise("w0", wg0[:], HALF)]
+        w_q = [quantise("w0", wg0, HALF)]
         x_q = [quantise("x0", xg0[:], SLOTS)]
-        wg1 = w_group(1)
-        gather(1, PACK - 1)
+        wg1 = keep.tile([P, PACK * HALF], BF16, name="w_grouped1", align_bytes=64)
+        w_group(1, wg1[:])
+        gather(1, 3)
         w_q.append(quantise("w1", wg1[:], HALF))
         xg1 = along_d(1)
 
@@ -173,7 +176,7 @@ def tile_attend_grbm_kernel(tc, vT, W, cf, tv, offs, foffs, out):
                     nc.tensor.transpose(
                         banks[r // per_bank][:, r % per_bank, jj * P : (jj + 1) * P], scaled[:, r, :], ident[:]
                     )
-            sig = ring.tile([P, PACK * width], F32, name="sig", bufs=3)
+            sig = ring.tile([P, PACK * width], F32, name="sig", bufs=4)
             for r in range(PACK):
                 nc.scalar.activation(
                     sig[:, r * width : (r + 1) * width],
@@ -181,31 +184,29 @@ def tile_attend_grbm_kernel(tc, vT, W, cf, tv, offs, foffs, out):
                     SIGMOID,
                     scale=t_cols[s][:, r : r + 1],
                 )
+            return sig
+
+        def weigh(s, sig, width, on_scalar=False):
+            rounded = ring.tile([P, PACK * width], BF16, name="h_planes")
+            for r in range(PACK):
+                cols = slice(r * width, (r + 1) * width)
+                if on_scalar:
+                    nc.scalar.activation(rounded[:, cols], sig[:, cols], COPY, scale=t_signed[s][:, r : r + 1])
+                else:
+                    nc.vector.tensor_scalar(rounded[:, cols], sig[:, cols], t_signed[s][:, r : r + 1], None, MULT)
             grouped = ring.tile([P, PACK * width], BF16, name="h_grouped", align_bytes=64)
-            factor = t_signed[s][:].rearrange("p (c t i) -> p c t i", c=1, i=1).to_broadcast([P, width // 4, PACK, 4])
-            nc.vector.tensor_tensor(weave(grouped[:]), planar(sig[:]), factor, MULT)
+            nc.vector.tensor_copy(weave(grouped[:]), planar(rounded[:]))
             return grouped
 
-        h_a = []
-        hg = hidden(0, 0, 2)
-        x_q.append(quantise("x1", xg1[:], SLOTS))
-        turn(0, PACK - 1)
-        turn(1, PACK - 1)
-        h_a.append(quantise("ha0", hg[:], HALF))
-        y_q = [quantise("y%d" % s, turned[s][:].bitcast(BF16), D) for s in range(2)]
-        hg = hidden(0, 2, 2)
-        h_a.append(quantise("ha1", hg[:], HALF))
-
         out_rows = out.rearrange("(p t) f -> p t f", t=PACK)
-        for j0, nj in ((0, 2), (2, 1), (3, 1)):
+
+        def finish(j0, nj, h_b, pool, tag):
             width = nj * P
-            hg = hidden(1, j0, nj)
-            h_b = quantise("hb%d" % j0, hg[:], width)
             a_cols = slice((j0 % 2) * P, (j0 % 2) * P + width)
             moving = [(h_a[j0 // 2][0][:, a_cols], h_a[j0 // 2][1][:, a_cols]), (h_b[0][:], h_b[1][:])]
             fcols = slice(j0 * P, j0 * P + width)
             for pair in range(2):
-                acc = psum2.tile([P, 2, width], F32, name="turn")
+                acc = pool.tile([P, 2, width], F32, name=tag)
                 for e in range(2):
                     t = 2 * pair + e
                     for s in range(2):
@@ -222,3 +223,18 @@ def tile_attend_grbm_kernel(tc, vT, W, cf, tv, offs, foffs, out):
                 scale = cf_sb[:, fcols].rearrange("p (e f) -> p e f", e=1).to_broadcast([P, 2, width])
                 nc.vector.tensor_tensor(result[:], acc[:], scale, MULT)
                 nc.sync.dma_start(out_rows[:, 2 * pair : 2 * pair + 2, fcols], result[:])
+
+        h_a = []
+        sig = hidden(0, 0, 2)
+        x_q.append(quantise("x1", xg1[:], SLOTS))
+        turn_lists(3)
+        h_a.append(quantise("ha0", weigh(0, sig, HALF, True)[:], HALF))
+        sig = hidden(1, 0, 2)
+        y_q = [quantise("y%d" % s, turned[:, s * 2 * D : (s + 1) * 2 * D].bitcast(BF16), D) for s in range(2)]
+        h_b0 = quantise("hb0", weigh(1, sig, HALF)[:], HALF)
+        sig = hidden(0, 2, 2)
+        finish(0, 2, h_b0, psum2, "turn")
+        h_a.append(quantise("ha1", weigh(0, sig, HALF)[:], HALF))
+        sigs = [hidden(1, j, 1) for j in (2, 3)]
+        finish(2, 1, quantise("hb2", weigh(1, sigs[0], P)[:], P), psum2, "score")
+        finish(3, 1, quantise("hb3", weigh(1, sigs[1], P, True)[:], P), psum4, "logit")

@@ -114,7 +114,13 @@ def tile_attend_grbm_kernel(tc, vT, W, cf, tv, offs, foffs, out):
 
         def along_d(s):
             grouped = keep.tile([P, PACK * SLOTS], BF16, name="x_grouped%d" % s, align_bytes=64)
-            nc.vector.tensor_copy(weave(grouped[:]), planar(picked[s][:, : PACK * SLOTS]))
+            if s == 0:
+                nc.vector.tensor_copy(weave(grouped[:]), planar(picked[s][:]))
+            else:
+                nc.vector.tensor_copy(
+                    grouped[:].rearrange("p (r k m t) -> p k r m t", r=PACK, m=2, t=PACK),
+                    picked[s][:, : PACK * SLOTS].rearrange("p (t k m r) -> p k r m t", t=PACK, m=2, r=PACK),
+                )
             return grouped
 
         def w_group(h, grouped):
@@ -186,29 +192,61 @@ def tile_attend_grbm_kernel(tc, vT, W, cf, tv, offs, foffs, out):
                 )
             return sig
 
+        def hidden_b(j0, nj):
+            width = nj * P
+            per_bank = PACK // nj
+            cols = slice((j0 % 2) * P, (j0 % 2) * P + width)
+            scaled = ring.tile([P, PACK * width], F32, name="scaled_b", bufs=3)
+            factor = cf_sb[:, j0 * P : j0 * P + width].rearrange("p (e f) -> p e f", e=1).to_broadcast([P, per_bank, width])
+            for b in range(nj):
+                bank = psum2.tile([P, per_bank, width], F32, name="score")
+                for e in range(per_bank):
+                    r = b * per_bank + e
+                    nc.tensor.matmul_mx(
+                        out=bank[:, e, :],
+                        lhsT=x_q[1][0][:, r * P : (r + 1) * P].bitcast(FP8X4),
+                        lhsT_scale=x_q[1][1][:, r * P : (r + 1) * P],
+                        rhs=w_q[j0 // 2][0][:, cols].bitcast(FP8X4),
+                        rhs_scale=w_q[j0 // 2][1][:, cols],
+                        start=True,
+                        stop=True,
+                    )
+                dst = scaled[:, b * per_bank * width : (b + 1) * per_bank * width].rearrange("p (e f) -> p e f", e=per_bank)
+                nc.vector.tensor_tensor(dst, bank[:], factor, MULT)
+            sig = ring.tile([P, PACK * width], F32, name="sig", bufs=4)
+            for r in range(PACK):
+                run = slice(r * width, (r + 1) * width)
+                nc.scalar.activation(sig[:, run], scaled[:, run], SIGMOID, scale=t_cols[1][:, r : r + 1])
+            return sig
+
         def weigh(s, sig, width, on_scalar=False):
-            rounded = ring.tile([P, PACK * width], BF16, name="h_planes")
+            rounded = ring.tile([P, PACK * width], BF16, name="h_planes", bufs=5)
             for r in range(PACK):
                 cols = slice(r * width, (r + 1) * width)
                 if on_scalar:
                     nc.scalar.activation(rounded[:, cols], sig[:, cols], COPY, scale=t_signed[s][:, r : r + 1])
                 else:
                     nc.vector.tensor_scalar(rounded[:, cols], sig[:, cols], t_signed[s][:, r : r + 1], None, MULT)
-            grouped = ring.tile([P, PACK * width], BF16, name="h_grouped", align_bytes=64)
-            nc.vector.tensor_copy(weave(grouped[:]), planar(rounded[:]))
+            grouped = ring.tile([P, PACK * width], BF16, name="h_grouped", align_bytes=64, bufs=5)
+            copy = nc.scalar.copy if width == P else nc.vector.tensor_copy
+            copy(weave(grouped[:]), planar(rounded[:]))
             return grouped
 
         out_rows = out.rearrange("(p t) f -> p t f", t=PACK)
 
-        def finish(j0, nj, h_b, pool, tag):
+        def finish(j0, nj, h_b, homes):
             width = nj * P
+            per_bank = PACK // len(homes)
             a_cols = slice((j0 % 2) * P, (j0 % 2) * P + width)
             moving = [(h_a[j0 // 2][0][:, a_cols], h_a[j0 // 2][1][:, a_cols]), (h_b[0][:], h_b[1][:])]
             fcols = slice(j0 * P, j0 * P + width)
-            for pair in range(2):
-                acc = pool.tile([P, 2, width], F32, name=tag)
-                for e in range(2):
-                    t = 2 * pair + e
+            factor = cf_sb[:, fcols].rearrange("p (e f) -> p e f", e=1).to_broadcast([P, per_bank, width])
+            results = [keep.tile([P, 2, width], F32, name="result%d%d" % (j0, pair)) for pair in range(2)]
+            for b, (pool, tag) in enumerate(homes):
+                acc = pool.tile([P, per_bank, width], F32, name=tag)
+                t0 = b * per_bank
+                for e in range(per_bank):
+                    t = t0 + e
                     for s in range(2):
                         nc.tensor.matmul_mx(
                             out=acc[:, e, :],
@@ -219,22 +257,27 @@ def tile_attend_grbm_kernel(tc, vT, W, cf, tv, offs, foffs, out):
                             start=(s == 0),
                             stop=(s == 1),
                         )
-                result = keep.tile([P, 2, width], F32, name="result%d%d" % (j0, pair))
-                scale = cf_sb[:, fcols].rearrange("p (e f) -> p e f", e=1).to_broadcast([P, 2, width])
-                nc.vector.tensor_tensor(result[:], acc[:], scale, MULT)
-                nc.sync.dma_start(out_rows[:, 2 * pair : 2 * pair + 2, fcols], result[:])
+                nc.vector.tensor_tensor(results[t0 // 2][:, t0 % 2 : t0 % 2 + per_bank, :], acc[:], factor, MULT)
+                if (t0 + per_bank) % 2 == 0:
+                    pair = t0 // 2
+                    nc.sync.dma_start(out_rows[:, 2 * pair : 2 * pair + 2, fcols], results[pair][:])
 
         h_a = []
-        sig = hidden(0, 0, 2)
+        sig_a0 = hidden(0, 0, 2)
         x_q.append(quantise("x1", xg1[:], SLOTS))
+        sig_a1 = hidden(0, 2, 2)
         turn_lists(3)
-        h_a.append(quantise("ha0", weigh(0, sig, HALF, True)[:], HALF))
-        sig = hidden(1, 0, 2)
+        sig_b0 = hidden_b(0, 2)
+        grouped_b0 = weigh(1, sig_b0, HALF, True)
+        h_a.append(quantise("ha0", weigh(0, sig_a0, HALF)[:], HALF))
         y_q = [quantise("y%d" % s, turned[:, s * 2 * D : (s + 1) * 2 * D].bitcast(BF16), D) for s in range(2)]
-        h_b0 = quantise("hb0", weigh(1, sig, HALF)[:], HALF)
-        sig = hidden(0, 2, 2)
-        finish(0, 2, h_b0, psum2, "turn")
-        h_a.append(quantise("ha1", weigh(0, sig, HALF)[:], HALF))
-        sigs = [hidden(1, j, 1) for j in (2, 3)]
-        finish(2, 1, quantise("hb2", weigh(1, sigs[0], P)[:], P), psum2, "score")
-        finish(3, 1, quantise("hb3", weigh(1, sigs[1], P, True)[:], P), psum4, "logit")
+        h_b0 = quantise("hb0", grouped_b0[:], HALF)
+        grouped_a1 = weigh(0, sig_a1, HALF, True)
+        sig_b2 = hidden_b(2, 1)
+        h_a.append(quantise("ha1", grouped_a1[:], HALF))
+        grouped_b2 = weigh(1, sig_b2, P, True)
+        sig_b3 = hidden_b(3, 1)
+        grouped_b3 = weigh(1, sig_b3, P, True)
+        finish(0, 2, h_b0, ((psum2, "turn"), (psum2, "turn"), (psum4, "logit"), (psum4, "logit")))
+        finish(2, 1, quantise("hb2", grouped_b2[:], P), ((psum4, "logit"), (psum4, "logit")))
+        finish(3, 1, quantise("hb3", grouped_b3[:], P), ((psum2, "score"), (psum2, "score")))

@@ -20,23 +20,43 @@ F = 512
 SLOTS = 512
 T = 2048
 HALF = F // 2
+W_PIECES = ((0, 128), (128, 128), (256, 256))
 FLOPS = 4 * 2 * D * F * SLOTS
-VECTOR_SCALES = ()
 
 
 def tile_attend_grbm_kernel(tc, vT, W, cf, tv, offs, foffs, out):
     nc = tc.nc
     with ExitStack() as ctx:
         keep = ctx.enter_context(tc.tile_pool(name="keep", bufs=1))
-        ring = ctx.enter_context(tc.tile_pool(name="ring", bufs=2))
-        psum2 = ctx.enter_context(tc.psum_pool(name="psum2", bufs=2))
-        psum4 = ctx.enter_context(tc.psum_pool(name="psum4", bufs=4))
+        psum = ctx.enter_context(tc.psum_pool(name="psum", bufs=1))
+        shared = ctx.enter_context(tc.tile_pool(name="shared", bufs=1))
 
-        def quantise(name, grouped, width):
-            codes = keep.tile([P, width], U32, name=name + "_codes", align_bytes=64)
+        def on_plane(t, name, shape, dtype, byte=0):
+            return shared.tile(shape, dtype, name=name, offset=t * T * 4 + byte, align_bytes=64)
+
+        def on_w(f0, name, shape, dtype):
+            return shared.tile(shape, dtype, name=name, offset=PACK * T * 4 + f0 * PACK * 4, align_bytes=64)
+
+        def bank(b, name, shape):
+            return psum.tile(shape, F32, name=name, tag="bank%d" % b)
+
+        def quantise(name, grouped, width, codes=None):
+            if codes is None:
+                codes = keep.tile([P, width], U32, name=name + "_codes", align_bytes=64)
             scales = keep.tile([P, width], U8, name=name + "_scales", align_bytes=64)
             nc.vector.quantize_mx(out=codes[:].bitcast(FP8X4), scales=scales[:], in_=grouped)
             return codes, scales
+
+        def product(acc, stationary, s_cols, moving, m_cols, start=True, stop=True):
+            nc.tensor.matmul_mx(
+                out=acc,
+                lhsT=stationary[0][:, s_cols].bitcast(FP8X4),
+                lhsT_scale=stationary[1][:, s_cols],
+                rhs=moving[0][:, m_cols].bitcast(FP8X4),
+                rhs_scale=moving[1][:, m_cols],
+                start=start,
+                stop=stop,
+            )
 
         def weave(ap):
             return ap.rearrange("p (c i t) -> p c t i", i=4, t=PACK)
@@ -45,239 +65,231 @@ def tile_attend_grbm_kernel(tc, vT, W, cf, tv, offs, foffs, out):
             return ap.rearrange("p (t c i) -> p c t i", i=4, t=PACK)
 
         tv_sb = keep.tile([P, T], F32, name="tv_sb")
-        nc.vector.memset(tv_sb[: P - 1, :], 0.0)
-        nc.sync.dma_start(tv_sb[P - 1 :, :], tv[0:1, :])
+        nc.scalar.dma_start(tv_sb[P - 1 :, :], tv[0:1, :])
         lists = []
         for name, src in (("offs", offs), ("foffs", foffs)):
             tile = keep.tile([P, SLOTS // 16], U16, name=name + "_sb")
             nc.sync.dma_start(tile[:], src)
             lists.append(tile)
+        cf_row = keep.tile([P, F], F32, name="cf_row")
+        nc.scalar.dma_start(cf_row[P - 1 :, :], cf[0:1, :])
+        nc.vector.memset(tv_sb[: P - 1, :], 0.0)
         ident = keep.tile([P, P], F32, name="ident")
         make_identity(nc, ident[:])
+        nc.gpsimd.memset(cf_row[: P - 1, :], 0.0)
         warm = keep.tile([P, 1], F32, name="warm")
-        nc.scalar.activation(warm[:], ident[:, 0:1], SIGMOID)
-
+        nc.scalar.activation(warm[:64, :], tv_sb[:64, 0:1], SIGMOID)
         vT_planes = vT.rearrange("(p t) x -> t p x", t=PACK)
         planes = []
         for t in range(PACK):
-            plane = keep.tile([P, T], F32, name="plane%d" % t)
+            plane = on_plane(t, "plane%d" % t, [P, T], F32)
             nc.sync.dma_start(plane[:], vT_planes[t])
             planes.append(plane)
         w_rows = W.rearrange("(p t) f -> p t f", t=PACK)
         w_raw = []
-        cf_sb = keep.tile([P, F], F32, name="cf_sb")
-        for h in range(2):
-            raw = keep.tile([P, PACK, HALF], F32, name="w_raw%d" % h)
-            nc.sync.dma_start(raw[:], w_rows[:, :, h * HALF : (h + 1) * HALF])
+        for h, (f0, width) in enumerate(W_PIECES):
+            raw = on_w(f0, "w_raw%d" % h, [P, PACK, width], F32)
+            nc.sync.dma_start(raw[:], w_rows[:, :, f0 : f0 + width])
             w_raw.append(raw)
-            if h == 0:
-                nc.sync.dma_start(cf_sb[:], cf)
+        cf_sb = keep.tile([P, F], F32, name="cf_sb")
+        nc.sync.dma_start(cf_sb[:], cf)
 
-        t_cols = []
-        t_signed = []
+        cf_bank = bank(0, "cf_bank", [P, PACK, P])
+        for j in range(PACK):
+            nc.tensor.transpose(cf_bank[:, j, :], cf_row[:, j * P : (j + 1) * P], ident[:])
+
+        tv_picked = [keep.tile([P, SLOTS], F32, name="tv_picked%d" % s) for s in range(2)]
+        nc.vector.tensor_copy(tv_picked[0][:], tv_sb[:].indirect(lists[0][:]))
+        nc.scalar.activation(tv_picked[1][:], tv_sb[:].indirect(lists[1][:]), COPY)
+        t_banks = []
         for s in range(2):
-            tv_picked = keep.tile([P, SLOTS], F32, name="tv_picked%d" % s)
-            nc.vector.tensor_copy(tv_picked[:], tv_sb[:].indirect(lists[s][:]))
-            bank = psum2.tile([P, PACK, P], F32, name="score")
+            t_bank = bank(1 + s, "t_bank%d" % s, [P, PACK, P])
             for r in range(PACK):
-                nc.tensor.transpose(bank[:, r, :], tv_picked[:, r::PACK], ident[:])
-            col = keep.tile([P, PACK], F32, name="t_col%d" % s)
-            nc.scalar.copy(col[:], bank[:, :, P - 1])
-            t_cols.append(col)
-            if s == 0:
-                t_signed.append(col)
-            else:
-                neg = keep.tile([P, PACK], F32, name="t_neg")
-                nc.scalar.activation(neg[:], bank[:, :, P - 1], COPY, scale=-1.0)
-                t_signed.append(neg)
+                nc.tensor.transpose(t_bank[:, r, :], tv_picked[s][:, r::PACK], ident[:])
+            t_banks.append(t_bank)
 
-        def gather(s, t):
-            nc.vector.tensor_copy(picked[s][:, t * SLOTS : (t + 1) * SLOTS], planes[t][:].indirect(lists[s][:]))
+        picked = [
+            [keep.tile([P, 2 * SLOTS], BF16, name="picked%d%d" % (s, u), align_bytes=64) for u in range(2)]
+            for s in range(2)
+        ]
 
-        turned = keep.tile([P, 2 * PACK * 2 * P], F32, name="turned", align_bytes=64)
+        def picked_plane(s, t):
+            return picked[s][t // 2][:, (t % 2) * SLOTS : (t % 2 + 1) * SLOTS]
 
-        def turn(items, dst):
-            bank = psum2.tile([P, 2, 2, P], F32, name="turn")
-            for e, (s, t) in enumerate(items):
-                words = picked[s][:, t * SLOTS : (t + 1) * SLOTS].bitcast(F32)
+        def gather(t):
+            nc.vector.tensor_copy(picked_plane(0, t), planes[t][:].indirect(lists[0][:]))
+            nc.scalar.activation(picked_plane(1, t), planes[t][:].indirect(lists[1][:]), COPY)
+
+        def weave_pair(s, u):
+            nc.vector.tensor_copy(
+                grouped_x[s][:].rearrange("p (r k m t) -> p k r m t", r=PACK, m=2, t=PACK)[:, :, :, :, 2 * u : 2 * u + 2],
+                picked[s][u][:].rearrange("p (t k m r) -> p k r m t", t=2, m=2, r=PACK),
+            )
+
+        def turn(t, b):
+            y_bank = bank(b, "y_bank%d" % t, [P, 2, 2, P])
+            for s in range(2):
+                words = picked_plane(s, t).bitcast(F32)
                 for u in range(2):
-                    nc.tensor.transpose(bank[:, e, u, :], words[:, u::2], ident[:])
-            nc.scalar.copy(dst, bank[:].rearrange("p e u x -> p e x u"))
+                    nc.tensor.transpose(y_bank[:, s, u, :], words[:, u::2], ident[:])
+            return y_bank
 
-        def turn_planes(s, t0):
-            dst = turned[:].rearrange("p (s t x u) -> p s t x u", s=2, t=PACK, u=2)[:, s, t0 : t0 + 2]
-            turn(((s, t0), (s, t0 + 1)), dst)
+        def empty_turn(y_bank, turned):
+            nc.scalar.copy(turned[:].rearrange("p (s x u) -> p s x u", s=2, u=2), y_bank[:].rearrange("p s u x -> p s x u"))
+            return turned
 
-        def turn_lists(t):
-            dst = turned[:].rearrange("p (s t x u) -> p t s x u", s=2, t=PACK, u=2)[:, t]
-            turn(((0, t), (1, t)), dst)
+        def quantise_turn(t, turned, codes=None):
+            return quantise("y%d" % t, turned[:].bitcast(BF16), 2 * P, codes)
 
-        def along_d(s):
-            grouped = keep.tile([P, PACK * SLOTS], BF16, name="x_grouped%d" % s, align_bytes=64)
-            if s == 0:
-                nc.vector.tensor_copy(weave(grouped[:]), planar(picked[s][:]))
-            else:
-                nc.vector.tensor_copy(
-                    grouped[:].rearrange("p (r k m t) -> p k r m t", r=PACK, m=2, t=PACK),
-                    picked[s][:, : PACK * SLOTS].rearrange("p (t k m r) -> p k r m t", t=PACK, m=2, r=PACK),
-                )
+        words = [P, 2 * 2 * P]
+        y_q = []
+        gather(0)
+        t_all = on_plane(0, "t_all", [P, 4, PACK], F32)
+        for s in range(2):
+            nc.vector.tensor_copy(t_all[:, s, :], t_banks[s][:, :, P - 1])
+        nc.vector.tensor_scalar(t_all[:, 2, :], t_banks[1][:, :, P - 1], -1.0, None, MULT)
+        nc.vector.tensor_copy(t_all[:, 3, :], cf_bank[:, :, P - 1])
+        cf_col = t_all[:, 3, :]
+        t_cols = [t_all[:, 0, :], t_all[:, 1, :]]
+        t_signed = [t_all[:, 0, :], t_all[:, 2, :]]
+        y_bank0 = turn(0, 3)
+        gather(1)
+        y_bank1 = turn(1, 4)
+        turned0 = empty_turn(y_bank0, on_plane(1, "turned0", words, F32))
+        grouped_x = [keep.tile([P, PACK * SLOTS], BF16, name="x_grouped0", align_bytes=64)]
+        weave_pair(0, 0)
+        gather(2)
+        y_bank2 = turn(2, 5)
+        turned1 = empty_turn(y_bank1, on_plane(2, "turned1", words, F32))
+        grouped_x.append(on_plane(2, "x_grouped1", [P, PACK * SLOTS], BF16, 2048))
+        weave_pair(1, 0)
+        gather(3)
+
+        w_codes = keep.tile([P, F], U32, name="w_codes", align_bytes=64)
+        w_scales = keep.tile([P, F], U8, name="w_scales", align_bytes=64)
+        w_q = (w_codes, w_scales)
+
+        def w_group(h):
+            grouped = keep.tile([P, PACK * W_PIECES[h][1]], BF16, name="w_grouped%d" % h, align_bytes=64)
+            nc.scalar.copy(weave(grouped[:]), planar(w_raw[h][:].rearrange("p t f -> p (t f)")))
             return grouped
 
-        def w_group(h, grouped):
-            nc.scalar.copy(weave(grouped), planar(w_raw[h][:].rearrange("p t f -> p (t f)")))
+        def w_quantise(h):
+            cols = slice(W_PIECES[h][0], W_PIECES[h][0] + W_PIECES[h][1])
+            nc.vector.quantize_mx(out=w_codes[:, cols].bitcast(FP8X4), scales=w_scales[:, cols], in_=wg[h][:])
 
-        picked = [keep.tile([P, (PACK + s) * SLOTS], BF16, name="picked%d" % s, align_bytes=64) for s in range(2)]
-        window = keep.tile([P, T], BF16, name="window")
-        nc.scalar.activation(window[:], planes[0][:], COPY)
-        nc.scalar.activation(picked[1][:, :SLOTS], window[:].indirect(lists[1][:]), COPY)
-        gather(0, 0)
-        gather(0, 1)
-        gather(1, 1)
-        turn_planes(0, 0)
-        turn_planes(1, 0)
-        gather(0, 2)
-        gather(1, 2)
-        turn_lists(2)
-        gather(0, 3)
-        xg0 = along_d(0)
-        wg0 = picked[1][:, (PACK - 1) * SLOTS :]
-        w_group(0, wg0)
-        cf_bank = psum2.tile([P, PACK, P], F32, name="score")
-        for j in range(PACK):
-            nc.tensor.transpose(cf_bank[:, j, :], cf_sb[:, j * P : (j + 1) * P], ident[:])
-        cf_col = keep.tile([P, PACK], F32, name="cf_col")
-        nc.scalar.copy(cf_col[:], cf_bank[:, :, 0])
-        w_q = [quantise("w0", wg0, HALF)]
-        x_q = [quantise("x0", xg0[:], SLOTS)]
-        wg1 = keep.tile([P, PACK * HALF], BF16, name="w_grouped1", align_bytes=64)
-        w_group(1, wg1[:])
-        gather(1, 3)
-        w_q.append(quantise("w1", wg1[:], HALF))
-        xg1 = along_d(1)
+        weave_pair(0, 1)
+        wg = [w_group(h) for h in range(len(W_PIECES))]
+        w_quantise(0)
+        y_q.append(quantise_turn(0, turned0, on_plane(3, "y0_codes", [P, 2 * P], U32)))
+        x_q = [quantise("x0", grouped_x[0][:], SLOTS)]
+        w_quantise(1)
+        weave_pair(1, 1)
+        w_quantise(2)
+        y_q.append(quantise_turn(1, turned1, on_plane(3, "y1_codes", [P, 2 * P], U32, 1024)))
+        x_q.append(quantise("x1", grouped_x[1][:], SLOTS))
 
-        def hidden(s, j0, nj):
+        every = slice(0, SLOTS)
+
+        def block(j):
+            return slice(j * P, (j + 1) * P)
+
+        scaled_at = (6144, 4096, 2560, 5632)
+
+        def scaled_scores(s, j, b):
+            score = bank(b, "score%d%d" % (s, j), [P, SLOTS])
+            product(score[:], w_q, block(j), x_q[s], every)
+            if s == 0:
+                scaled = on_plane(3 if j else 2, "scaled%d%d" % (s, j), [P, SLOTS], F32, scaled_at[j])
+            else:
+                scaled = keep.tile([P, SLOTS], F32, name="scaled%d%d" % (s, j))
+            nc.scalar.activation(scaled[:], score[:], COPY, scale=cf_col[:, j : j + 1])
+            return scaled
+
+        def turned_sigmoid(s, j0, scaled, homes):
+            nj = len(scaled)
             width = nj * P
             per_bank = PACK // nj
-            banks = [psum4.tile([P, per_bank, width], F32, name="logit") for b in range(nj)]
+            logits = [bank(b, "logit%d%d%d" % (s, j0, b), [P, per_bank, width]) for b in homes]
             for jj in range(nj):
-                j = j0 + jj
-                score = psum2.tile([P, SLOTS], F32, name="score")
-                cols = slice((j % 2) * P, (j % 2 + 1) * P)
-                nc.tensor.matmul_mx(
-                    out=score[:],
-                    lhsT=w_q[j // 2][0][:, cols].bitcast(FP8X4),
-                    lhsT_scale=w_q[j // 2][1][:, cols],
-                    rhs=x_q[s][0][:].bitcast(FP8X4),
-                    rhs_scale=x_q[s][1][:],
-                    start=True,
-                    stop=True,
-                )
-                scaled = ring.tile([P, PACK, P], F32, name="scaled")
-                dealt = score[:].rearrange("p (m r) -> p r m", r=PACK)
-                if (s, j) in VECTOR_SCALES:
-                    nc.vector.tensor_scalar(scaled[:], dealt, cf_col[:, j : j + 1], None, MULT)
-                else:
-                    nc.scalar.activation(scaled[:], dealt, COPY, scale=cf_col[:, j : j + 1])
                 for r in range(PACK):
-                    nc.tensor.transpose(
-                        banks[r // per_bank][:, r % per_bank, jj * P : (jj + 1) * P], scaled[:, r, :], ident[:]
-                    )
-            sig = ring.tile([P, PACK * width], F32, name="sig", bufs=4)
+                    nc.tensor.transpose(logits[r // per_bank][:, r % per_bank, block(jj)], scaled[jj][:, block(r)], ident[:])
+            sig = keep.tile([P, PACK * width], F32, name="sig%d%d" % (s, j0))
             for r in range(PACK):
                 nc.scalar.activation(
-                    sig[:, r * width : (r + 1) * width],
-                    banks[r // per_bank][:, r % per_bank, :],
-                    SIGMOID,
-                    scale=t_cols[s][:, r : r + 1],
+                    sig[:, r * width : (r + 1) * width], logits[r // per_bank][:, r % per_bank, :], SIGMOID, scale=t_cols[s][:, r : r + 1]
                 )
             return sig
 
-        def hidden_b(j0, nj):
+        def cf_rows(j0, width, count):
+            return cf_sb[:, j0 * P : j0 * P + width].rearrange("p (e f) -> p e f", e=1).to_broadcast([P, count, width])
+
+        def direct_scores(s, j0, homes):
+            nj = len(homes)
             width = nj * P
             per_bank = PACK // nj
-            cols = slice((j0 % 2) * P, (j0 % 2) * P + width)
-            scaled = ring.tile([P, PACK * width], F32, name="scaled_b", bufs=3)
-            factor = cf_sb[:, j0 * P : j0 * P + width].rearrange("p (e f) -> p e f", e=1).to_broadcast([P, per_bank, width])
-            for b in range(nj):
-                bank = psum2.tile([P, per_bank, width], F32, name="score")
+            cols = slice(j0 * P, j0 * P + width)
+            scaled = keep.tile([P, PACK, width], F32, name="direct%d%d" % (s, j0), align_bytes=64)
+            for i, b in enumerate(homes):
+                score = bank(b, "dscore%d%d%d" % (s, j0, i), [P, per_bank, width])
                 for e in range(per_bank):
-                    r = b * per_bank + e
-                    nc.tensor.matmul_mx(
-                        out=bank[:, e, :],
-                        lhsT=x_q[1][0][:, r * P : (r + 1) * P].bitcast(FP8X4),
-                        lhsT_scale=x_q[1][1][:, r * P : (r + 1) * P],
-                        rhs=w_q[j0 // 2][0][:, cols].bitcast(FP8X4),
-                        rhs_scale=w_q[j0 // 2][1][:, cols],
-                        start=True,
-                        stop=True,
-                    )
-                dst = scaled[:, b * per_bank * width : (b + 1) * per_bank * width].rearrange("p (e f) -> p e f", e=per_bank)
-                nc.vector.tensor_tensor(dst, bank[:], factor, MULT)
-            sig = ring.tile([P, PACK * width], F32, name="sig", bufs=4)
+                    product(score[:, e, :], x_q[s], block(i * per_bank + e), w_q, cols)
+                nc.vector.tensor_tensor(scaled[:, i * per_bank : (i + 1) * per_bank, :], score[:], cf_rows(j0, width, per_bank), MULT)
+            return scaled
+
+        def direct_sigmoid(s, j0, scaled, width):
+            sig = keep.tile([P, PACK * width], F32, name="sig%d%d" % (s, j0))
             for r in range(PACK):
-                run = slice(r * width, (r + 1) * width)
-                nc.scalar.activation(sig[:, run], scaled[:, run], SIGMOID, scale=t_cols[1][:, r : r + 1])
+                nc.scalar.activation(sig[:, r * width : (r + 1) * width], scaled[:, r, :], SIGMOID, scale=t_cols[s][:, r : r + 1])
             return sig
 
-        def weigh(s, sig, width, on_scalar=False):
-            rounded = ring.tile([P, PACK * width], BF16, name="h_planes", bufs=5)
-            for r in range(PACK):
-                cols = slice(r * width, (r + 1) * width)
-                if on_scalar:
-                    nc.scalar.activation(rounded[:, cols], sig[:, cols], COPY, scale=t_signed[s][:, r : r + 1])
-                else:
-                    nc.vector.tensor_scalar(rounded[:, cols], sig[:, cols], t_signed[s][:, r : r + 1], None, MULT)
-            grouped = ring.tile([P, PACK * width], BF16, name="h_grouped", align_bytes=64, bufs=5)
-            copy = nc.scalar.copy if width == P else nc.vector.tensor_copy
-            copy(weave(grouped[:]), planar(rounded[:]))
+        def weigh(s, j0, sig, width):
+            grouped = keep.tile([P, PACK * width], BF16, name="h_grouped%d%d" % (s, j0), align_bytes=64)
+            factor = t_signed[s].rearrange("p (c t i) -> p c t i", c=1, i=1).to_broadcast([P, width // 4, PACK, 4])
+            nc.vector.tensor_tensor(weave(grouped[:]), planar(sig[:]), factor, MULT)
             return grouped
 
         out_rows = out.rearrange("(p t) f -> p t f", t=PACK)
 
-        def finish(j0, nj, h_b, homes):
+        def finish(j0, h_a, a_cols, h_b, homes):
+            nj = len(homes)
             width = nj * P
-            per_bank = PACK // len(homes)
-            a_cols = slice((j0 % 2) * P, (j0 % 2) * P + width)
-            moving = [(h_a[j0 // 2][0][:, a_cols], h_a[j0 // 2][1][:, a_cols]), (h_b[0][:], h_b[1][:])]
-            fcols = slice(j0 * P, j0 * P + width)
-            factor = cf_sb[:, fcols].rearrange("p (e f) -> p e f", e=1).to_broadcast([P, per_bank, width])
-            results = [keep.tile([P, 2, width], F32, name="result%d%d" % (j0, pair)) for pair in range(2)]
-            for b, (pool, tag) in enumerate(homes):
-                acc = pool.tile([P, per_bank, width], F32, name=tag)
-                t0 = b * per_bank
+            per_bank = PACK // nj
+            for i, b in enumerate(homes):
+                acc = bank(b, "acc%d%d" % (j0, i), [P, per_bank, width])
                 for e in range(per_bank):
-                    t = t0 + e
-                    for s in range(2):
-                        nc.tensor.matmul_mx(
-                            out=acc[:, e, :],
-                            lhsT=y_q[s][0][:, t * P : (t + 1) * P].bitcast(FP8X4),
-                            lhsT_scale=y_q[s][1][:, t * P : (t + 1) * P],
-                            rhs=moving[s][0].bitcast(FP8X4),
-                            rhs_scale=moving[s][1],
-                            start=(s == 0),
-                            stop=(s == 1),
-                        )
-                nc.vector.tensor_tensor(results[t0 // 2][:, t0 % 2 : t0 % 2 + per_bank, :], acc[:], factor, MULT)
-                if (t0 + per_bank) % 2 == 0:
-                    pair = t0 // 2
-                    nc.sync.dma_start(out_rows[:, 2 * pair : 2 * pair + 2, fcols], results[pair][:])
+                    t = i * per_bank + e
+                    product(acc[:, e, :], y_q[t], block(0), h_a, a_cols, True, False)
+                    product(acc[:, e, :], y_q[t], block(1), h_b, slice(0, width), False, True)
+                result = keep.tile([P, per_bank, width], F32, name="result%d%d" % (j0, i))
+                nc.vector.tensor_tensor(result[:], acc[:], cf_rows(j0, width, per_bank), MULT)
+                nc.sync.dma_start(out_rows[:, i * per_bank : (i + 1) * per_bank, j0 * P : j0 * P + width], result[:])
 
-        h_a = []
-        sig_a0 = hidden(0, 0, 2)
-        x_q.append(quantise("x1", xg1[:], SLOTS))
-        sig_a1 = hidden(0, 2, 2)
-        turn_lists(3)
-        sig_b0 = hidden_b(0, 2)
-        grouped_b0 = weigh(1, sig_b0, HALF, True)
-        h_a.append(quantise("ha0", weigh(0, sig_a0, HALF)[:], HALF))
-        y_q = [quantise("y%d" % s, turned[:, s * 2 * D : (s + 1) * 2 * D].bitcast(BF16), D) for s in range(2)]
-        h_b0 = quantise("hb0", grouped_b0[:], HALF)
-        grouped_a1 = weigh(0, sig_a1, HALF, True)
-        sig_b2 = hidden_b(2, 1)
-        h_a.append(quantise("ha1", grouped_a1[:], HALF))
-        grouped_b2 = weigh(1, sig_b2, P, True)
-        sig_b3 = hidden_b(3, 1)
-        grouped_b3 = weigh(1, sig_b3, P, True)
-        finish(0, 2, h_b0, ((psum2, "turn"), (psum2, "turn"), (psum4, "logit"), (psum4, "logit")))
-        finish(2, 1, quantise("hb2", grouped_b2[:], P), ((psum4, "logit"), (psum4, "logit")))
-        finish(3, 1, quantise("hb3", grouped_b3[:], P), ((psum2, "score"), (psum2, "score")))
+        scaled_a = [scaled_scores(0, j, j) for j in range(2)]
+        turned2 = empty_turn(y_bank2, on_w(256, "turned2", words, F32))
+        sig_a0 = turned_sigmoid(0, 0, scaled_a, (2, 3))
+        scaled_a = [scaled_scores(0, 2, 4), scaled_scores(0, 3, 6)]
+        direct_b0 = direct_scores(1, 0, (0, 1))
+        g_a0 = weigh(0, 0, sig_a0, HALF)
+        sig_b0 = direct_sigmoid(1, 0, direct_b0, HALF)
+        scaled_b2 = scaled_scores(1, 2, 7)
+        y_bank3 = turn(3, 5)
+        turned3 = empty_turn(y_bank3, keep.tile(words, F32, name="turned3", tag="direct10", align_bytes=64))
+        y_q.append(quantise_turn(2, turned2))
+        h_a0 = quantise("ha0", g_a0[:], HALF)
+        sig_a1 = turned_sigmoid(0, 2, scaled_a, (2, 3))
+        scaled_b3 = scaled_scores(1, 3, 4)
+        g_b0 = weigh(1, 0, sig_b0, HALF)
+        y_q.append(quantise_turn(3, turned3))
+        h_b0 = quantise("hb0", g_b0[:], HALF)
+        sig_b2 = turned_sigmoid(1, 2, [scaled_b2], (6,))
+        sig_b3 = turned_sigmoid(1, 3, [scaled_b3], (7,))
+        g_a1 = weigh(0, 2, sig_a1, HALF)
+        finish(0, h_a0, slice(0, HALF), h_b0, (0, 1))
+        g_b2 = weigh(1, 2, sig_b2, P)
+        h_a1 = quantise("ha1", g_a1[:], HALF)
+        h_b2 = quantise("hb2", g_b2[:], P)
+        g_b3 = weigh(1, 3, sig_b3, P)
+        finish(2, h_a1, block(0), h_b2, (5,))
+        h_b3 = quantise("hb3", g_b3[:], P)
+        finish(3, h_a1, block(1), h_b3, (4,))

@@ -20,7 +20,7 @@ F = 512
 SLOTS = 512
 T = 2048
 HALF = F // 2
-W_PIECES = ((0, 128), (128, 128), (256, 256))
+W_PIECES = ((0, 256), (256, 256))
 FLOPS = 4 * 2 * D * F * SLOTS
 
 
@@ -59,10 +59,10 @@ def tile_attend_grbm_kernel(tc, vT, W, cf, tv, offs, foffs, out):
             )
 
         def weave(ap):
-            return ap.rearrange("p (c i t) -> p c t i", i=4, t=PACK)
+            return ap.rearrange("p (c i t) -> p c t i", i=2, t=PACK)
 
         def planar(ap):
-            return ap.rearrange("p (t c i) -> p c t i", i=4, t=PACK)
+            return ap.rearrange("p (t c i) -> p c t i", i=2, t=PACK)
 
         tv_sb = keep.tile([P, T], F32, name="tv_sb")
         nc.scalar.dma_start(tv_sb[P - 1 :, :], tv[0:1, :])
@@ -71,12 +71,9 @@ def tile_attend_grbm_kernel(tc, vT, W, cf, tv, offs, foffs, out):
             tile = keep.tile([P, SLOTS // 16], U16, name=name + "_sb")
             nc.sync.dma_start(tile[:], src)
             lists.append(tile)
-        cf_row = keep.tile([P, F], F32, name="cf_row")
-        nc.scalar.dma_start(cf_row[P - 1 :, :], cf[0:1, :])
         nc.vector.memset(tv_sb[: P - 1, :], 0.0)
         ident = keep.tile([P, P], F32, name="ident")
         make_identity(nc, ident[:])
-        nc.gpsimd.memset(cf_row[: P - 1, :], 0.0)
         warm = keep.tile([P, 1], F32, name="warm")
         nc.scalar.activation(warm[:64, :], tv_sb[:64, 0:1], SIGMOID)
         vT_planes = vT.rearrange("(p t) x -> t p x", t=PACK)
@@ -94,10 +91,6 @@ def tile_attend_grbm_kernel(tc, vT, W, cf, tv, offs, foffs, out):
         cf_sb = keep.tile([P, F], F32, name="cf_sb")
         nc.sync.dma_start(cf_sb[:], cf)
 
-        cf_bank = bank(0, "cf_bank", [P, PACK, P])
-        for j in range(PACK):
-            nc.tensor.transpose(cf_bank[:, j, :], cf_row[:, j * P : (j + 1) * P], ident[:])
-
         tv_picked = [keep.tile([P, SLOTS], F32, name="tv_picked%d" % s) for s in range(2)]
         nc.vector.tensor_copy(tv_picked[0][:], tv_sb[:].indirect(lists[0][:]))
         nc.scalar.activation(tv_picked[1][:], tv_sb[:].indirect(lists[1][:]), COPY)
@@ -108,22 +101,29 @@ def tile_attend_grbm_kernel(tc, vT, W, cf, tv, offs, foffs, out):
                 nc.tensor.transpose(t_bank[:, r, :], tv_picked[s][:, r::PACK], ident[:])
             t_banks.append(t_bank)
 
-        picked = [
-            [keep.tile([P, 2 * SLOTS], BF16, name="picked%d%d" % (s, u), align_bytes=64) for u in range(2)]
-            for s in range(2)
-        ]
+        picked_a = keep.tile([P, 3 * SLOTS], BF16, name="picked_a", align_bytes=64)
+        picked_b = keep.tile([P, PACK * SLOTS], BF16, name="picked_b", align_bytes=64)
+        grouped_x = [keep.tile([P, PACK * SLOTS], BF16, name="x_grouped0", align_bytes=64)]
+        ident_bf = keep.tile([P, P], BF16, name="ident_bf")
+        nc.gpsimd.tensor_copy(ident_bf[:], ident[:])
 
         def picked_plane(s, t):
-            return picked[s][t // 2][:, (t % 2) * SLOTS : (t % 2 + 1) * SLOTS]
+            if s == 0:
+                return picked_a[:, t * SLOTS : (t + 1) * SLOTS]
+            return picked_b[:, t * SLOTS : (t + 1) * SLOTS]
 
         def gather(t):
-            nc.vector.tensor_copy(picked_plane(0, t), planes[t][:].indirect(lists[0][:]))
+            if t < 3:
+                to = picked_plane(0, t)
+            else:
+                to = grouped_x[0][:].rearrange("p (r m t) -> p m r t", r=PACK, t=PACK)[:, :, :, t]
+            nc.vector.tensor_copy(to, planes[t][:].indirect(lists[0][:]))
             nc.scalar.activation(picked_plane(1, t), planes[t][:].indirect(lists[1][:]), COPY)
 
-        def weave_pair(s, u):
-            nc.vector.tensor_copy(
-                grouped_x[s][:].rearrange("p (r k m t) -> p k r m t", r=PACK, m=2, t=PACK)[:, :, :, :, 2 * u : 2 * u + 2],
-                picked[s][u][:].rearrange("p (t k m r) -> p k r m t", t=2, m=2, r=PACK),
+        def weave_planes(copy, s, t0, count, src):
+            copy(
+                grouped_x[s][:].rearrange("p (r k m t) -> p k r m t", r=PACK, m=2, t=PACK)[:, :, :, :, t0 : t0 + count],
+                src.rearrange("p (t k m r) -> p k r m t", t=count, m=2, r=PACK),
             )
 
         def turn(t, b):
@@ -144,97 +144,76 @@ def tile_attend_grbm_kernel(tc, vT, W, cf, tv, offs, foffs, out):
         words = [P, 2 * 2 * P]
         y_q = []
         gather(0)
-        t_all = on_plane(0, "t_all", [P, 4, PACK], F32)
+        t_all = on_plane(0, "t_all", [P, 3, PACK], F32)
         for s in range(2):
             nc.vector.tensor_copy(t_all[:, s, :], t_banks[s][:, :, P - 1])
         nc.vector.tensor_scalar(t_all[:, 2, :], t_banks[1][:, :, P - 1], -1.0, None, MULT)
-        nc.vector.tensor_copy(t_all[:, 3, :], cf_bank[:, :, P - 1])
-        cf_col = t_all[:, 3, :]
         t_cols = [t_all[:, 0, :], t_all[:, 1, :]]
         t_signed = [t_all[:, 0, :], t_all[:, 2, :]]
         y_bank0 = turn(0, 3)
         gather(1)
         y_bank1 = turn(1, 4)
         turned0 = empty_turn(y_bank0, on_plane(1, "turned0", words, F32))
-        grouped_x = [keep.tile([P, PACK * SLOTS], BF16, name="x_grouped0", align_bytes=64)]
-        weave_pair(0, 0)
+        y_q.append(quantise_turn(0, turned0))
         gather(2)
-        y_bank2 = turn(2, 5)
         turned1 = empty_turn(y_bank1, on_plane(2, "turned1", words, F32))
-        grouped_x.append(on_plane(2, "x_grouped1", [P, PACK * SLOTS], BF16, 2048))
-        weave_pair(1, 0)
+        weave_planes(nc.vector.tensor_copy, 0, 0, 3, picked_a[:])
         gather(3)
+        y_bank2 = turn(2, 5)
 
-        w_codes = keep.tile([P, F], U32, name="w_codes", align_bytes=64)
-        w_scales = keep.tile([P, F], U8, name="w_scales", align_bytes=64)
-        w_q = (w_codes, w_scales)
+        w_q = []
 
-        def w_group(h):
-            grouped = keep.tile([P, PACK * W_PIECES[h][1]], BF16, name="w_grouped%d" % h, align_bytes=64)
+        def w_group(h, home):
+            grouped = home
             nc.scalar.copy(weave(grouped[:]), planar(w_raw[h][:].rearrange("p t f -> p (t f)")))
             return grouped
 
         def w_quantise(h):
-            cols = slice(W_PIECES[h][0], W_PIECES[h][0] + W_PIECES[h][1])
-            nc.vector.quantize_mx(out=w_codes[:, cols].bitcast(FP8X4), scales=w_scales[:, cols], in_=wg[h][:])
+            codes, scales = quantise("w%d" % h, wg[h][:], W_PIECES[h][1])
+            for c0 in range(0, W_PIECES[h][1], P):
+                w_q.append((codes[:, c0 : c0 + P], scales[:, c0 : c0 + P]))
 
-        weave_pair(0, 1)
-        wg = [w_group(h) for h in range(len(W_PIECES))]
+        wg = [w_group(0, keep.tile([P, PACK * HALF], BF16, name="w_grouped0", align_bytes=64))]
         w_quantise(0)
-        y_q.append(quantise_turn(0, turned0, on_plane(3, "y0_codes", [P, 2 * P], U32)))
+        y_q.append(quantise_turn(1, turned1, on_plane(3, "y1_codes", [P, 2 * P], U32)))
         x_q = [quantise("x0", grouped_x[0][:], SLOTS)]
-        w_quantise(1)
-        weave_pair(1, 1)
-        w_quantise(2)
-        y_q.append(quantise_turn(1, turned1, on_plane(3, "y1_codes", [P, 2 * P], U32, 1024)))
-        x_q.append(quantise("x1", grouped_x[1][:], SLOTS))
+        grouped_x.append(on_w(0, "x_grouped1", [P, PACK * SLOTS], BF16))
+        weave_planes(nc.scalar.copy, 1, 0, PACK, picked_b[:])
+        wg.append(w_group(1, keep.tile([P, PACK * HALF], BF16, name="w_grouped1", align_bytes=64)))
+
+        def turn_last(b, turned):
+            y_bank = bank(b, "y_bank3", [P, 2, 2 * P])
+            halves = y_bank[:, 0, :].bitcast(BF16).rearrange("p (r x) -> p r x", r=PACK)
+            last = grouped_x[0][:].rearrange("p (r m t) -> p r m t", r=PACK, t=PACK)
+            for r in range(PACK):
+                nc.tensor.transpose(halves[:, r, :], last[:, r, :, PACK - 1], ident_bf[:])
+            pairs = picked_plane(1, 3).bitcast(F32)
+            for u in range(2):
+                nc.tensor.transpose(y_bank[:, 1, u * P : (u + 1) * P], pairs[:, u::2], ident[:])
+            nc.scalar.copy(
+                turned[:, : 2 * P].bitcast(BF16).rearrange("p (x r) -> p x r", r=PACK), halves.rearrange("p r x -> p x r")
+            )
+            nc.scalar.copy(
+                turned[:, 2 * P :].rearrange("p (x u) -> p x u", u=2), y_bank[:, 1, :].rearrange("p (u x) -> p x u", u=2)
+            )
+            return turned
 
         every = slice(0, SLOTS)
 
         def block(j):
             return slice(j * P, (j + 1) * P)
 
-        scaled_at = (6144, 4096, 2560, 5632)
-
-        def scaled_scores(s, j, b):
-            score = bank(b, "score%d%d" % (s, j), [P, SLOTS])
-            product(score[:], w_q, block(j), x_q[s], every)
-            if s == 0:
-                scaled = on_plane(3 if j else 2, "scaled%d%d" % (s, j), [P, SLOTS], F32, scaled_at[j])
-            else:
-                scaled = keep.tile([P, SLOTS], F32, name="scaled%d%d" % (s, j))
-            nc.scalar.activation(scaled[:], score[:], COPY, scale=cf_col[:, j : j + 1])
-            return scaled
-
-        def turned_sigmoid(s, j0, scaled, homes):
-            nj = len(scaled)
-            width = nj * P
-            per_bank = PACK // nj
-            logits = [bank(b, "logit%d%d%d" % (s, j0, b), [P, per_bank, width]) for b in homes]
-            for jj in range(nj):
-                for r in range(PACK):
-                    nc.tensor.transpose(logits[r // per_bank][:, r % per_bank, block(jj)], scaled[jj][:, block(r)], ident[:])
-            sig = keep.tile([P, PACK * width], F32, name="sig%d%d" % (s, j0))
-            for r in range(PACK):
-                nc.scalar.activation(
-                    sig[:, r * width : (r + 1) * width], logits[r // per_bank][:, r % per_bank, :], SIGMOID, scale=t_cols[s][:, r : r + 1]
-                )
-            return sig
-
         def cf_rows(j0, width, count):
             return cf_sb[:, j0 * P : j0 * P + width].rearrange("p (e f) -> p e f", e=1).to_broadcast([P, count, width])
 
         def direct_scores(s, j0, homes):
-            nj = len(homes)
-            width = nj * P
-            per_bank = PACK // nj
-            cols = slice(j0 * P, j0 * P + width)
+            width = len(homes) * P
             scaled = keep.tile([P, PACK, width], F32, name="direct%d%d" % (s, j0), align_bytes=64)
             for i, b in enumerate(homes):
-                score = bank(b, "dscore%d%d%d" % (s, j0, i), [P, per_bank, width])
-                for e in range(per_bank):
-                    product(score[:, e, :], x_q[s], block(i * per_bank + e), w_q, cols)
-                nc.vector.tensor_tensor(scaled[:, i * per_bank : (i + 1) * per_bank, :], score[:], cf_rows(j0, width, per_bank), MULT)
+                score = bank(b, "dscore%d%d%d" % (s, j0, i), [P, PACK, P])
+                for r in range(PACK):
+                    product(score[:, r, :], x_q[s], block(r), w_q[j0 + i], block(0))
+                nc.vector.tensor_tensor(scaled[:, :, block(i)], score[:], cf_rows(j0 + i, P, PACK), MULT)
             return scaled
 
         def direct_sigmoid(s, j0, scaled, width):
@@ -243,53 +222,64 @@ def tile_attend_grbm_kernel(tc, vT, W, cf, tv, offs, foffs, out):
                 nc.scalar.activation(sig[:, r * width : (r + 1) * width], scaled[:, r, :], SIGMOID, scale=t_cols[s][:, r : r + 1])
             return sig
 
-        def weigh(s, j0, sig, width):
+        def weigh(s, j0, sig, width, engine=nc.vector, piece=HALF):
             grouped = keep.tile([P, PACK * width], BF16, name="h_grouped%d%d" % (s, j0), align_bytes=64)
-            factor = t_signed[s].rearrange("p (c t i) -> p c t i", c=1, i=1).to_broadcast([P, width // 4, PACK, 4])
-            nc.vector.tensor_tensor(weave(grouped[:]), planar(sig[:]), factor, MULT)
+            piece = min(piece, width)
+            factor = t_signed[s].rearrange("p (c t i) -> p c t i", c=1, i=1).to_broadcast([P, piece // 2, PACK, 2])
+            for c0 in range(0, width // 2, piece // 2):
+                run = slice(c0, c0 + piece // 2)
+                engine.tensor_tensor(weave(grouped[:])[:, run], planar(sig[:])[:, run], factor, MULT)
             return grouped
 
         out_rows = out.rearrange("(p t) f -> p t f", t=PACK)
 
-        def finish(j0, h_a, a_cols, h_b, homes):
-            nj = len(homes)
-            width = nj * P
-            per_bank = PACK // nj
-            for i, b in enumerate(homes):
-                acc = bank(b, "acc%d%d" % (j0, i), [P, per_bank, width])
+        def open_sums(j0, h_a, a_cols, homes):
+            width = len(homes) * P
+            per_bank = PACK // len(homes)
+            sums = [bank(b, "acc%d%d" % (j0, i), [P, per_bank, width]) for i, b in enumerate(homes)]
+            for t in range(PACK):
+                product(sums[t // per_bank][:, t % per_bank, :], y_q[t], block(0), h_a, a_cols, t % per_bank == 0, False)
+            return sums
+
+        def finish(j0, sums, h_b):
+            width = len(sums) * P
+            per_bank = PACK // len(sums)
+            for i, acc in enumerate(sums):
                 for e in range(per_bank):
-                    t = i * per_bank + e
-                    product(acc[:, e, :], y_q[t], block(0), h_a, a_cols, True, False)
-                    product(acc[:, e, :], y_q[t], block(1), h_b, slice(0, width), False, True)
+                    product(acc[:, e, :], y_q[i * per_bank + e], block(1), h_b, slice(0, width), False, e == per_bank - 1)
                 result = keep.tile([P, per_bank, width], F32, name="result%d%d" % (j0, i))
                 nc.vector.tensor_tensor(result[:], acc[:], cf_rows(j0, width, per_bank), MULT)
                 nc.sync.dma_start(out_rows[:, i * per_bank : (i + 1) * per_bank, j0 * P : j0 * P + width], result[:])
 
-        scaled_a = [scaled_scores(0, j, j) for j in range(2)]
+        direct_a0 = direct_scores(0, 0, (0, 1))
+        x_q.append(quantise("x1", grouped_x[1][:], SLOTS))
+        w_quantise(1)
+        sig_a0 = direct_sigmoid(0, 0, direct_a0, HALF)
+        direct_b0 = direct_scores(1, 0, (2, 3))
         turned2 = empty_turn(y_bank2, on_w(256, "turned2", words, F32))
-        sig_a0 = turned_sigmoid(0, 0, scaled_a, (2, 3))
-        scaled_a = [scaled_scores(0, 2, 4), scaled_scores(0, 3, 6)]
-        direct_b0 = direct_scores(1, 0, (0, 1))
-        g_a0 = weigh(0, 0, sig_a0, HALF)
+        g_a0 = weigh(0, 0, sig_a0, HALF, nc.gpsimd, P)
         sig_b0 = direct_sigmoid(1, 0, direct_b0, HALF)
-        scaled_b2 = scaled_scores(1, 2, 7)
-        y_bank3 = turn(3, 5)
-        turned3 = empty_turn(y_bank3, keep.tile(words, F32, name="turned3", tag="direct10", align_bytes=64))
-        y_q.append(quantise_turn(2, turned2))
+        direct_a1 = direct_scores(0, 2, (4, 6))
+        turned3 = turn_last(5, keep.tile(words, F32, name="turned3", tag="direct10", align_bytes=64))
+        direct_b2 = direct_scores(1, 2, (7,))
+        direct_b3 = direct_scores(1, 3, (0,))
         h_a0 = quantise("ha0", g_a0[:], HALF)
-        sig_a1 = turned_sigmoid(0, 2, scaled_a, (2, 3))
-        scaled_b3 = scaled_scores(1, 3, 4)
+        sig_a1 = direct_sigmoid(0, 2, direct_a1, HALF)
         g_b0 = weigh(1, 0, sig_b0, HALF)
+        y_q.append(quantise_turn(2, turned2))
         y_q.append(quantise_turn(3, turned3))
         h_b0 = quantise("hb0", g_b0[:], HALF)
-        sig_b2 = turned_sigmoid(1, 2, [scaled_b2], (6,))
-        sig_b3 = turned_sigmoid(1, 3, [scaled_b3], (7,))
+        sig_b2 = direct_sigmoid(1, 2, direct_b2, P)
+        sig_b3 = direct_sigmoid(1, 3, direct_b3, P)
         g_a1 = weigh(0, 2, sig_a1, HALF)
-        finish(0, h_a0, slice(0, HALF), h_b0, (0, 1))
+        sums0 = open_sums(0, h_a0, slice(0, HALF), (1, 2))
         g_b2 = weigh(1, 2, sig_b2, P)
         h_a1 = quantise("ha1", g_a1[:], HALF)
-        h_b2 = quantise("hb2", g_b2[:], P)
         g_b3 = weigh(1, 3, sig_b3, P)
-        finish(2, h_a1, block(0), h_b2, (5,))
+        h_b2 = quantise("hb2", g_b2[:], P)
         h_b3 = quantise("hb3", g_b3[:], P)
-        finish(3, h_a1, block(1), h_b3, (4,))
+        finish(0, sums0, h_b0)
+        sums2 = open_sums(2, h_a1, block(0), (3,))
+        sums3 = open_sums(3, h_a1, block(1), (4,))
+        finish(2, sums2, h_b2)
+        finish(3, sums3, h_b3)

@@ -21,6 +21,7 @@ SLOTS = 512
 T = 2048
 HALF = F // 2
 W_PIECES = ((0, 256), (256, 256))
+WARM_PASSES = 8
 FLOPS = 4 * 2 * D * F * SLOTS
 
 
@@ -58,11 +59,11 @@ def tile_attend_grbm_kernel(tc, vT, W, cf, tv, offs, foffs, out):
                 stop=stop,
             )
 
-        def weave(ap):
-            return ap.rearrange("p (c i t) -> p c t i", i=2, t=PACK)
+        def weave(ap, run=4):
+            return ap.rearrange("p (c i t) -> p c t i", i=run, t=PACK)
 
-        def planar(ap):
-            return ap.rearrange("p (t c i) -> p c t i", i=2, t=PACK)
+        def planar(ap, run=4):
+            return ap.rearrange("p (t c i) -> p c t i", i=run, t=PACK)
 
         tv_sb = keep.tile([P, T], F32, name="tv_sb")
         nc.scalar.dma_start(tv_sb[P - 1 :, :], tv[0:1, :])
@@ -71,9 +72,12 @@ def tile_attend_grbm_kernel(tc, vT, W, cf, tv, offs, foffs, out):
             tile = keep.tile([P, SLOTS // 16], U16, name=name + "_sb")
             nc.sync.dma_start(tile[:], src)
             lists.append(tile)
+        cf_row = keep.tile([P, F], F32, name="cf_row")
+        nc.scalar.dma_start(cf_row[P - 1 :, :], cf[0:1, :])
         nc.vector.memset(tv_sb[: P - 1, :], 0.0)
         ident = keep.tile([P, P], F32, name="ident")
         make_identity(nc, ident[:])
+        nc.gpsimd.memset(cf_row[: P - 1, :], 0.0)
         warm = keep.tile([P, 1], F32, name="warm")
         nc.scalar.activation(warm[:64, :], tv_sb[:64, 0:1], SIGMOID)
         vT_planes = vT.rearrange("(p t) x -> t p x", t=PACK)
@@ -90,6 +94,10 @@ def tile_attend_grbm_kernel(tc, vT, W, cf, tv, offs, foffs, out):
             w_raw.append(raw)
         cf_sb = keep.tile([P, F], F32, name="cf_sb")
         nc.sync.dma_start(cf_sb[:], cf)
+
+        cf_bank = bank(0, "cf_bank", [P, PACK, P])
+        for j in range(PACK):
+            nc.tensor.transpose(cf_bank[:, j, :], cf_row[:, j * P : (j + 1) * P], ident[:])
 
         tv_picked = [keep.tile([P, SLOTS], F32, name="tv_picked%d" % s) for s in range(2)]
         nc.vector.tensor_copy(tv_picked[0][:], tv_sb[:].indirect(lists[0][:]))
@@ -122,13 +130,13 @@ def tile_attend_grbm_kernel(tc, vT, W, cf, tv, offs, foffs, out):
 
         def weave_planes(copy, s, t0, count, src):
             copy(
-                grouped_x[s][:].rearrange("p (r k m t) -> p k r m t", r=PACK, m=2, t=PACK)[:, :, :, :, t0 : t0 + count],
-                src.rearrange("p (t k m r) -> p k r m t", t=count, m=2, r=PACK),
+                grouped_x[s][:].rearrange("p (r k m t) -> p k t m r", r=PACK, m=2, t=PACK)[:, :, t0 : t0 + count],
+                src.rearrange("p (t k m r) -> p k t m r", t=count, m=2, r=PACK),
             )
 
-        def turn(t, b):
+        def turn(t, b, order=(0, 1)):
             y_bank = bank(b, "y_bank%d" % t, [P, 2, 2, P])
-            for s in range(2):
+            for s in order:
                 words = picked_plane(s, t).bitcast(F32)
                 for u in range(2):
                     nc.tensor.transpose(y_bank[:, s, u, :], words[:, u::2], ident[:])
@@ -144,10 +152,12 @@ def tile_attend_grbm_kernel(tc, vT, W, cf, tv, offs, foffs, out):
         words = [P, 2 * 2 * P]
         y_q = []
         gather(0)
-        t_all = on_plane(0, "t_all", [P, 3, PACK], F32)
+        t_all = on_plane(0, "t_all", [P, 4, PACK], F32)
         for s in range(2):
             nc.vector.tensor_copy(t_all[:, s, :], t_banks[s][:, :, P - 1])
         nc.vector.tensor_scalar(t_all[:, 2, :], t_banks[1][:, :, P - 1], -1.0, None, MULT)
+        nc.vector.tensor_copy(t_all[:, 3, :], cf_bank[:, :, P - 1])
+        cf_col = t_all[:, 3, :]
         t_cols = [t_all[:, 0, :], t_all[:, 1, :]]
         t_signed = [t_all[:, 0, :], t_all[:, 2, :]]
         y_bank0 = turn(0, 3)
@@ -156,16 +166,18 @@ def tile_attend_grbm_kernel(tc, vT, W, cf, tv, offs, foffs, out):
         turned0 = empty_turn(y_bank0, on_plane(1, "turned0", words, F32))
         y_q.append(quantise_turn(0, turned0))
         gather(2)
+        y_bank2 = turn(2, 5, (1, 0))
         turned1 = empty_turn(y_bank1, on_plane(2, "turned1", words, F32))
         weave_planes(nc.vector.tensor_copy, 0, 0, 3, picked_a[:])
         gather(3)
-        y_bank2 = turn(2, 5)
+        idle = bank(4, "idle", [P, 2, 2 * P])
+        for e in range(WARM_PASSES):
+            product(idle[:, e % 2, :], y_q[0], slice(0, P), y_q[0], slice(0, 2 * P))
 
         w_q = []
 
-        def w_group(h, home):
-            grouped = home
-            nc.scalar.copy(weave(grouped[:]), planar(w_raw[h][:].rearrange("p t f -> p (t f)")))
+        def w_group(copy, h, grouped):
+            copy(weave(grouped[:]), planar(w_raw[h][:].rearrange("p t f -> p (t f)")))
             return grouped
 
         def w_quantise(h):
@@ -173,13 +185,12 @@ def tile_attend_grbm_kernel(tc, vT, W, cf, tv, offs, foffs, out):
             for c0 in range(0, W_PIECES[h][1], P):
                 w_q.append((codes[:, c0 : c0 + P], scales[:, c0 : c0 + P]))
 
-        wg = [w_group(0, keep.tile([P, PACK * HALF], BF16, name="w_grouped0", align_bytes=64))]
+        wg = [w_group(nc.scalar.copy, 0, on_plane(1, "w_grouped0", [P, PACK * HALF], BF16, 2048))]
         w_quantise(0)
         y_q.append(quantise_turn(1, turned1, on_plane(3, "y1_codes", [P, 2 * P], U32)))
         x_q = [quantise("x0", grouped_x[0][:], SLOTS)]
-        grouped_x.append(on_w(0, "x_grouped1", [P, PACK * SLOTS], BF16))
-        weave_planes(nc.scalar.copy, 1, 0, PACK, picked_b[:])
-        wg.append(w_group(1, keep.tile([P, PACK * HALF], BF16, name="w_grouped1", align_bytes=64)))
+        grouped_x.append(on_plane(1, "x_grouped1", [P, PACK * SLOTS], BF16, 2048))
+        weave_planes(nc.vector.tensor_copy, 1, 0, PACK, picked_b[:])
 
         def turn_last(b, turned):
             y_bank = bank(b, "y_bank3", [P, 2, 2 * P])
@@ -203,6 +214,29 @@ def tile_attend_grbm_kernel(tc, vT, W, cf, tv, offs, foffs, out):
         def block(j):
             return slice(j * P, (j + 1) * P)
 
+        def scaled_scores(s, j, b, scaled=None):
+            score = bank(b, "score%d%d" % (s, j), [P, SLOTS])
+            product(score[:], w_q[j], block(0), x_q[s], every)
+            if scaled is None:
+                scaled = keep.tile([P, SLOTS], F32, name="scaled%d%d" % (s, j))
+            nc.scalar.activation(scaled[:], score[:], COPY, scale=cf_col[:, j : j + 1])
+            return scaled
+
+        def turned_sigmoid(s, j0, scaled, homes):
+            nj = len(scaled)
+            width = nj * P
+            per_bank = PACK // nj
+            logits = [bank(b, "logit%d%d%d" % (s, j0, b), [P, per_bank, width]) for b in homes]
+            for jj in range(nj):
+                for r in range(PACK):
+                    nc.tensor.transpose(logits[r // per_bank][:, r % per_bank, block(jj)], scaled[jj][:, block(r)], ident[:])
+            sig = keep.tile([P, PACK * width], F32, name="sig%d%d" % (s, j0))
+            for r in range(PACK):
+                nc.scalar.activation(
+                    sig[:, r * width : (r + 1) * width], logits[r // per_bank][:, r % per_bank, :], SIGMOID, scale=t_cols[s][:, r : r + 1]
+                )
+            return sig
+
         def cf_rows(j0, width, count):
             return cf_sb[:, j0 * P : j0 * P + width].rearrange("p (e f) -> p e f", e=1).to_broadcast([P, count, width])
 
@@ -222,64 +256,67 @@ def tile_attend_grbm_kernel(tc, vT, W, cf, tv, offs, foffs, out):
                 nc.scalar.activation(sig[:, r * width : (r + 1) * width], scaled[:, r, :], SIGMOID, scale=t_cols[s][:, r : r + 1])
             return sig
 
-        def weigh(s, j0, sig, width, engine=nc.vector, piece=HALF):
+        def weigh(s, j0, sig, width):
             grouped = keep.tile([P, PACK * width], BF16, name="h_grouped%d%d" % (s, j0), align_bytes=64)
-            piece = min(piece, width)
-            factor = t_signed[s].rearrange("p (c t i) -> p c t i", c=1, i=1).to_broadcast([P, piece // 2, PACK, 2])
-            for c0 in range(0, width // 2, piece // 2):
-                run = slice(c0, c0 + piece // 2)
-                engine.tensor_tensor(weave(grouped[:])[:, run], planar(sig[:])[:, run], factor, MULT)
+            factor = t_signed[s].rearrange("p (c t i) -> p c t i", c=1, i=1).to_broadcast([P, width // 4, PACK, 4])
+            nc.vector.tensor_tensor(weave(grouped[:]), planar(sig[:]), factor, MULT)
+            return grouped
+
+        def weigh_on_scalar(s, j0, sig, width):
+            rounded = keep.tile([P, PACK * width], BF16, name="h_planes%d%d" % (s, j0))
+            for r in range(PACK):
+                run = slice(r * width, (r + 1) * width)
+                nc.scalar.activation(rounded[:, run], sig[:, run], COPY, scale=t_signed[s][:, r : r + 1])
+            grouped = keep.tile([P, PACK * width], BF16, name="h_grouped%d%d" % (s, j0), align_bytes=64)
+            nc.scalar.copy(weave(grouped[:]), planar(rounded[:]))
             return grouped
 
         out_rows = out.rearrange("(p t) f -> p t f", t=PACK)
 
-        def open_sums(j0, h_a, a_cols, homes):
-            width = len(homes) * P
-            per_bank = PACK // len(homes)
-            sums = [bank(b, "acc%d%d" % (j0, i), [P, per_bank, width]) for i, b in enumerate(homes)]
+        def open_sums(half, h_a, homes):
+            sums = [bank(b, "acc%d%d" % (half, i), [P, 2, HALF]) for i, b in enumerate(homes)]
             for t in range(PACK):
-                product(sums[t // per_bank][:, t % per_bank, :], y_q[t], block(0), h_a, a_cols, t % per_bank == 0, False)
+                product(sums[t // 2][:, t % 2, :], y_q[t], block(0), h_a, slice(0, HALF), t % 2 == 0, False)
             return sums
 
-        def finish(j0, sums, h_b):
-            width = len(sums) * P
-            per_bank = PACK // len(sums)
+        def finish(half, sums, pieces):
             for i, acc in enumerate(sums):
-                for e in range(per_bank):
-                    product(acc[:, e, :], y_q[i * per_bank + e], block(1), h_b, slice(0, width), False, e == per_bank - 1)
-                result = keep.tile([P, per_bank, width], F32, name="result%d%d" % (j0, i))
-                nc.vector.tensor_tensor(result[:], acc[:], cf_rows(j0, width, per_bank), MULT)
-                nc.sync.dma_start(out_rows[:, i * per_bank : (i + 1) * per_bank, j0 * P : j0 * P + width], result[:])
+                passes = [(e, c0, width, h_b) for c0, width, h_b in pieces for e in range(2)]
+                for n, (e, c0, width, h_b) in enumerate(passes):
+                    last = n == len(passes) - 1
+                    product(acc[:, e, c0 : c0 + width], y_q[2 * i + e], block(1), h_b, slice(0, width), False, last)
+                result = keep.tile([P, 2, HALF], F32, name="result%d%d" % (half, i))
+                nc.vector.tensor_tensor(result[:], acc[:], cf_rows(2 * half, HALF, 2), MULT)
+                nc.sync.dma_start(out_rows[:, 2 * i : 2 * i + 2, half * HALF : (half + 1) * HALF], result[:])
 
-        direct_a0 = direct_scores(0, 0, (0, 1))
-        x_q.append(quantise("x1", grouped_x[1][:], SLOTS))
-        w_quantise(1)
-        sig_a0 = direct_sigmoid(0, 0, direct_a0, HALF)
-        direct_b0 = direct_scores(1, 0, (2, 3))
-        turned2 = empty_turn(y_bank2, on_w(256, "turned2", words, F32))
-        g_a0 = weigh(0, 0, sig_a0, HALF, nc.gpsimd, P)
-        sig_b0 = direct_sigmoid(1, 0, direct_b0, HALF)
-        direct_a1 = direct_scores(0, 2, (4, 6))
-        turned3 = turn_last(5, keep.tile(words, F32, name="turned3", tag="direct10", align_bytes=64))
-        direct_b2 = direct_scores(1, 2, (7,))
-        direct_b3 = direct_scores(1, 3, (0,))
-        h_a0 = quantise("ha0", g_a0[:], HALF)
-        sig_a1 = direct_sigmoid(0, 2, direct_a1, HALF)
-        g_b0 = weigh(1, 0, sig_b0, HALF)
+        turned2 = empty_turn(y_bank2, on_w(0, "turned2", words, F32))
+        turned3 = turn_last(6, on_w(128, "turned3", words, F32))
+        scaled_a = [scaled_scores(0, 0, 0), scaled_scores(0, 1, 1)]
+        wg.append(w_group(nc.scalar.copy, 1, keep.tile([P, PACK * HALF], BF16, name="w_grouped1", align_bytes=64)))
         y_q.append(quantise_turn(2, turned2))
+        x_q.append(quantise("x1", grouped_x[1][:], SLOTS))
         y_q.append(quantise_turn(3, turned3))
+        sig_a0 = turned_sigmoid(0, 0, scaled_a, (2, 3))
+        direct_b0 = direct_scores(1, 0, (0, 1))
+        w_quantise(1)
+        scaled_a = [scaled_scores(0, 2, 4), scaled_scores(0, 3, 5)]
+        g_a0 = weigh(0, 0, sig_a0, HALF)
+        sig_b0 = direct_sigmoid(1, 0, direct_b0, HALF)
+        direct_b3 = direct_scores(1, 3, (6,))
+        scaled_b2 = scaled_scores(1, 2, 7)
+        h_a0 = quantise("ha0", g_a0[:], HALF)
+        sig_a1 = turned_sigmoid(0, 2, scaled_a, (2, 3))
+        g_b0 = weigh(1, 0, sig_b0, HALF)
+        sums0 = open_sums(0, h_a0, (0, 1))
         h_b0 = quantise("hb0", g_b0[:], HALF)
-        sig_b2 = direct_sigmoid(1, 2, direct_b2, P)
         sig_b3 = direct_sigmoid(1, 3, direct_b3, P)
+        sig_b2 = turned_sigmoid(1, 2, [scaled_b2], (4,))
+        g_b2 = weigh_on_scalar(1, 2, sig_b2, P)
         g_a1 = weigh(0, 2, sig_a1, HALF)
-        sums0 = open_sums(0, h_a0, slice(0, HALF), (1, 2))
-        g_b2 = weigh(1, 2, sig_b2, P)
-        h_a1 = quantise("ha1", g_a1[:], HALF)
         g_b3 = weigh(1, 3, sig_b3, P)
-        h_b2 = quantise("hb2", g_b2[:], P)
+        h_a1 = quantise("ha1", g_a1[:], HALF)
         h_b3 = quantise("hb3", g_b3[:], P)
-        finish(0, sums0, h_b0)
-        sums2 = open_sums(2, h_a1, block(0), (3,))
-        sums3 = open_sums(3, h_a1, block(1), (4,))
-        finish(2, sums2, h_b2)
-        finish(3, sums3, h_b3)
+        h_b2 = quantise("hb2", g_b2[:], P)
+        sums1 = open_sums(1, h_a1, (5, 6))
+        finish(0, sums0, [(0, HALF, h_b0)])
+        finish(1, sums1, [(P, P, h_b3), (0, P, h_b2)])

@@ -21,7 +21,7 @@ SLOTS = 512
 T = 2048
 HALF = F // 2
 W_PIECES = ((0, 256), (256, 256))
-WARM_PASSES = 8
+WARM_PASSES = 4
 FLOPS = 4 * 2 * D * F * SLOTS
 
 
@@ -279,15 +279,18 @@ def tile_attend_grbm_kernel(tc, vT, W, cf, tv, offs, foffs, out):
                 product(sums[t // 2][:, t % 2, :], y_q[t], block(0), h_a, slice(0, HALF), t % 2 == 0, False)
             return sums
 
-        def finish(half, sums, pieces):
+        def finish(half, sums, pieces, cuts=1):
             for i, acc in enumerate(sums):
                 passes = [(e, c0, width, h_b) for c0, width, h_b in pieces for e in range(2)]
                 for n, (e, c0, width, h_b) in enumerate(passes):
                     last = n == len(passes) - 1
                     product(acc[:, e, c0 : c0 + width], y_q[2 * i + e], block(1), h_b, slice(0, width), False, last)
-                result = keep.tile([P, 2, HALF], F32, name="result%d%d" % (half, i))
-                nc.vector.tensor_tensor(result[:], acc[:], cf_rows(2 * half, HALF, 2), MULT)
-                nc.sync.dma_start(out_rows[:, 2 * i : 2 * i + 2, half * HALF : (half + 1) * HALF], result[:])
+                rows = 2 // cuts if i == 1 else 2
+                for e0 in range(0, 2, rows):
+                    result = keep.tile([P, rows, HALF], F32, name="result%d%d%d" % (half, i, e0))
+                    nc.vector.tensor_tensor(result[:], acc[:, e0 : e0 + rows, :], cf_rows(2 * half, HALF, rows), MULT)
+                    t0 = 2 * i + e0
+                    nc.sync.dma_start(out_rows[:, t0 : t0 + rows, half * HALF : (half + 1) * HALF], result[:])
 
         turned2 = empty_turn(y_bank2, on_w(0, "turned2", words, F32))
         turned3 = turn_last(6, on_w(128, "turned3", words, F32))
@@ -307,7 +310,10 @@ def tile_attend_grbm_kernel(tc, vT, W, cf, tv, offs, foffs, out):
         h_a0 = quantise("ha0", g_a0[:], HALF)
         sig_a1 = turned_sigmoid(0, 2, scaled_a, (2, 3))
         g_b0 = weigh(1, 0, sig_b0, HALF)
-        sums0 = open_sums(0, h_a0, (0, 1))
+        idle = bank(2, "idle_late", [P, 2, 2 * P])
+        for e in range(WARM_PASSES):
+            product(idle[:, e % 2, :], y_q[0], slice(0, P), y_q[0], slice(0, 2 * P))
+        sums0 = open_sums(0, h_a0, (2, 3))
         h_b0 = quantise("hb0", g_b0[:], HALF)
         sig_b3 = direct_sigmoid(1, 3, direct_b3, P)
         sig_b2 = turned_sigmoid(1, 2, [scaled_b2], (4,))
@@ -319,4 +325,4 @@ def tile_attend_grbm_kernel(tc, vT, W, cf, tv, offs, foffs, out):
         h_b2 = quantise("hb2", g_b2[:], P)
         sums1 = open_sums(1, h_a1, (5, 6))
         finish(0, sums0, [(0, HALF, h_b0)])
-        finish(1, sums1, [(P, P, h_b3), (0, P, h_b2)])
+        finish(1, sums1, [(P, P, h_b3), (0, P, h_b2)], 2)

@@ -170,9 +170,6 @@ def tile_attend_grbm_kernel(tc, vT, W, cf, tv, offs, foffs, out):
         turned1 = empty_turn(y_bank1, on_plane(2, "turned1", words, F32))
         weave_planes(nc.vector.tensor_copy, 0, 0, 3, picked_a[:])
         gather(3)
-        idle = bank(4, "idle", [P, 2, 2 * P])
-        for e in range(WARM_PASSES):
-            product(idle[:, e % 2, :], y_q[0], slice(0, P), y_q[0], slice(0, 2 * P))
 
         w_q = []
 
@@ -237,6 +234,11 @@ def tile_attend_grbm_kernel(tc, vT, W, cf, tv, offs, foffs, out):
                 )
             return sig
 
+        def warm_up(b, name):
+            idle = bank(b, name, [P, 2, 2 * P])
+            for e in range(WARM_PASSES):
+                product(idle[:, e % 2, :], y_q[0], slice(0, P), y_q[0], slice(0, 2 * P))
+
         def cf_rows(j0, width, count):
             return cf_sb[:, j0 * P : j0 * P + width].rearrange("p (e f) -> p e f", e=1).to_broadcast([P, count, width])
 
@@ -295,6 +297,7 @@ def tile_attend_grbm_kernel(tc, vT, W, cf, tv, offs, foffs, out):
         turned2 = empty_turn(y_bank2, on_w(0, "turned2", words, F32))
         turned3 = turn_last(6, on_w(128, "turned3", words, F32))
         scaled_a = [scaled_scores(0, 0, 0), scaled_scores(0, 1, 1)]
+        warm_up(5, "idle_early")
         wg.append(w_group(nc.scalar.copy, 1, keep.tile([P, PACK * HALF], BF16, name="w_grouped1", align_bytes=64)))
         y_q.append(quantise_turn(2, turned2))
         x_q.append(quantise("x1", grouped_x[1][:], SLOTS))
@@ -306,14 +309,12 @@ def tile_attend_grbm_kernel(tc, vT, W, cf, tv, offs, foffs, out):
         g_a0 = weigh(0, 0, sig_a0, HALF)
         sig_b0 = direct_sigmoid(1, 0, direct_b0, HALF)
         direct_b3 = direct_scores(1, 3, (6,))
-        scaled_b2 = scaled_scores(1, 2, 7)
+        scaled_b2 = scaled_scores(1, 2, 2)
         h_a0 = quantise("ha0", g_a0[:], HALF)
-        sig_a1 = turned_sigmoid(0, 2, scaled_a, (2, 3))
+        sig_a1 = turned_sigmoid(0, 2, scaled_a, (0, 1))
         g_b0 = weigh(1, 0, sig_b0, HALF)
-        idle = bank(2, "idle_late", [P, 2, 2 * P])
-        for e in range(WARM_PASSES):
-            product(idle[:, e % 2, :], y_q[0], slice(0, P), y_q[0], slice(0, 2 * P))
-        sums0 = open_sums(0, h_a0, (2, 3))
+        warm_up(0, "idle_late")
+        sums0 = open_sums(0, h_a0, (0, 1))
         h_b0 = quantise("hb0", g_b0[:], HALF)
         sig_b3 = direct_sigmoid(1, 3, direct_b3, P)
         sig_b2 = turned_sigmoid(1, 2, [scaled_b2], (4,))

@@ -124,7 +124,7 @@ def tile_attend_grbm_kernel(tc, vT, W, cf, tv, offs, foffs, out):
             if t < 3:
                 to = picked_plane(0, t)
             else:
-                to = grouped_x[0][:].rearrange("p (r m t) -> p m r t", r=PACK, t=PACK)[:, :, :, t]
+                to = grouped_x[0][:, t::PACK]
             nc.vector.tensor_copy(to, planes[t][:].indirect(lists[0][:]))
             nc.scalar.activation(picked_plane(1, t), planes[t][:].indirect(lists[1][:]), COPY)
 
@@ -168,7 +168,7 @@ def tile_attend_grbm_kernel(tc, vT, W, cf, tv, offs, foffs, out):
         gather(2)
         y_bank2 = turn(2, 5, (1, 0))
         turned1 = empty_turn(y_bank1, on_plane(2, "turned1", words, F32))
-        weave_planes(nc.vector.tensor_copy, 0, 0, 3, picked_a[:])
+        nc.vector.tensor_copy(weave(grouped_x[0][:])[:, :, : PACK - 1], picked_a[:].rearrange("p (t c i) -> p c t i", i=4, t=PACK - 1))
         gather(3)
 
         w_q = []
@@ -192,7 +192,7 @@ def tile_attend_grbm_kernel(tc, vT, W, cf, tv, offs, foffs, out):
         def turn_last(b, turned):
             y_bank = bank(b, "y_bank3", [P, 2, 2 * P])
             halves = y_bank[:, 0, :].bitcast(BF16).rearrange("p (r x) -> p r x", r=PACK)
-            last = grouped_x[0][:].rearrange("p (r m t) -> p r m t", r=PACK, t=PACK)
+            last = grouped_x[0][:].rearrange("p (m r t) -> p r m t", r=PACK, t=PACK)
             for r in range(PACK):
                 nc.tensor.transpose(halves[:, r, :], last[:, r, :, PACK - 1], ident_bf[:])
             pairs = picked_plane(1, 3).bitcast(F32)
@@ -216,7 +216,11 @@ def tile_attend_grbm_kernel(tc, vT, W, cf, tv, offs, foffs, out):
             product(score[:], w_q[j], block(0), x_q[s], every)
             if scaled is None:
                 scaled = keep.tile([P, SLOTS], F32, name="scaled%d%d" % (s, j))
-            nc.scalar.activation(scaled[:], score[:], COPY, scale=cf_col[:, j : j + 1])
+            if s == 0:
+                dealt = score[:].rearrange("p (m r) -> p r m", r=PACK)
+                nc.scalar.activation(scaled[:].rearrange("p (r m) -> p r m", r=PACK), dealt, COPY, scale=cf_col[:, j : j + 1])
+            else:
+                nc.scalar.activation(scaled[:], score[:], COPY, scale=cf_col[:, j : j + 1])
             return scaled
 
         def turned_sigmoid(s, j0, scaled, homes):

@@ -10,6 +10,7 @@ U16 = mybir.dt.uint16
 U8 = mybir.dt.uint8
 FP8X4 = mybir.dt.float8_e4m3fn_x4
 MULT = mybir.AluOpType.mult
+ADD = mybir.AluOpType.add
 COPY = mybir.ActivationFunctionType.Copy
 SIGMOID = mybir.ActivationFunctionType.Sigmoid
 
@@ -100,14 +101,12 @@ def tile_attend_grbm_kernel(tc, vT, W, cf, tv, offs, foffs, out):
             nc.tensor.transpose(cf_bank[:, j, :], cf_row[:, j * P : (j + 1) * P], ident[:])
 
         tv_picked = [keep.tile([P, SLOTS], F32, name="tv_picked%d" % s) for s in range(2)]
-        nc.vector.tensor_copy(tv_picked[0][:], tv_sb[:].indirect(lists[0][:]))
-        nc.scalar.activation(tv_picked[1][:], tv_sb[:].indirect(lists[1][:]), COPY)
-        t_banks = []
-        for s in range(2):
-            t_bank = bank(1 + s, "t_bank%d" % s, [P, PACK, P])
-            for r in range(PACK):
-                nc.tensor.transpose(t_bank[:, r, :], tv_picked[s][:, r::PACK], ident[:])
-            t_banks.append(t_bank)
+        nc.scalar.activation(tv_picked[0][:], tv_sb[:].indirect(lists[0][:]), COPY)
+        nc.vector.tensor_scalar(tv_picked[1][:], tv_sb[:].indirect(lists[1][:]), -1.0, 0.0, MULT, ADD)
+        t_bank = bank(7, "t_bank", [P, SLOTS])
+        for k in reversed(range(2 * PACK)):
+            nc.tensor.transpose(t_bank[:, 16 * k : 16 * k + P], tv_picked[k // PACK][:, k % PACK :: PACK], ident[:])
+        t_psum = [t_bank[:, P - 1 + 64 * s : P - 1 + 64 * (s + 1) : 16] for s in range(2)]
 
         picked_a = keep.tile([P, 3 * SLOTS], BF16, name="picked_a", align_bytes=64)
         picked_b = keep.tile([P, PACK * SLOTS], BF16, name="picked_b", align_bytes=64)
@@ -153,13 +152,12 @@ def tile_attend_grbm_kernel(tc, vT, W, cf, tv, offs, foffs, out):
         y_q = []
         gather(0)
         t_all = on_plane(0, "t_all", [P, 4, PACK], F32)
-        for s in range(2):
-            nc.vector.tensor_copy(t_all[:, s, :], t_banks[s][:, :, P - 1])
-        nc.vector.tensor_scalar(t_all[:, 2, :], t_banks[1][:, :, P - 1], -1.0, None, MULT)
+        nc.vector.tensor_copy(t_all[:, :2, :].rearrange("p s r -> p (s r)"), t_bank[:, P - 1 : P - 1 + 128 : 16])
+        nc.vector.tensor_scalar(t_all[:, 2, :], t_psum[1], -1.0, None, MULT)
         nc.vector.tensor_copy(t_all[:, 3, :], cf_bank[:, :, P - 1])
         cf_col = t_all[:, 3, :]
-        t_cols = [t_all[:, 0, :], t_all[:, 1, :]]
-        t_signed = [t_all[:, 0, :], t_all[:, 2, :]]
+        t_cols = [t_all[:, 0, :], t_all[:, 2, :]]
+        t_signed = [t_all[:, 0, :], t_all[:, 1, :]]
         y_bank0 = turn(0, 3)
         gather(1)
         y_bank1 = turn(1, 4)
@@ -262,10 +260,22 @@ def tile_attend_grbm_kernel(tc, vT, W, cf, tv, offs, foffs, out):
                 nc.scalar.activation(sig[:, r * width : (r + 1) * width], scaled[:, r, :], SIGMOID, scale=t_cols[s][:, r : r + 1])
             return sig
 
-        def weigh(s, j0, sig, width):
+        def weigh(s, j0, sig, width, own=None):
+            own = width if own is None else own
             grouped = keep.tile([P, PACK * width], BF16, name="h_grouped%d%d" % (s, j0), align_bytes=64)
-            factor = t_signed[s].rearrange("p (c t i) -> p c t i", c=1, i=1).to_broadcast([P, width // 4, PACK, 4])
-            nc.vector.tensor_tensor(weave(grouped[:]), planar(sig[:]), factor, MULT)
+            places = sig[:].rearrange("p (t x) -> p t x", t=PACK)
+            factor = t_psum[s].rearrange("p (c t i) -> p c t i", c=1, i=1).to_broadcast([P, own // 4, PACK, 4])
+            nc.vector.tensor_tensor(
+                weave(grouped[:, : PACK * own]), places[:, :, :own].rearrange("p t (c i) -> p c t i", i=4), factor, MULT
+            )
+            if own < width:
+                factor = t_signed[s].rearrange("p (c t) -> p c t", c=1).to_broadcast([P, width - own, PACK])
+                nc.gpsimd.tensor_tensor(
+                    grouped[:, PACK * own :].rearrange("p (x t) -> p x t", t=PACK),
+                    places[:, :, own:].rearrange("p t x -> p x t"),
+                    factor,
+                    MULT,
+                )
             return grouped
 
         def weigh_on_scalar(s, j0, sig, width):
@@ -285,18 +295,18 @@ def tile_attend_grbm_kernel(tc, vT, W, cf, tv, offs, foffs, out):
                 product(sums[t // 2][:, t % 2, :], y_q[t], block(0), h_a, slice(0, HALF), t % 2 == 0, False)
             return sums
 
-        def finish(half, sums, pieces, cuts=1):
-            for i, acc in enumerate(sums):
-                passes = [(e, c0, width, h_b) for c0, width, h_b in pieces for e in range(2)]
-                for n, (e, c0, width, h_b) in enumerate(passes):
-                    last = n == len(passes) - 1
-                    product(acc[:, e, c0 : c0 + width], y_q[2 * i + e], block(1), h_b, slice(0, width), False, last)
-                rows = 2 // cuts if i == 1 else 2
-                for e0 in range(0, 2, rows):
-                    result = keep.tile([P, rows, HALF], F32, name="result%d%d%d" % (half, i, e0))
-                    nc.vector.tensor_tensor(result[:], acc[:, e0 : e0 + rows, :], cf_rows(2 * half, HALF, rows), MULT)
-                    t0 = 2 * i + e0
-                    nc.sync.dma_start(out_rows[:, t0 : t0 + rows, half * HALF : (half + 1) * HALF], result[:])
+        def close_sum(i, acc, pieces):
+            passes = [(e, c0, width, h_b) for c0, width, h_b in pieces for e in range(2)]
+            for n, (e, c0, width, h_b) in enumerate(passes):
+                last = n == len(passes) - 1
+                product(acc[:, e, c0 : c0 + width], y_q[2 * i + e], block(1), h_b, slice(0, width), False, last)
+
+        def emit(half, i, acc, rows=2):
+            for e0 in range(0, 2, rows):
+                result = keep.tile([P, rows, HALF], F32, name="result%d%d%d" % (half, i, e0))
+                nc.vector.tensor_tensor(result[:], acc[:, e0 : e0 + rows, :], cf_rows(2 * half, HALF, rows), MULT)
+                t0 = 2 * i + e0
+                nc.sync.dma_start(out_rows[:, t0 : t0 + rows, half * HALF : (half + 1) * HALF], result[:])
 
         turned2 = empty_turn(y_bank2, on_w(0, "turned2", words, F32))
         turned3 = turn_last(6, on_w(128, "turned3", words, F32))
@@ -323,11 +333,16 @@ def tile_attend_grbm_kernel(tc, vT, W, cf, tv, offs, foffs, out):
         sig_b3 = direct_sigmoid(1, 3, direct_b3, P)
         sig_b2 = turned_sigmoid(1, 2, [scaled_b2], (4,))
         g_b2 = weigh_on_scalar(1, 2, sig_b2, P)
-        g_a1 = weigh(0, 2, sig_a1, HALF)
+        g_a1 = weigh(0, 2, sig_a1, HALF, P)
         g_b3 = weigh(1, 3, sig_b3, P)
+        for i in range(2):
+            close_sum(i, sums0[i], [(0, HALF, h_b0)])
+        emit(0, 0, sums0[0])
         h_a1 = quantise("ha1", g_a1[:], HALF)
         h_b3 = quantise("hb3", g_b3[:], P)
         h_b2 = quantise("hb2", g_b2[:], P)
         sums1 = open_sums(1, h_a1, (5, 6))
-        finish(0, sums0, [(0, HALF, h_b0)])
-        finish(1, sums1, [(P, P, h_b3), (0, P, h_b2)], 2)
+        emit(0, 1, sums0[1])
+        for i in range(2):
+            close_sum(i, sums1[i], [(P, P, h_b3), (0, P, h_b2)])
+            emit(1, i, sums1[i], 2 - i)

@@ -21,8 +21,8 @@ F = 512
 SLOTS = 512
 T = 2048
 HALF = F // 2
-W_PIECES = ((0, 256), (256, 256))
 WARM_PASSES = 4
+T_STEP = 16
 FLOPS = 4 * 2 * D * F * SLOTS
 
 
@@ -33,21 +33,27 @@ def tile_attend_grbm_kernel(tc, vT, W, cf, tv, offs, foffs, out):
         psum = ctx.enter_context(tc.psum_pool(name="psum", bufs=1))
         shared = ctx.enter_context(tc.tile_pool(name="shared", bufs=1))
 
-        def on_plane(t, name, shape, dtype, byte=0):
-            return shared.tile(shape, dtype, name=name, offset=t * T * 4 + byte, align_bytes=64)
-
-        def on_w(f0, name, shape, dtype):
-            return shared.tile(shape, dtype, name=name, offset=PACK * T * 4 + f0 * PACK * 4, align_bytes=64)
+        def placed(kib, name, shape, dtype):
+            return shared.tile(shape, dtype, name=name, offset=kib * 1024, align_bytes=64)
 
         def bank(b, name, shape):
             return psum.tile(shape, F32, name=name, tag="bank%d" % b)
 
-        def quantise(name, grouped, width, codes=None):
+        def block(j):
+            return slice(j * P, (j + 1) * P)
+
+        def mx_tiles(name, width, codes=None):
             if codes is None:
                 codes = keep.tile([P, width], U32, name=name + "_codes", align_bytes=64)
-            scales = keep.tile([P, width], U8, name=name + "_scales", align_bytes=64)
-            nc.vector.quantize_mx(out=codes[:].bitcast(FP8X4), scales=scales[:], in_=grouped)
-            return codes, scales
+            return codes, keep.tile([P, width], U8, name=name + "_scales", align_bytes=64)
+
+        def quantise_into(operand, cols, grouped):
+            nc.vector.quantize_mx(out=operand[0][:, cols].bitcast(FP8X4), scales=operand[1][:, cols], in_=grouped)
+
+        def quantise(name, grouped, width, codes=None):
+            operand = mx_tiles(name, width, codes)
+            quantise_into(operand, slice(0, width), grouped)
+            return operand
 
         def product(acc, stationary, s_cols, moving, m_cols, start=True, stop=True):
             nc.tensor.matmul_mx(
@@ -60,11 +66,11 @@ def tile_attend_grbm_kernel(tc, vT, W, cf, tv, offs, foffs, out):
                 stop=stop,
             )
 
-        def weave(ap, run=4):
-            return ap.rearrange("p (c i t) -> p c t i", i=run, t=PACK)
+        def weave(ap):
+            return ap.rearrange("p (c i t) -> p c t i", i=4, t=PACK)
 
-        def planar(ap, run=4):
-            return ap.rearrange("p (t c i) -> p c t i", i=run, t=PACK)
+        def planar(ap):
+            return ap.rearrange("p t (c i) -> p c t i", i=4)
 
         tv_sb = keep.tile([P, T], F32, name="tv_sb")
         nc.scalar.dma_start(tv_sb[P - 1 :, :], tv[0:1, :])
@@ -84,118 +90,74 @@ def tile_attend_grbm_kernel(tc, vT, W, cf, tv, offs, foffs, out):
         vT_planes = vT.rearrange("(p t) x -> t p x", t=PACK)
         planes = []
         for t in range(PACK):
-            plane = on_plane(t, "plane%d" % t, [P, T], F32)
+            plane = placed(8 * t, "plane%d" % t, [P, T], F32)
             nc.sync.dma_start(plane[:], vT_planes[t])
             planes.append(plane)
         w_rows = W.rearrange("(p t) f -> p t f", t=PACK)
         w_raw = []
-        for h, (f0, width) in enumerate(W_PIECES):
-            raw = on_w(f0, "w_raw%d" % h, [P, PACK, width], F32)
-            nc.sync.dma_start(raw[:], w_rows[:, :, f0 : f0 + width])
+        for h in range(2):
+            raw = placed(32 + 4 * h, "w_raw%d" % h, [P, PACK, HALF], F32)
+            nc.sync.dma_start(raw[:], w_rows[:, :, h * HALF : (h + 1) * HALF])
             w_raw.append(raw)
         cf_sb = keep.tile([P, F], F32, name="cf_sb")
         nc.sync.dma_start(cf_sb[:], cf)
 
         cf_bank = bank(0, "cf_bank", [P, PACK, P])
         for j in range(PACK):
-            nc.tensor.transpose(cf_bank[:, j, :], cf_row[:, j * P : (j + 1) * P], ident[:])
+            nc.tensor.transpose(cf_bank[:, j, :], cf_row[:, block(j)], ident[:])
 
         tv_picked = [keep.tile([P, SLOTS], F32, name="tv_picked%d" % s) for s in range(2)]
         nc.scalar.activation(tv_picked[0][:], tv_sb[:].indirect(lists[0][:]), COPY)
         nc.vector.tensor_scalar(tv_picked[1][:], tv_sb[:].indirect(lists[1][:]), -1.0, 0.0, MULT, ADD)
         t_bank = bank(7, "t_bank", [P, SLOTS])
         for k in reversed(range(2 * PACK)):
-            nc.tensor.transpose(t_bank[:, 16 * k : 16 * k + P], tv_picked[k // PACK][:, k % PACK :: PACK], ident[:])
-        t_psum = [t_bank[:, P - 1 + 64 * s : P - 1 + 64 * (s + 1) : 16] for s in range(2)]
+            nc.tensor.transpose(t_bank[:, T_STEP * k : T_STEP * k + P], tv_picked[k // PACK][:, k % PACK :: PACK], ident[:])
+        t_columns = t_bank[:, P - 1 : P - 1 + 2 * PACK * T_STEP : T_STEP]
+        t_psum = [t_columns[:, s * PACK : (s + 1) * PACK] for s in range(2)]
 
-        picked_a = keep.tile([P, 3 * SLOTS], BF16, name="picked_a", align_bytes=64)
-        picked_b = keep.tile([P, PACK * SLOTS], BF16, name="picked_b", align_bytes=64)
+        picked = [placed(44 - 4 * s, "picked%d" % s, [P, (PACK - 1 + s) * SLOTS], BF16) for s in range(2)]
         grouped_x = [keep.tile([P, PACK * SLOTS], BF16, name="x_grouped0", align_bytes=64)]
         ident_bf = keep.tile([P, P], BF16, name="ident_bf")
         nc.gpsimd.tensor_copy(ident_bf[:], ident[:])
 
         def picked_plane(s, t):
-            if s == 0:
-                return picked_a[:, t * SLOTS : (t + 1) * SLOTS]
-            return picked_b[:, t * SLOTS : (t + 1) * SLOTS]
+            return picked[s][:, t * SLOTS : (t + 1) * SLOTS]
 
         def gather(t):
-            if t < 3:
+            if t < PACK - 1:
                 to = picked_plane(0, t)
             else:
-                to = grouped_x[0][:, t::PACK]
+                to = grouped_x[0][:].rearrange("p (r c t) -> p c r t", r=PACK, t=PACK)[:, :, :, t]
             nc.vector.tensor_copy(to, planes[t][:].indirect(lists[0][:]))
             nc.scalar.activation(picked_plane(1, t), planes[t][:].indirect(lists[1][:]), COPY)
 
-        def weave_planes(copy, s, t0, count, src):
-            copy(
-                grouped_x[s][:].rearrange("p (r k m t) -> p k t m r", r=PACK, m=2, t=PACK)[:, :, t0 : t0 + count],
-                src.rearrange("p (t k m r) -> p k t m r", t=count, m=2, r=PACK),
+        def weave_planes(s, count, grouped, r0=0, places=PACK):
+            nc.vector.tensor_copy(
+                grouped[:].rearrange("p (r k m t) -> p k t m r", r=places, m=2, t=PACK)[:, :, :count],
+                picked[s][:].rearrange("p (t k m r) -> p k t m r", t=count, m=2, r=PACK)[:, :, :, :, r0 : r0 + places],
             )
 
         def turn(t, b, order=(0, 1)):
             y_bank = bank(b, "y_bank%d" % t, [P, 2, 2, P])
             for s in order:
-                words = picked_plane(s, t).bitcast(F32)
+                pairs = picked_plane(s, t).bitcast(F32)
                 for u in range(2):
-                    nc.tensor.transpose(y_bank[:, s, u, :], words[:, u::2], ident[:])
+                    nc.tensor.transpose(y_bank[:, s, u, :], pairs[:, u::2], ident[:])
             return y_bank
 
         def empty_turn(y_bank, turned):
             nc.scalar.copy(turned[:].rearrange("p (s x u) -> p s x u", s=2, u=2), y_bank[:].rearrange("p s u x -> p s x u"))
             return turned
 
-        def quantise_turn(t, turned, codes=None):
-            return quantise("y%d" % t, turned[:].bitcast(BF16), 2 * P, codes)
-
-        words = [P, 2 * 2 * P]
-        y_q = []
-        gather(0)
-        t_all = on_plane(0, "t_all", [P, 4, PACK], F32)
-        nc.vector.tensor_copy(t_all[:, :2, :].rearrange("p s r -> p (s r)"), t_bank[:, P - 1 : P - 1 + 128 : 16])
-        nc.vector.tensor_scalar(t_all[:, 2, :], t_psum[1], -1.0, None, MULT)
-        nc.vector.tensor_copy(t_all[:, 3, :], cf_bank[:, :, P - 1])
-        cf_col = t_all[:, 3, :]
-        t_cols = [t_all[:, 0, :], t_all[:, 2, :]]
-        t_signed = [t_all[:, 0, :], t_all[:, 1, :]]
-        y_bank0 = turn(0, 3)
-        gather(1)
-        y_bank1 = turn(1, 4)
-        turned0 = empty_turn(y_bank0, on_plane(1, "turned0", words, F32))
-        y_q.append(quantise_turn(0, turned0))
-        gather(2)
-        y_bank2 = turn(2, 5, (1, 0))
-        turned1 = empty_turn(y_bank1, on_plane(2, "turned1", words, F32))
-        nc.vector.tensor_copy(weave(grouped_x[0][:])[:, :, : PACK - 1], picked_a[:].rearrange("p (t c i) -> p c t i", i=4, t=PACK - 1))
-        gather(3)
-
-        w_q = []
-
-        def w_group(copy, h, grouped):
-            copy(weave(grouped[:]), planar(w_raw[h][:].rearrange("p t f -> p (t f)")))
-            return grouped
-
-        def w_quantise(h):
-            codes, scales = quantise("w%d" % h, wg[h][:], W_PIECES[h][1])
-            for c0 in range(0, W_PIECES[h][1], P):
-                w_q.append((codes[:, c0 : c0 + P], scales[:, c0 : c0 + P]))
-
-        wg = [w_group(nc.scalar.copy, 0, on_plane(1, "w_grouped0", [P, PACK * HALF], BF16, 2048))]
-        w_quantise(0)
-        y_q.append(quantise_turn(1, turned1, on_plane(3, "y1_codes", [P, 2 * P], U32)))
-        x_q = [quantise("x0", grouped_x[0][:], SLOTS)]
-        grouped_x.append(on_plane(1, "x_grouped1", [P, PACK * SLOTS], BF16, 2048))
-        weave_planes(nc.vector.tensor_copy, 1, 0, PACK, picked_b[:])
-
         def turn_last(b, turned):
             y_bank = bank(b, "y_bank3", [P, 2, 2 * P])
             halves = y_bank[:, 0, :].bitcast(BF16).rearrange("p (r x) -> p r x", r=PACK)
-            last = grouped_x[0][:].rearrange("p (m r t) -> p r m t", r=PACK, t=PACK)
+            last = grouped_x[0][:].rearrange("p (r c t) -> p r c t", r=PACK, t=PACK)
             for r in range(PACK):
                 nc.tensor.transpose(halves[:, r, :], last[:, r, :, PACK - 1], ident_bf[:])
-            pairs = picked_plane(1, 3).bitcast(F32)
+            pairs = picked_plane(1, PACK - 1).bitcast(F32)
             for u in range(2):
-                nc.tensor.transpose(y_bank[:, 1, u * P : (u + 1) * P], pairs[:, u::2], ident[:])
+                nc.tensor.transpose(y_bank[:, 1, block(u)], pairs[:, u::2], ident[:])
             nc.scalar.copy(
                 turned[:, : 2 * P].bitcast(BF16).rearrange("p (x r) -> p x r", r=PACK), halves.rearrange("p r x -> p x r")
             )
@@ -204,24 +166,43 @@ def tile_attend_grbm_kernel(tc, vT, W, cf, tv, offs, foffs, out):
             )
             return turned
 
-        every = slice(0, SLOTS)
+        def quantise_turn(t, turned, codes=None):
+            return quantise("y%d" % t, turned[:].bitcast(BF16), 2 * P, codes)
 
-        def block(j):
-            return slice(j * P, (j + 1) * P)
+        def w_group(copy, h, grouped):
+            copy(weave(grouped[:]), planar(w_raw[h][:]))
+            return grouped
 
-        def scaled_scores(s, j, b, scaled=None):
+        words = [P, 2 * 2 * P]
+        y_q = []
+        gather(0)
+        t_all = placed(0, "t_all", [P, 4, PACK], F32)
+        nc.vector.tensor_copy(t_all[:, :2, :].rearrange("p s r -> p (s r)"), t_columns)
+        nc.vector.tensor_scalar(t_all[:, 2, :], t_psum[1], -1.0, None, MULT)
+        nc.vector.tensor_copy(t_all[:, 3, :], cf_bank[:, :, P - 1])
+        cf_col = t_all[:, 3, :]
+        t_plain = [t_all[:, 0, :], t_all[:, 2, :]]
+        t_signed = [t_all[:, 0, :], t_all[:, 1, :]]
+        y_bank0 = turn(0, 3)
+        gather(1)
+        y_bank1 = turn(1, 4)
+        turned0 = empty_turn(y_bank0, placed(8, "turned0", words, F32))
+        y_q.append(quantise_turn(0, turned0))
+        gather(2)
+        y_bank2 = turn(2, 5, (1, 0))
+        turned1 = empty_turn(y_bank1, placed(16, "turned1", words, F32))
+        weave_planes(0, PACK - 1, grouped_x[0])
+        gather(3)
+
+        def turned_scores(s, j, b, scaled=None):
             score = bank(b, "score%d%d" % (s, j), [P, SLOTS])
-            product(score[:], w_q[j], block(0), x_q[s], every)
+            product(score[:], w_q[j // 2], block(j % 2), x_q[s], slice(0, SLOTS))
             if scaled is None:
                 scaled = keep.tile([P, SLOTS], F32, name="scaled%d%d" % (s, j))
-            if s == 0:
-                dealt = score[:].rearrange("p (m r) -> p r m", r=PACK)
-                nc.scalar.activation(scaled[:].rearrange("p (r m) -> p r m", r=PACK), dealt, COPY, scale=cf_col[:, j : j + 1])
-            else:
-                nc.scalar.activation(scaled[:], score[:], COPY, scale=cf_col[:, j : j + 1])
+            nc.scalar.activation(scaled[:], score[:], COPY, scale=cf_col[:, j : j + 1])
             return scaled
 
-        def turned_sigmoid(s, j0, scaled, homes):
+        def turned_sigmoid(s, j0, scaled, homes, between=None):
             nj = len(scaled)
             width = nj * P
             per_bank = PACK // nj
@@ -229,120 +210,134 @@ def tile_attend_grbm_kernel(tc, vT, W, cf, tv, offs, foffs, out):
             for jj in range(nj):
                 for r in range(PACK):
                     nc.tensor.transpose(logits[r // per_bank][:, r % per_bank, block(jj)], scaled[jj][:, block(r)], ident[:])
-            sig = keep.tile([P, PACK * width], F32, name="sig%d%d" % (s, j0))
+            if between is not None:
+                between()
+            sig = keep.tile([P, PACK, width], F32, name="sig%d%d" % (s, j0))
             for r in range(PACK):
-                nc.scalar.activation(
-                    sig[:, r * width : (r + 1) * width], logits[r // per_bank][:, r % per_bank, :], SIGMOID, scale=t_cols[s][:, r : r + 1]
-                )
+                nc.scalar.activation(sig[:, r, :], logits[r // per_bank][:, r % per_bank, :], SIGMOID, scale=t_plain[s][:, r : r + 1])
             return sig
-
-        def warm_up(b, name):
-            idle = bank(b, name, [P, 2, 2 * P])
-            for e in range(WARM_PASSES):
-                product(idle[:, e % 2, :], y_q[0], slice(0, P), y_q[0], slice(0, 2 * P))
 
         def cf_rows(j0, width, count):
             return cf_sb[:, j0 * P : j0 * P + width].rearrange("p (e f) -> p e f", e=1).to_broadcast([P, count, width])
 
         def direct_scores(s, j0, homes):
-            width = len(homes) * P
-            scaled = keep.tile([P, PACK, width], F32, name="direct%d%d" % (s, j0), align_bytes=64)
+            scaled = keep.tile([P, PACK, len(homes) * P], F32, name="direct%d%d" % (s, j0))
             for i, b in enumerate(homes):
-                score = bank(b, "dscore%d%d%d" % (s, j0, i), [P, PACK, P])
+                j = j0 + i
+                score = bank(b, "dscore%d%d" % (s, j), [P, PACK, P])
                 for r in range(PACK):
-                    product(score[:, r, :], x_q[s], block(r), w_q[j0 + i], block(0))
-                nc.vector.tensor_tensor(scaled[:, :, block(i)], score[:], cf_rows(j0 + i, P, PACK), MULT)
+                    product(score[:, r, :], x_q[s], block(r), w_q[j // 2], block(j % 2))
+                nc.vector.tensor_tensor(scaled[:, :, block(i)], score[:], cf_rows(j, P, PACK), MULT)
             return scaled
 
-        def direct_sigmoid(s, j0, scaled, width):
-            sig = keep.tile([P, PACK * width], F32, name="sig%d%d" % (s, j0))
+        def direct_sigmoid(s, j0, scaled):
+            sig = keep.tile(list(scaled.shape), F32, name="sig%d%d" % (s, j0))
             for r in range(PACK):
-                nc.scalar.activation(sig[:, r * width : (r + 1) * width], scaled[:, r, :], SIGMOID, scale=t_cols[s][:, r : r + 1])
+                nc.scalar.activation(sig[:, r, :], scaled[:, r, :], SIGMOID, scale=t_plain[s][:, r : r + 1])
             return sig
 
-        def weigh(s, j0, sig, width, own=None):
-            own = width if own is None else own
-            grouped = keep.tile([P, PACK * width], BF16, name="h_grouped%d%d" % (s, j0), align_bytes=64)
-            places = sig[:].rearrange("p (t x) -> p t x", t=PACK)
-            factor = t_psum[s].rearrange("p (c t i) -> p c t i", c=1, i=1).to_broadcast([P, own // 4, PACK, 4])
-            nc.vector.tensor_tensor(
-                weave(grouped[:, : PACK * own]), places[:, :, :own].rearrange("p t (c i) -> p c t i", i=4), factor, MULT
-            )
-            if own < width:
-                factor = t_signed[s].rearrange("p (c t) -> p c t", c=1).to_broadcast([P, width - own, PACK])
-                nc.gpsimd.tensor_tensor(
-                    grouped[:, PACK * own :].rearrange("p (x t) -> p x t", t=PACK),
-                    places[:, :, own:].rearrange("p t x -> p x t"),
-                    factor,
-                    MULT,
-                )
-            return grouped
+        def weigh(s, grouped, sig):
+            factor = t_psum[s].rearrange("p (c t i) -> p c t i", c=1, i=1).to_broadcast([P, sig.shape[2] // 4, PACK, 4])
+            nc.vector.tensor_tensor(weave(grouped), planar(sig), factor, MULT)
 
-        def weigh_on_scalar(s, j0, sig, width):
-            rounded = keep.tile([P, PACK * width], BF16, name="h_planes%d%d" % (s, j0))
-            for r in range(PACK):
-                run = slice(r * width, (r + 1) * width)
-                nc.scalar.activation(rounded[:, run], sig[:, run], COPY, scale=t_signed[s][:, r : r + 1])
-            grouped = keep.tile([P, PACK * width], BF16, name="h_grouped%d%d" % (s, j0), align_bytes=64)
-            nc.scalar.copy(weave(grouped[:]), planar(rounded[:]))
-            return grouped
+        def weigh_on_gpsimd(s, grouped, sig):
+            factor = t_signed[s].rearrange("p (c t) -> p c t", c=1).to_broadcast([P, sig.shape[2], PACK])
+            nc.gpsimd.tensor_tensor(grouped.rearrange("p (x t) -> p x t", t=PACK), sig.rearrange("p t x -> p x t"), factor, MULT)
+
+        def warm_up(b, name, operand):
+            idle = bank(b, name, [P, 2, 2 * P])
+            for e in range(WARM_PASSES):
+                product(idle[:, e % 2, :], operand, block(0), operand, slice(0, 2 * P))
+
+        def passes(acc, planes_of, s, h, h_cols, opens):
+            for e, t in enumerate(planes_of):
+                first = opens and e == 0
+                last = not opens and e == len(planes_of) - 1
+                product(acc[:, e, :], y_q[t], block(s), h, h_cols, first, last)
 
         out_rows = out.rearrange("(p t) f -> p t f", t=PACK)
 
-        def open_sums(half, h_a, homes):
-            sums = [bank(b, "acc%d%d" % (half, i), [P, 2, HALF]) for i, b in enumerate(homes)]
-            for t in range(PACK):
-                product(sums[t // 2][:, t % 2, :], y_q[t], block(0), h_a, slice(0, HALF), t % 2 == 0, False)
-            return sums
+        def emit(acc, t0, j0):
+            rows, width = acc.shape[1], acc.shape[2]
+            result = keep.tile([P, rows, width], F32, name="result%d%d" % (t0, j0))
+            nc.vector.tensor_tensor(result[:], acc, cf_rows(j0, width, rows), MULT)
+            nc.sync.dma_start(out_rows[:, t0 : t0 + rows, j0 * P : j0 * P + width], result[:])
 
-        def close_sum(i, acc, pieces):
-            passes = [(e, c0, width, h_b) for c0, width, h_b in pieces for e in range(2)]
-            for n, (e, c0, width, h_b) in enumerate(passes):
-                last = n == len(passes) - 1
-                product(acc[:, e, c0 : c0 + width], y_q[2 * i + e], block(1), h_b, slice(0, width), False, last)
+        def flipped_passes(flipped, s, h):
+            for n in range(PACK):
+                j, t = divmod(n, 2)
+                product(flipped[:, j, t, :], h, block(j), y_q[t], block(s), s == 0 and n == 0, s == 1 and n == PACK - 1)
 
-        def emit(half, i, acc, rows=2):
-            for e0 in range(0, 2, rows):
-                result = keep.tile([P, rows, HALF], F32, name="result%d%d%d" % (half, i, e0))
-                nc.vector.tensor_tensor(result[:], acc[:, e0 : e0 + rows, :], cf_rows(2 * half, HALF, rows), MULT)
-                t0 = 2 * i + e0
-                nc.sync.dma_start(out_rows[:, t0 : t0 + rows, half * HALF : (half + 1) * HALF], result[:])
+        def emit_flipped(flipped, b):
+            flipped_sb = keep.tile([P, 2, 2, P], F32, name="flipped_sb")
+            for j in range(2):
+                nc.scalar.activation(flipped_sb[:, j], flipped[:, j], COPY, scale=cf_col[:, j : j + 1])
+            back = bank(b, "back", [P, 2, 2, P])
+            for n in range(PACK):
+                j, t = divmod(n, 2)
+                nc.tensor.transpose(back[:, t, j, :], flipped_sb[:, j, t, :], ident[:])
+            result = keep.tile([P, 2, HALF], F32, name="result_back")
+            nc.scalar.copy(result[:], back[:].rearrange("p t j f -> p t (j f)"))
+            nc.scalar.dma_start(out_rows[:, 0:2, 0:HALF], result[:])
 
-        turned2 = empty_turn(y_bank2, on_w(0, "turned2", words, F32))
-        turned3 = turn_last(6, on_w(128, "turned3", words, F32))
-        scaled_a = [scaled_scores(0, 0, 0), scaled_scores(0, 1, 1)]
-        warm_up(5, "idle_early")
-        wg.append(w_group(nc.scalar.copy, 1, keep.tile([P, PACK * HALF], BF16, name="w_grouped1", align_bytes=64)))
-        y_q.append(quantise_turn(2, turned2))
+        def h_tile(name, width, kib=None):
+            if kib is None:
+                return keep.tile([P, PACK * width], BF16, name=name, align_bytes=64)
+            return placed(kib, name, [P, PACK * width], BF16)
+
+        w_grouped0 = w_group(nc.scalar.copy, 0, placed(10, "w_grouped0", [P, PACK * HALF], BF16))
+        w_q = [quantise("w0", w_grouped0[:], HALF)]
+        y_q.append(quantise_turn(1, turned1, placed(24, "y1_codes", [P, 2 * P], U32)))
+        x_q = [quantise("x0", grouped_x[0][:], SLOTS)]
+        grouped_x.append(placed(10, "x_grouped1", [P, PACK * SLOTS], BF16))
+        weave_planes(1, PACK, grouped_x[1])
+        turned2 = empty_turn(y_bank2, placed(32, "turned2", words, F32))
+        w_grouped1 = w_group(nc.scalar.copy, 1, keep.tile([P, PACK * HALF], BF16, name="w_grouped1", align_bytes=64))
+        turned3 = turn_last(6, placed(34, "turned3", words, F32))
+        direct_a = direct_scores(0, 0, (0, 1))
+        warm_up(6, "idle_early", y_q[0])
+        w_q.append(quantise("w1", w_grouped1[:], HALF))
         x_q.append(quantise("x1", grouped_x[1][:], SLOTS))
+        y_q.append(quantise_turn(2, turned2))
         y_q.append(quantise_turn(3, turned3))
-        sig_a0 = turned_sigmoid(0, 0, scaled_a, (2, 3))
-        direct_b0 = direct_scores(1, 0, (0, 1))
-        w_quantise(1)
-        scaled_a = [scaled_scores(0, 2, 4), scaled_scores(0, 3, 5)]
-        g_a0 = weigh(0, 0, sig_a0, HALF)
-        sig_b0 = direct_sigmoid(1, 0, direct_b0, HALF)
-        direct_b3 = direct_scores(1, 3, (6,))
-        scaled_b2 = scaled_scores(1, 2, 2)
+        sig_a0 = direct_sigmoid(0, 0, direct_a)
+        scaled_a = [turned_scores(0, 2, 4), turned_scores(0, 3, 5)]
+        direct_b = direct_scores(1, 0, (2, 3))
+        scaled_b2 = turned_scores(1, 2, 0)
+        sig_b0 = direct_sigmoid(1, 0, direct_b)
+        scaled_b3 = turned_scores(1, 3, 3)
+        sig_a1 = turned_sigmoid(0, 2, scaled_a, (1, 6))
+        g_a0 = h_tile("g_a0", HALF, 34)
+        weigh_on_gpsimd(0, g_a0[:, PACK * P :], sig_a0[:, :, block(1)])
+        weigh(0, g_a0[:, : PACK * P], sig_a0[:, :, block(0)])
         h_a0 = quantise("ha0", g_a0[:], HALF)
-        sig_a1 = turned_sigmoid(0, 2, scaled_a, (0, 1))
-        g_b0 = weigh(1, 0, sig_b0, HALF)
-        warm_up(0, "idle_late")
-        sums0 = open_sums(0, h_a0, (0, 1))
+        g_b0 = h_tile("g_b0", HALF, 48)
+        weigh(1, g_b0[:], sig_b0[:])
         h_b0 = quantise("hb0", g_b0[:], HALF)
-        sig_b3 = direct_sigmoid(1, 3, direct_b3, P)
-        sig_b2 = turned_sigmoid(1, 2, [scaled_b2], (4,))
-        g_b2 = weigh_on_scalar(1, 2, sig_b2, P)
-        g_a1 = weigh(0, 2, sig_a1, HALF, P)
-        g_b3 = weigh(1, 3, sig_b3, P)
-        for i in range(2):
-            close_sum(i, sums0[i], [(0, HALF, h_b0)])
-        emit(0, 0, sums0[0])
+        sig_b2 = turned_sigmoid(1, 2, [scaled_b2], (0,))
+        sig_b3 = turned_sigmoid(1, 3, [scaled_b3], (3,))
+        upright = bank(4, "upright", [P, 2, HALF])
+        flipped = bank(5, "flipped", [P, 2, 2, P])
+        passes(upright, (2, 3), 0, h_a0, slice(0, HALF), True)
+        flipped_passes(flipped, 0, h_a0)
+        flipped_passes(flipped, 1, h_b0)
+        passes(upright, (2, 3), 1, h_b0, slice(0, HALF), False)
+        warm_up(0, "idle_late", y_q[0])
+        g_a1 = h_tile("g_a1", HALF, 48)
+        weigh_on_gpsimd(0, g_a1[:, PACK * P :], sig_a1[:, :, block(1)])
+        weigh(0, g_a1[:, : PACK * P], sig_a1[:, :, block(0)])
+        emit_flipped(flipped, 2)
+        g_b1 = h_tile("g_b1", HALF)
+        weigh(1, g_b1[:, : PACK * P], sig_b2[:])
+        weigh(1, g_b1[:, PACK * P :], sig_b3[:])
         h_a1 = quantise("ha1", g_a1[:], HALF)
-        h_b3 = quantise("hb3", g_b3[:], P)
-        h_b2 = quantise("hb2", g_b2[:], P)
-        sums1 = open_sums(1, h_a1, (5, 6))
-        emit(0, 1, sums0[1])
+        h_b1 = quantise("hb1", g_b1[:], HALF)
+        emit(upright[:], 2, 0)
+        quarters = [bank(b, "quarter%d" % b, [P, PACK, P]) for b in (1, 6)]
         for i in range(2):
-            close_sum(i, sums1[i], [(P, P, h_b3), (0, P, h_b2)])
-            emit(1, i, sums1[i], 2 - i)
+            passes(quarters[i], range(PACK), 0, h_a1, block(i), True)
+        for i in range(2):
+            passes(quarters[i], range(PACK), 1, h_b1, block(i), False)
+        emit(quarters[0][:], 0, 2)
+        emit(quarters[1][:, :2, :], 0, 3)
+        emit(quarters[1][:, 2:, :], 2, 3)

@@ -244,6 +244,12 @@ def tile_attend_grbm_kernel(tc, vT, W, cf, tv, offs, foffs, out):
             factor = t_signed[s].rearrange("p (c t) -> p c t", c=1).to_broadcast([P, sig.shape[2], PACK])
             nc.gpsimd.tensor_tensor(grouped.rearrange("p (x t) -> p x t", t=PACK), sig.rearrange("p t x -> p x t"), factor, MULT)
 
+        def weigh_on_scalar(s, grouped, sig):
+            rounded = keep.tile(list(sig.shape), BF16, name="h_planes")
+            for r in range(PACK):
+                nc.scalar.activation(rounded[:, r, :], sig[:, r, :], COPY, scale=t_signed[s][:, r : r + 1])
+            nc.scalar.copy(weave(grouped), planar(rounded[:]))
+
         def warm_up(b, name, operand):
             idle = bank(b, name, [P, 2, 2 * P])
             for e in range(WARM_PASSES):
@@ -262,23 +268,6 @@ def tile_attend_grbm_kernel(tc, vT, W, cf, tv, offs, foffs, out):
             result = keep.tile([P, rows, width], F32, name="result%d%d" % (t0, j0))
             nc.vector.tensor_tensor(result[:], acc, cf_rows(j0, width, rows), MULT)
             nc.sync.dma_start(out_rows[:, t0 : t0 + rows, j0 * P : j0 * P + width], result[:])
-
-        def flipped_passes(flipped, s, h):
-            for n in range(PACK):
-                j, t = divmod(n, 2)
-                product(flipped[:, j, t, :], h, block(j), y_q[t], block(s), s == 0 and n == 0, s == 1 and n == PACK - 1)
-
-        def emit_flipped(flipped, b):
-            flipped_sb = keep.tile([P, 2, 2, P], F32, name="flipped_sb")
-            for j in range(2):
-                nc.scalar.activation(flipped_sb[:, j], flipped[:, j], COPY, scale=cf_col[:, j : j + 1])
-            back = bank(b, "back", [P, 2, 2, P])
-            for n in range(PACK):
-                j, t = divmod(n, 2)
-                nc.tensor.transpose(back[:, t, j, :], flipped_sb[:, j, t, :], ident[:])
-            result = keep.tile([P, 2, HALF], F32, name="result_back")
-            nc.scalar.copy(result[:], back[:].rearrange("p t j f -> p t (j f)"))
-            nc.scalar.dma_start(out_rows[:, 0:2, 0:HALF], result[:])
 
         def h_tile(name, width, kib=None):
             if kib is None:
@@ -316,23 +305,21 @@ def tile_attend_grbm_kernel(tc, vT, W, cf, tv, offs, foffs, out):
         h_b0 = quantise("hb0", g_b0[:], HALF)
         sig_b2 = turned_sigmoid(1, 2, [scaled_b2], (0,))
         sig_b3 = turned_sigmoid(1, 3, [scaled_b3], (3,))
-        upright = bank(4, "upright", [P, 2, HALF])
-        flipped = bank(5, "flipped", [P, 2, 2, P])
-        passes(upright, (2, 3), 0, h_a0, slice(0, HALF), True)
-        flipped_passes(flipped, 0, h_a0)
-        flipped_passes(flipped, 1, h_b0)
-        passes(upright, (2, 3), 1, h_b0, slice(0, HALF), False)
+        sums = [bank(4 + i, "sum%d" % i, [P, 2, HALF]) for i in range(2)]
+        for s, h in enumerate((h_a0, h_b0)):
+            for i in range(2):
+                passes(sums[i], (2 * i, 2 * i + 1), s, h, slice(0, HALF), s == 0)
         warm_up(0, "idle_late", y_q[0])
         g_a1 = h_tile("g_a1", HALF, 48)
         weigh_on_gpsimd(0, g_a1[:, PACK * P :], sig_a1[:, :, block(1)])
         weigh(0, g_a1[:, : PACK * P], sig_a1[:, :, block(0)])
-        emit_flipped(flipped, 2)
+        emit(sums[0][:], 0, 0)
         g_b1 = h_tile("g_b1", HALF)
         weigh(1, g_b1[:, : PACK * P], sig_b2[:])
-        weigh(1, g_b1[:, PACK * P :], sig_b3[:])
+        weigh_on_scalar(1, g_b1[:, PACK * P :], sig_b3[:])
         h_a1 = quantise("ha1", g_a1[:], HALF)
         h_b1 = quantise("hb1", g_b1[:], HALF)
-        emit(upright[:], 2, 0)
+        emit(sums[1][:], 2, 0)
         quarters = [bank(b, "quarter%d" % b, [P, PACK, P]) for b in (1, 6)]
         for i in range(2):
             passes(quarters[i], range(PACK), 0, h_a1, block(i), True)

@@ -240,10 +240,6 @@ def tile_attend_grbm_kernel(tc, vT, W, cf, tv, offs, foffs, out):
             factor = t_psum[s].rearrange("p (c t i) -> p c t i", c=1, i=1).to_broadcast([P, sig.shape[2] // 4, PACK, 4])
             nc.vector.tensor_tensor(weave(grouped), planar(sig), factor, MULT)
 
-        def weigh_on_gpsimd(s, grouped, sig):
-            factor = t_signed[s].rearrange("p (c t) -> p c t", c=1).to_broadcast([P, sig.shape[2], PACK])
-            nc.gpsimd.tensor_tensor(grouped.rearrange("p (x t) -> p x t", t=PACK), sig.rearrange("p t x -> p x t"), factor, MULT)
-
         def weigh_on_scalar(s, grouped, sig):
             rounded = keep.tile(list(sig.shape), BF16, name="h_planes")
             for r in range(PACK):
@@ -297,8 +293,7 @@ def tile_attend_grbm_kernel(tc, vT, W, cf, tv, offs, foffs, out):
         scaled_b3 = turned_scores(1, 3, 3)
         sig_a1 = turned_sigmoid(0, 2, scaled_a, (1, 6))
         g_a0 = h_tile("g_a0", HALF, 34)
-        weigh_on_gpsimd(0, g_a0[:, PACK * P :], sig_a0[:, :, block(1)])
-        weigh(0, g_a0[:, : PACK * P], sig_a0[:, :, block(0)])
+        weigh(0, g_a0[:], sig_a0[:])
         h_a0 = quantise("ha0", g_a0[:], HALF)
         g_b0 = h_tile("g_b0", HALF, 48)
         weigh(1, g_b0[:], sig_b0[:])
@@ -310,9 +305,8 @@ def tile_attend_grbm_kernel(tc, vT, W, cf, tv, offs, foffs, out):
             for i in range(2):
                 passes(sums[i], (2 * i, 2 * i + 1), s, h, slice(0, HALF), s == 0)
         warm_up(0, "idle_late", y_q[0])
-        g_a1 = h_tile("g_a1", HALF, 48)
-        weigh_on_gpsimd(0, g_a1[:, PACK * P :], sig_a1[:, :, block(1)])
-        weigh(0, g_a1[:, : PACK * P], sig_a1[:, :, block(0)])
+        g_a1 = h_tile("g_a1", HALF)
+        weigh(0, g_a1[:], sig_a1[:])
         emit(sums[0][:], 0, 0)
         g_b1 = h_tile("g_b1", HALF)
         weigh(1, g_b1[:, : PACK * P], sig_b2[:])

@@ -240,12 +240,6 @@ def tile_attend_grbm_kernel(tc, vT, W, cf, tv, offs, foffs, out):
             factor = t_psum[s].rearrange("p (c t i) -> p c t i", c=1, i=1).to_broadcast([P, sig.shape[2] // 4, PACK, 4])
             nc.vector.tensor_tensor(weave(grouped), planar(sig), factor, MULT)
 
-        def weigh_on_scalar(s, grouped, sig):
-            rounded = keep.tile(list(sig.shape), BF16, name="h_planes")
-            for r in range(PACK):
-                nc.scalar.activation(rounded[:, r, :], sig[:, r, :], COPY, scale=t_signed[s][:, r : r + 1])
-            nc.scalar.copy(weave(grouped), planar(rounded[:]))
-
         def warm_up(b, name, operand):
             idle = bank(b, name, [P, 2, 2 * P])
             for e in range(WARM_PASSES):
@@ -264,6 +258,26 @@ def tile_attend_grbm_kernel(tc, vT, W, cf, tv, offs, foffs, out):
             result = keep.tile([P, rows, width], F32, name="result%d%d" % (t0, j0))
             nc.vector.tensor_tensor(result[:], acc, cf_rows(j0, width, rows), MULT)
             nc.sync.dma_start(out_rows[:, t0 : t0 + rows, j0 * P : j0 * P + width], result[:])
+
+        def flipped_passes(flipped, i, s, h):
+            for n in range(PACK):
+                j, e = divmod(n, 2)
+                product(flipped[:, j, e, :], h, block(j), y_q[2 * i + e], block(s), s == 0 and n == 0, s == 1 and n == PACK - 1)
+
+        def scale_flipped(flipped, i, b):
+            flipped_sb = keep.tile([P, 2, 2, P], F32, name="flipped_sb%d" % i)
+            for j in range(2):
+                nc.scalar.activation(flipped_sb[:, j], flipped[:, j], COPY, scale=cf_col[:, j : j + 1])
+            back = bank(b, "back%d" % i, [P, 2, 2, P])
+            for n in range(PACK):
+                j, e = divmod(n, 2)
+                nc.tensor.transpose(back[:, e, j, :], flipped_sb[:, j, e, :], ident[:])
+            return back
+
+        def emit_back(back, i):
+            result = keep.tile([P, 2, HALF], F32, name="result_back%d" % i)
+            nc.scalar.copy(result[:], back[:].rearrange("p t j f -> p t (j f)"))
+            nc.scalar.dma_start(out_rows[:, 2 * i : 2 * i + 2, 0:HALF], result[:])
 
         def h_tile(name, width, kib=None):
             if kib is None:
@@ -300,25 +314,28 @@ def tile_attend_grbm_kernel(tc, vT, W, cf, tv, offs, foffs, out):
         h_b0 = quantise("hb0", g_b0[:], HALF)
         sig_b2 = turned_sigmoid(1, 2, [scaled_b2], (0,))
         sig_b3 = turned_sigmoid(1, 3, [scaled_b3], (3,))
-        sums = [bank(4 + i, "sum%d" % i, [P, 2, HALF]) for i in range(2)]
+        flipped = [bank(4 + i, "flipped%d" % i, [P, 2, 2, P]) for i in range(2)]
         for s, h in enumerate((h_a0, h_b0)):
             for i in range(2):
-                passes(sums[i], (2 * i, 2 * i + 1), s, h, slice(0, HALF), s == 0)
+                flipped_passes(flipped[i], i, s, h)
         warm_up(0, "idle_late", y_q[0])
         g_a1 = h_tile("g_a1", HALF)
         weigh(0, g_a1[:], sig_a1[:])
-        emit(sums[0][:], 0, 0)
-        g_b1 = h_tile("g_b1", HALF)
-        weigh(1, g_b1[:, : PACK * P], sig_b2[:])
-        weigh_on_scalar(1, g_b1[:, PACK * P :], sig_b3[:])
+        backs = [scale_flipped(flipped[i], i, 2 + i) for i in range(2)]
+        for i in range(2):
+            emit_back(backs[i], i)
+        g_b2 = h_tile("g_b2", P)
+        weigh(1, g_b2[:], sig_b2[:])
         h_a1 = quantise("ha1", g_a1[:], HALF)
-        h_b1 = quantise("hb1", g_b1[:], HALF)
-        emit(sums[1][:], 2, 0)
+        h_b2 = quantise("hb2", g_b2[:], P)
+        g_b3 = h_tile("g_b3", P)
+        weigh(1, g_b3[:], sig_b3[:])
+        h_b3 = quantise("hb3", g_b3[:], P)
         quarters = [bank(b, "quarter%d" % b, [P, PACK, P]) for b in (1, 6)]
-        for i in range(2):
-            passes(quarters[i], range(PACK), 0, h_a1, block(i), True)
-        for i in range(2):
-            passes(quarters[i], range(PACK), 1, h_b1, block(i), False)
+        passes(quarters[0], range(PACK), 0, h_a1, block(0), True)
+        passes(quarters[0], range(PACK), 1, h_b2, block(0), False)
+        passes(quarters[1], range(PACK), 0, h_a1, block(1), True)
+        passes(quarters[1], range(PACK), 1, h_b3, block(0), False)
         emit(quarters[0][:], 0, 2)
         emit(quarters[1][:, :2, :], 0, 3)
         emit(quarters[1][:, 2:, :], 2, 3)

@@ -187,7 +187,6 @@ def tile_attend_grbm_kernel(tc, vT, W, cf, tv, offs, foffs, out):
         gather(1)
         y_bank1 = turn(1, 4)
         turned0 = empty_turn(y_bank0, placed(8, "turned0", words, F32))
-        y_q.append(quantise_turn(0, turned0))
         gather(2)
         y_bank2 = turn(2, 5, (1, 0))
         turned1 = empty_turn(y_bank1, placed(16, "turned1", words, F32))
@@ -221,13 +220,12 @@ def tile_attend_grbm_kernel(tc, vT, W, cf, tv, offs, foffs, out):
             return cf_sb[:, j0 * P : j0 * P + width].rearrange("p (e f) -> p e f", e=1).to_broadcast([P, count, width])
 
         def direct_scores(s, j0, homes):
-            scaled = keep.tile([P, PACK, len(homes) * P], F32, name="direct%d%d" % (s, j0))
+            scaled = keep.tile([P, PACK, HALF], F32, name="direct%d%d" % (s, j0))
             for i, b in enumerate(homes):
-                j = j0 + i
-                score = bank(b, "dscore%d%d" % (s, j), [P, PACK, P])
-                for r in range(PACK):
-                    product(score[:, r, :], x_q[s], block(r), w_q[j // 2], block(j % 2))
-                nc.vector.tensor_tensor(scaled[:, :, block(i)], score[:], cf_rows(j, P, PACK), MULT)
+                score = bank(b, "dscore%d%d" % (s, i), [P, 2, HALF])
+                for e in range(2):
+                    product(score[:, e, :], x_q[s], block(2 * i + e), w_q[j0 // 2], slice(0, HALF))
+                nc.vector.tensor_tensor(scaled[:, 2 * i : 2 * i + 2, :], score[:], cf_rows(j0, HALF, 2), MULT)
             return scaled
 
         def direct_sigmoid(s, j0, scaled):
@@ -286,13 +284,14 @@ def tile_attend_grbm_kernel(tc, vT, W, cf, tv, offs, foffs, out):
 
         w_grouped0 = w_group(nc.scalar.copy, 0, placed(10, "w_grouped0", [P, PACK * HALF], BF16))
         w_q = [quantise("w0", w_grouped0[:], HALF)]
-        y_q.append(quantise_turn(1, turned1, placed(24, "y1_codes", [P, 2 * P], U32)))
+        y_q.append(quantise_turn(0, turned0, placed(24, "y0_codes", [P, 2 * P], U32)))
         x_q = [quantise("x0", grouped_x[0][:], SLOTS)]
+        y_q.append(quantise_turn(1, turned1, placed(32, "y1_codes", [P, 2 * P], U32)))
         grouped_x.append(placed(10, "x_grouped1", [P, PACK * SLOTS], BF16))
         weave_planes(1, PACK, grouped_x[1])
-        turned2 = empty_turn(y_bank2, placed(32, "turned2", words, F32))
+        turned2 = empty_turn(y_bank2, placed(33, "turned2", words, F32))
         w_grouped1 = w_group(nc.scalar.copy, 1, keep.tile([P, PACK * HALF], BF16, name="w_grouped1", align_bytes=64))
-        turned3 = turn_last(6, placed(34, "turned3", words, F32))
+        turned3 = turn_last(6, placed(35, "turned3", words, F32))
         direct_a = direct_scores(0, 0, (0, 1))
         warm_up(6, "idle_early", y_q[0])
         w_q.append(quantise("w1", w_grouped1[:], HALF))
@@ -306,12 +305,18 @@ def tile_attend_grbm_kernel(tc, vT, W, cf, tv, offs, foffs, out):
         sig_b0 = direct_sigmoid(1, 0, direct_b)
         scaled_b3 = turned_scores(1, 3, 3)
         sig_a1 = turned_sigmoid(0, 2, scaled_a, (1, 6))
-        g_a0 = h_tile("g_a0", HALF, 34)
-        weigh(0, g_a0[:], sig_a0[:])
-        h_a0 = quantise("ha0", g_a0[:], HALF)
-        g_b0 = h_tile("g_b0", HALF, 48)
-        weigh(1, g_b0[:], sig_b0[:])
-        h_b0 = quantise("hb0", g_b0[:], HALF)
+        g_a0 = [h_tile("g_a%d" % j, P, 35 + j) for j in range(2)]
+        h_a0 = mx_tiles("ha0", HALF)
+        for j in range(2):
+            weigh(0, g_a0[j][:], sig_a0[:, :, block(j)])
+        for j in range(2):
+            quantise_into(h_a0, block(j), g_a0[j][:])
+        g_b0 = [h_tile("g_b%d" % j, P) for j in range(2)]
+        h_b0 = mx_tiles("hb0", HALF)
+        for j in range(2):
+            weigh(1, g_b0[j][:], sig_b0[:, :, block(j)])
+        for j in range(2):
+            quantise_into(h_b0, block(j), g_b0[j][:])
         sig_b2 = turned_sigmoid(1, 2, [scaled_b2], (0,))
         sig_b3 = turned_sigmoid(1, 3, [scaled_b3], (3,))
         flipped = [bank(4 + i, "flipped%d" % i, [P, 2, 2, P]) for i in range(2)]
@@ -319,7 +324,7 @@ def tile_attend_grbm_kernel(tc, vT, W, cf, tv, offs, foffs, out):
             for i in range(2):
                 flipped_passes(flipped[i], i, s, h)
         warm_up(0, "idle_late", y_q[0])
-        g_a1 = h_tile("g_a1", HALF)
+        g_a1 = h_tile("g_a23", HALF)
         weigh(0, g_a1[:], sig_a1[:])
         backs = [scale_flipped(flipped[i], i, 2 + i) for i in range(2)]
         for i in range(2):
@@ -331,11 +336,15 @@ def tile_attend_grbm_kernel(tc, vT, W, cf, tv, offs, foffs, out):
         g_b3 = h_tile("g_b3", P)
         weigh(1, g_b3[:], sig_b3[:])
         h_b3 = quantise("hb3", g_b3[:], P)
-        quarters = [bank(b, "quarter%d" % b, [P, PACK, P]) for b in (1, 6)]
-        passes(quarters[0], range(PACK), 0, h_a1, block(0), True)
-        passes(quarters[0], range(PACK), 1, h_b2, block(0), False)
-        passes(quarters[1], range(PACK), 0, h_a1, block(1), True)
-        passes(quarters[1], range(PACK), 1, h_b3, block(0), False)
-        emit(quarters[0][:], 0, 2)
-        emit(quarters[1][:, :2, :], 0, 3)
-        emit(quarters[1][:, 2:, :], 2, 3)
+        third = bank(1, "third", [P, PACK, P])
+        passes(third, range(PACK), 0, h_a1, block(0), True)
+        passes(third, range(PACK), 1, h_b2, block(0), False)
+        last = [bank(b, "last%d" % b, [P, 2, P]) for b in (6, 4)]
+        for i in range(2):
+            passes(last[i], (2 * i, 2 * i + 1), 0, h_a1, block(1), True)
+        for i in range(2):
+            passes(last[i], (2 * i, 2 * i + 1), 1, h_b3, block(0), False)
+        for i in range(2):
+            emit(third[:, 2 * i : 2 * i + 2, :], 2 * i, 2)
+        for i in range(2):
+            emit(last[i][:], 2 * i, 3)

@@ -21,7 +21,6 @@ F = 512
 SLOTS = 512
 T = 2048
 HALF = F // 2
-WARM_PASSES = 4
 T_STEP = 16
 FLOPS = 4 * 2 * D * F * SLOTS
 
@@ -182,7 +181,6 @@ def tile_attend_grbm_kernel(tc, vT, W, cf, tv, offs, foffs, out):
         nc.vector.tensor_copy(t_all[:, 3, :], cf_bank[:, :, P - 1])
         cf_col = t_all[:, 3, :]
         t_plain = [t_all[:, 0, :], t_all[:, 2, :]]
-        t_signed = [t_all[:, 0, :], t_all[:, 1, :]]
         y_bank0 = turn(0, 3)
         gather(1)
         y_bank1 = turn(1, 4)
@@ -219,28 +217,27 @@ def tile_attend_grbm_kernel(tc, vT, W, cf, tv, offs, foffs, out):
         def cf_rows(j0, width, count):
             return cf_sb[:, j0 * P : j0 * P + width].rearrange("p (e f) -> p e f", e=1).to_broadcast([P, count, width])
 
-        def direct_scores(s, j0, homes):
-            scaled = keep.tile([P, PACK, HALF], F32, name="direct%d%d" % (s, j0))
-            for i, b in enumerate(homes):
-                score = bank(b, "dscore%d%d" % (s, i), [P, 2, HALF])
-                for e in range(2):
-                    product(score[:, e, :], x_q[s], block(2 * i + e), w_q[j0 // 2], slice(0, HALF))
-                nc.vector.tensor_tensor(scaled[:, 2 * i : 2 * i + 2, :], score[:], cf_rows(j0, HALF, 2), MULT)
+        def direct_scores(s, i, b, kib):
+            score = bank(b, "dscore%d%d" % (s, i), [P, 2, HALF])
+            for e in range(2):
+                product(score[:, e, :], x_q[s], block(2 * i + e), w_q[0], slice(0, HALF))
+            scaled = placed(kib, "direct%d%d" % (s, i), [P, 2, HALF], F32)
+            nc.vector.tensor_tensor(scaled[:], score[:], cf_rows(0, HALF, 2), MULT)
             return scaled
 
-        def direct_sigmoid(s, j0, scaled):
-            sig = keep.tile(list(scaled.shape), F32, name="sig%d%d" % (s, j0))
+        def direct_sigmoid(s, scaled):
+            sig = keep.tile([P, PACK, HALF], F32, name="sig%d0" % s)
             for r in range(PACK):
-                nc.scalar.activation(sig[:, r, :], scaled[:, r, :], SIGMOID, scale=t_plain[s][:, r : r + 1])
+                nc.scalar.activation(sig[:, r, :], scaled[r // 2][:, r % 2, :], SIGMOID, scale=t_plain[s][:, r : r + 1])
             return sig
 
         def weigh(s, grouped, sig):
             factor = t_psum[s].rearrange("p (c t i) -> p c t i", c=1, i=1).to_broadcast([P, sig.shape[2] // 4, PACK, 4])
             nc.vector.tensor_tensor(weave(grouped), planar(sig), factor, MULT)
 
-        def warm_up(b, name, operand):
+        def warm_up(b, name, operand, count):
             idle = bank(b, name, [P, 2, 2 * P])
-            for e in range(WARM_PASSES):
+            for e in range(count):
                 product(idle[:, e % 2, :], operand, block(0), operand, slice(0, 2 * P))
 
         def passes(acc, planes_of, s, h, h_cols, opens):
@@ -251,16 +248,18 @@ def tile_attend_grbm_kernel(tc, vT, W, cf, tv, offs, foffs, out):
 
         out_rows = out.rearrange("(p t) f -> p t f", t=PACK)
 
-        def emit(acc, t0, j0):
+        def emit(acc, t0, j0, kib):
             rows, width = acc.shape[1], acc.shape[2]
-            result = keep.tile([P, rows, width], F32, name="result%d%d" % (t0, j0))
+            result = placed(kib, "result%d%d" % (t0, j0), [P, rows, width], F32)
             nc.vector.tensor_tensor(result[:], acc, cf_rows(j0, width, rows), MULT)
             nc.sync.dma_start(out_rows[:, t0 : t0 + rows, j0 * P : j0 * P + width], result[:])
 
-        def flipped_passes(flipped, i, s, h):
-            for n in range(PACK):
-                j, e = divmod(n, 2)
-                product(flipped[:, j, e, :], h, block(j), y_q[2 * i + e], block(s), s == 0 and n == 0, s == 1 and n == PACK - 1)
+        def flipped_passes(flipped, s, j, h):
+            for i in range(2):
+                for e in range(2):
+                    first = s == 0 and j == 0 and e == 0
+                    last = s == 1 and j == 1 and e == 1
+                    product(flipped[i][:, j, e, :], h, block(j), y_q[2 * i + e], block(s), first, last)
 
         def scale_flipped(flipped, i, b):
             flipped_sb = keep.tile([P, 2, 2, P], F32, name="flipped_sb%d" % i)
@@ -292,50 +291,53 @@ def tile_attend_grbm_kernel(tc, vT, W, cf, tv, offs, foffs, out):
         turned2 = empty_turn(y_bank2, placed(33, "turned2", words, F32))
         w_grouped1 = w_group(nc.scalar.copy, 1, keep.tile([P, PACK * HALF], BF16, name="w_grouped1", align_bytes=64))
         turned3 = turn_last(6, placed(35, "turned3", words, F32))
-        direct_a = direct_scores(0, 0, (0, 1))
-        warm_up(6, "idle_early", y_q[0])
+        direct_a = [direct_scores(0, 0, 0, 52)]
+        warm_up(6, "idle_early", y_q[0], 2)
         w_q.append(quantise("w1", w_grouped1[:], HALF))
+        direct_a.append(direct_scores(0, 1, 1, 54))
         x_q.append(quantise("x1", grouped_x[1][:], SLOTS))
         y_q.append(quantise_turn(2, turned2))
-        y_q.append(quantise_turn(3, turned3))
-        sig_a0 = direct_sigmoid(0, 0, direct_a)
+        sig_a0 = direct_sigmoid(0, direct_a)
         scaled_a = [turned_scores(0, 2, 4), turned_scores(0, 3, 5)]
-        direct_b = direct_scores(1, 0, (2, 3))
-        scaled_b2 = turned_scores(1, 2, 0)
-        sig_b0 = direct_sigmoid(1, 0, direct_b)
-        scaled_b3 = turned_scores(1, 3, 3)
-        sig_a1 = turned_sigmoid(0, 2, scaled_a, (1, 6))
-        g_a0 = [h_tile("g_a%d" % j, P, 35 + j) for j in range(2)]
+        direct_b = [direct_scores(1, i, 2 + i, 48 + 2 * i) for i in range(2)]
+        g_a0 = [h_tile("g_a%d" % j, P) for j in range(2)]
         h_a0 = mx_tiles("ha0", HALF)
-        for j in range(2):
-            weigh(0, g_a0[j][:], sig_a0[:, :, block(j)])
-        for j in range(2):
-            quantise_into(h_a0, block(j), g_a0[j][:])
+        weigh(0, g_a0[0][:], sig_a0[:, :, block(0)])
+        y_q.append(quantise_turn(3, turned3))
+        quantise_into(h_a0, block(0), g_a0[0][:])
+        weigh(0, g_a0[1][:], sig_a0[:, :, block(1)])
+        scaled_b2 = turned_scores(1, 2, 0)
+        sig_b0 = direct_sigmoid(1, direct_b)
+        scaled_b3 = turned_scores(1, 3, 3)
+        warm_up(3, "idle_middle", y_q[0], 1)
+        sig_a1 = turned_sigmoid(0, 2, scaled_a, (1, 6))
         g_b0 = [h_tile("g_b%d" % j, P) for j in range(2)]
         h_b0 = mx_tiles("hb0", HALF)
-        for j in range(2):
-            weigh(1, g_b0[j][:], sig_b0[:, :, block(j)])
+        weigh(1, g_b0[0][:], sig_b0[:, :, block(0)])
+        quantise_into(h_a0, block(1), g_a0[1][:])
+        weigh(1, g_b0[1][:], sig_b0[:, :, block(1)])
         for j in range(2):
             quantise_into(h_b0, block(j), g_b0[j][:])
         sig_b2 = turned_sigmoid(1, 2, [scaled_b2], (0,))
         sig_b3 = turned_sigmoid(1, 3, [scaled_b3], (3,))
         flipped = [bank(4 + i, "flipped%d" % i, [P, 2, 2, P]) for i in range(2)]
         for s, h in enumerate((h_a0, h_b0)):
-            for i in range(2):
-                flipped_passes(flipped[i], i, s, h)
-        warm_up(0, "idle_late", y_q[0])
-        g_a1 = h_tile("g_a23", HALF)
-        weigh(0, g_a1[:], sig_a1[:])
+            for j in range(2):
+                flipped_passes(flipped, s, j, h)
+        g_a1 = [h_tile("g_a%d" % (2 + j), P, 50 + j) for j in range(2)]
+        h_a1 = mx_tiles("ha1", HALF)
+        g_b1 = [h_tile("g_b%d" % (2 + j), P, 56 + j) for j in range(2)]
+        weigh(0, g_a1[0][:], sig_a1[:, :, block(0)])
+        weigh(1, g_b1[0][:], sig_b2[:])
+        quantise_into(h_a1, block(0), g_a1[0][:])
+        weigh(0, g_a1[1][:], sig_a1[:, :, block(1)])
+        h_b2 = quantise("hb2", g_b1[0][:], P)
         backs = [scale_flipped(flipped[i], i, 2 + i) for i in range(2)]
         for i in range(2):
             emit_back(backs[i], i)
-        g_b2 = h_tile("g_b2", P)
-        weigh(1, g_b2[:], sig_b2[:])
-        h_a1 = quantise("ha1", g_a1[:], HALF)
-        h_b2 = quantise("hb2", g_b2[:], P)
-        g_b3 = h_tile("g_b3", P)
-        weigh(1, g_b3[:], sig_b3[:])
-        h_b3 = quantise("hb3", g_b3[:], P)
+        weigh(1, g_b1[1][:], sig_b3[:])
+        quantise_into(h_a1, block(1), g_a1[1][:])
+        h_b3 = quantise("hb3", g_b1[1][:], P)
         third = bank(1, "third", [P, PACK, P])
         passes(third, range(PACK), 0, h_a1, block(0), True)
         passes(third, range(PACK), 1, h_b2, block(0), False)
@@ -345,6 +347,6 @@ def tile_attend_grbm_kernel(tc, vT, W, cf, tv, offs, foffs, out):
         for i in range(2):
             passes(last[i], (2 * i, 2 * i + 1), 1, h_b3, block(0), False)
         for i in range(2):
-            emit(third[:, 2 * i : 2 * i + 2, :], 2 * i, 2)
+            emit(third[:, 2 * i : 2 * i + 2, :], 2 * i, 2, (51, 57)[i])
         for i in range(2):
-            emit(last[i][:], 2 * i, 3)
+            emit(last[i][:], 2 * i, 3, 58 + i)

@@ -132,8 +132,8 @@ def tile_attend_grbm_kernel(tc, vT, W, cf, tv, offs, foffs, out):
 
         def weave_planes(s, count, grouped, r0=0, places=PACK):
             nc.vector.tensor_copy(
-                grouped[:].rearrange("p (r k m t) -> p k t m r", r=places, m=2, t=PACK)[:, :, :count],
-                picked[s][:].rearrange("p (t k m r) -> p k t m r", t=count, m=2, r=PACK)[:, :, :, :, r0 : r0 + places],
+                grouped[:].rearrange("p (r k m t) -> p r k t m", r=places, m=2, t=PACK)[:, :, :, :count],
+                picked[s][:].rearrange("p (t k m r) -> p r k t m", t=count, m=2, r=PACK)[:, r0 : r0 + places],
             )
 
         def turn(t, b, order=(0, 1)):

@@ -66,10 +66,10 @@ def tile_attend_grbm_kernel(tc, vT, W, cf, tv, offs, foffs, out):
             )
 
         def weave(ap):
-            return ap.rearrange("p (c i t) -> p c t i", i=4, t=PACK)
+            return ap.rearrange("p (c i t) -> p c t i", i=2, t=PACK)
 
         def planar(ap):
-            return ap.rearrange("p t (c i) -> p c t i", i=4)
+            return ap.rearrange("p t (c i) -> p c t i", i=2)
 
         tv_sb = keep.tile([P, T], F32, name="tv_sb")
         nc.scalar.dma_start(tv_sb[P - 1 :, :], tv[0:1, :])
@@ -232,7 +232,7 @@ def tile_attend_grbm_kernel(tc, vT, W, cf, tv, offs, foffs, out):
             return sig
 
         def weigh(s, grouped, sig):
-            factor = t_psum[s].rearrange("p (c t i) -> p c t i", c=1, i=1).to_broadcast([P, sig.shape[2] // 4, PACK, 4])
+            factor = t_psum[s].rearrange("p (c t i) -> p c t i", c=1, i=1).to_broadcast([P, sig.shape[2] // 2, PACK, 2])
             nc.vector.tensor_tensor(weave(grouped), planar(sig), factor, MULT)
 
         def warm_up(b, name, operand, count):

@@ -21,7 +21,7 @@ F = 512
 SLOTS = 512
 T = 2048
 HALF = F // 2
-T_STEP = 16
+T_STEP = 1
 FLOPS = 4 * 2 * D * F * SLOTS
 
 
@@ -33,7 +33,7 @@ def tile_attend_grbm_kernel(tc, vT, W, cf, tv, offs, foffs, out):
         shared = ctx.enter_context(tc.tile_pool(name="shared", bufs=1))
 
         def placed(kib, name, shape, dtype):
-            return shared.tile(shape, dtype, name=name, offset=kib * 1024, align_bytes=64)
+            return shared.tile(shape, dtype, name=name, offset=int(kib * 1024), align_bytes=64)
 
         def bank(b, name, shape):
             return psum.tile(shape, F32, name=name, tag="bank%d" % b)
@@ -94,9 +94,9 @@ def tile_attend_grbm_kernel(tc, vT, W, cf, tv, offs, foffs, out):
             planes.append(plane)
         w_rows = W.rearrange("(p t) f -> p t f", t=PACK)
         w_raw = []
-        for h in range(2):
-            raw = placed(32 + 4 * h, "w_raw%d" % h, [P, PACK, HALF], F32)
-            nc.sync.dma_start(raw[:], w_rows[:, :, h * HALF : (h + 1) * HALF])
+        for n, (f0, width) in enumerate(((0, HALF), (HALF, P), (HALF + P, P))):
+            raw = placed(32 + f0 // 64, "w_raw%d" % n, [P, PACK, width], F32)
+            nc.sync.dma_start(raw[:], w_rows[:, :, f0 : f0 + width])
             w_raw.append(raw)
         cf_sb = keep.tile([P, F], F32, name="cf_sb")
         nc.sync.dma_start(cf_sb[:], cf)
@@ -132,8 +132,8 @@ def tile_attend_grbm_kernel(tc, vT, W, cf, tv, offs, foffs, out):
 
         def weave_planes(s, count, grouped, r0=0, places=PACK):
             nc.vector.tensor_copy(
-                grouped[:].rearrange("p (r k m t) -> p r k t m", r=places, m=2, t=PACK)[:, :, :, :count],
-                picked[s][:].rearrange("p (t k m r) -> p r k t m", t=count, m=2, r=PACK)[:, r0 : r0 + places],
+                grouped[:].rearrange("p (r k m t) -> p k r t m", r=places, m=2, t=PACK)[:, :, :, :count],
+                picked[s][:].rearrange("p (t k m r) -> p k r t m", t=count, m=2, r=PACK)[:, :, r0 : r0 + places],
             )
 
         def turn(t, b, order=(0, 1)):
@@ -145,7 +145,10 @@ def tile_attend_grbm_kernel(tc, vT, W, cf, tv, offs, foffs, out):
             return y_bank
 
         def empty_turn(y_bank, turned):
-            nc.scalar.copy(turned[:].rearrange("p (s x u) -> p s x u", s=2, u=2), y_bank[:].rearrange("p s u x -> p s x u"))
+            nc.scalar.copy(
+                turned[:].rearrange("p (s c i u) -> p s c u i", s=2, i=2, u=2),
+                y_bank[:].rearrange("p s u (c i) -> p s c u i", i=2),
+            )
             return turned
 
         def turn_last(b, turned):
@@ -158,10 +161,12 @@ def tile_attend_grbm_kernel(tc, vT, W, cf, tv, offs, foffs, out):
             for u in range(2):
                 nc.tensor.transpose(y_bank[:, 1, block(u)], pairs[:, u::2], ident[:])
             nc.scalar.copy(
-                turned[:, : 2 * P].bitcast(BF16).rearrange("p (x r) -> p x r", r=PACK), halves.rearrange("p r x -> p x r")
+                turned[:, : 2 * P].bitcast(BF16).rearrange("p (c i r) -> p c r i", i=2, r=PACK),
+                halves.rearrange("p r (c i) -> p c r i", i=2),
             )
             nc.scalar.copy(
-                turned[:, 2 * P :].rearrange("p (x u) -> p x u", u=2), y_bank[:, 1, :].rearrange("p (u x) -> p x u", u=2)
+                turned[:, 2 * P :].rearrange("p (c i u) -> p c u i", i=2, u=2),
+                y_bank[:, 1, :].rearrange("p (u c i) -> p c u i", u=2, i=2),
             )
             return turned
 
@@ -274,28 +279,35 @@ def tile_attend_grbm_kernel(tc, vT, W, cf, tv, offs, foffs, out):
         def emit_back(back, i):
             result = keep.tile([P, 2, HALF], F32, name="result_back%d" % i)
             nc.scalar.copy(result[:], back[:].rearrange("p t j f -> p t (j f)"))
-            nc.scalar.dma_start(out_rows[:, 2 * i : 2 * i + 2, 0:HALF], result[:])
+            queue = (nc.sync, nc.scalar)[i]
+            queue.dma_start(out_rows[:, 2 * i : 2 * i + 2, 0:HALF], result[:])
 
         def h_tile(name, width, kib=None):
             if kib is None:
                 return keep.tile([P, PACK * width], BF16, name=name, align_bytes=64)
             return placed(kib, name, [P, PACK * width], BF16)
 
+        x_first = keep.tile([P, PACK * P], BF16, name="x_grouped1_first", align_bytes=64)
+        weave_planes(1, PACK, x_first, 0, 1)
         w_grouped0 = w_group(nc.scalar.copy, 0, placed(10, "w_grouped0", [P, PACK * HALF], BF16))
         w_q = [quantise("w0", w_grouped0[:], HALF)]
         y_q.append(quantise_turn(0, turned0, placed(24, "y0_codes", [P, 2 * P], U32)))
-        x_q = [quantise("x0", grouped_x[0][:], SLOTS)]
-        y_q.append(quantise_turn(1, turned1, placed(32, "y1_codes", [P, 2 * P], U32)))
-        grouped_x.append(placed(10, "x_grouped1", [P, PACK * SLOTS], BF16))
-        weave_planes(1, PACK, grouped_x[1])
-        turned2 = empty_turn(y_bank2, placed(33, "turned2", words, F32))
-        w_grouped1 = w_group(nc.scalar.copy, 1, keep.tile([P, PACK * HALF], BF16, name="w_grouped1", align_bytes=64))
-        turned3 = turn_last(6, placed(35, "turned3", words, F32))
+        x_q = [quantise("x0", grouped_x[0][:], SLOTS, placed(26, "x0_codes", [P, SLOTS], U32))]
+        y_q.append(quantise_turn(1, turned1, placed(31.5, "y1_codes", [P, 2 * P], U32)))
+        grouped_x.append(placed(10, "x_grouped1", [P, (PACK - 1) * SLOTS], BF16))
+        weave_planes(1, PACK, grouped_x[1], 1, PACK - 1)
+        w_grouped1 = keep.tile([P, PACK * HALF], BF16, name="w_grouped1", align_bytes=64)
+        for j in range(2):
+            nc.scalar.copy(weave(w_grouped1[:, j * PACK * P : (j + 1) * PACK * P]), planar(w_raw[1 + j][:]))
+        turned2 = empty_turn(y_bank2, placed(32.5, "turned2", words, F32))
+        turned3 = turn_last(6, placed(34.5, "turned3", words, F32))
         direct_a = [direct_scores(0, 0, 0, 52)]
         warm_up(6, "idle_early", y_q[0], 2)
         w_q.append(quantise("w1", w_grouped1[:], HALF))
         direct_a.append(direct_scores(0, 1, 1, 54))
-        x_q.append(quantise("x1", grouped_x[1][:], SLOTS))
+        x_q.append(mx_tiles("x1", SLOTS))
+        quantise_into(x_q[1], block(0), x_first[:])
+        quantise_into(x_q[1], slice(P, SLOTS), grouped_x[1][:])
         y_q.append(quantise_turn(2, turned2))
         sig_a0 = direct_sigmoid(0, direct_a)
         scaled_a = [turned_scores(0, 2, 4), turned_scores(0, 3, 5)]

@@ -123,6 +123,12 @@ def tile_attend_grbm_kernel(tc, vT, W, cf, tv, offs, foffs, out):
             return picked[s][:, t * SLOTS : (t + 1) * SLOTS]
 
         def gather(t):
+            if t == PACK - 2:
+                for half in range(2):
+                    to = picked_plane(0, t)[:, half * HALF : (half + 1) * HALF]
+                    nc.vector.tensor_copy(to, planes[t][:].indirect(lists[0][:, half * 16 : (half + 1) * 16]))
+                nc.scalar.activation(picked_plane(1, t), planes[t][:].indirect(lists[1][:]), COPY)
+                return
             if t < PACK - 1:
                 to = picked_plane(0, t)
             else:
@@ -130,10 +136,10 @@ def tile_attend_grbm_kernel(tc, vT, W, cf, tv, offs, foffs, out):
             nc.vector.tensor_copy(to, planes[t][:].indirect(lists[0][:]))
             nc.scalar.activation(picked_plane(1, t), planes[t][:].indirect(lists[1][:]), COPY)
 
-        def weave_planes(s, count, grouped, r0=0, places=PACK):
+        def weave_planes(s, count, grouped, r0=0, places=PACK, runs=slice(0, SLOTS // 8)):
             nc.vector.tensor_copy(
-                grouped[:].rearrange("p (r k m t) -> p k r t m", r=places, m=2, t=PACK)[:, :, :, :count],
-                picked[s][:].rearrange("p (t k m r) -> p k r t m", t=count, m=2, r=PACK)[:, :, r0 : r0 + places],
+                grouped[:].rearrange("p (r k m t) -> p k r t m", r=places, m=2, t=PACK)[:, runs, :, :count],
+                picked[s][:].rearrange("p (t k m r) -> p k r t m", t=count, m=2, r=PACK)[:, runs, r0 : r0 + places],
             )
 
         def turn(t, b, order=(0, 1)):
@@ -193,7 +199,8 @@ def tile_attend_grbm_kernel(tc, vT, W, cf, tv, offs, foffs, out):
         gather(2)
         y_bank2 = turn(2, 5, (1, 0))
         turned1 = empty_turn(y_bank1, placed(16, "turned1", words, F32))
-        weave_planes(0, PACK - 1, grouped_x[0])
+        for half in range(2):
+            weave_planes(0, PACK - 1, grouped_x[0], runs=slice(32 * half, 32 * (half + 1)))
         gather(3)
 
         def turned_scores(s, j, b, scaled=None):
@@ -277,10 +284,11 @@ def tile_attend_grbm_kernel(tc, vT, W, cf, tv, offs, foffs, out):
             return back
 
         def emit_back(back, i):
-            result = keep.tile([P, 2, HALF], F32, name="result_back%d" % i)
-            nc.scalar.copy(result[:], back[:].rearrange("p t j f -> p t (j f)"))
-            queue = (nc.sync, nc.scalar)[i]
-            queue.dma_start(out_rows[:, 2 * i : 2 * i + 2, 0:HALF], result[:])
+            rows = back[:].rearrange("p t j f -> p t (j f)")
+            for t0, count, queue in ((0, 1, (nc.sync, nc.scalar)[i]), (1, 1, (nc.sync, nc.scalar)[i])):
+                result = keep.tile([P, count, HALF], F32, name="result_back%d%d" % (i, t0))
+                nc.scalar.copy(result[:], rows[:, t0 : t0 + count, :])
+                queue.dma_start(out_rows[:, 2 * i + t0 : 2 * i + t0 + count, 0:HALF], result[:])
 
         def h_tile(name, width, kib=None):
             if kib is None:
@@ -344,19 +352,19 @@ def tile_attend_grbm_kernel(tc, vT, W, cf, tv, offs, foffs, out):
         quantise_into(h_a1, block(0), g_a1[0][:])
         weigh(0, g_a1[1][:], sig_a1[:, :, block(1)])
         h_b2 = quantise("hb2", g_b1[0][:], P)
-        backs = [scale_flipped(flipped[i], i, 2 + i) for i in range(2)]
+        backs = [scale_flipped(flipped[0], 0, 2)]
+        third = bank(1, "third", [P, PACK, P])
+        passes(third, range(PACK), 0, h_a1, block(0), True)
+        passes(third, range(PACK), 1, h_b2, block(0), False)
+        backs.append(scale_flipped(flipped[1], 1, 3))
         for i in range(2):
             emit_back(backs[i], i)
         weigh(1, g_b1[1][:], sig_b3[:])
         quantise_into(h_a1, block(1), g_a1[1][:])
         h_b3 = quantise("hb3", g_b1[1][:], P)
-        third = bank(1, "third", [P, PACK, P])
-        passes(third, range(PACK), 0, h_a1, block(0), True)
-        passes(third, range(PACK), 1, h_b2, block(0), False)
         last = [bank(b, "last%d" % b, [P, 2, P]) for b in (6, 4)]
         for i in range(2):
             passes(last[i], (2 * i, 2 * i + 1), 0, h_a1, block(1), True)
-        for i in range(2):
             passes(last[i], (2 * i, 2 * i + 1), 1, h_b3, block(0), False)
         for i in range(2):
             emit(third[:, 2 * i : 2 * i + 2, :], 2 * i, 2, (51, 57)[i])

@@ -323,18 +323,17 @@ def tile_attend_grbm_kernel(tc, vT, W, cf, tv, offs, foffs, out):
         g_a0 = [h_tile("g_a%d" % j, P) for j in range(2)]
         h_a0 = mx_tiles("ha0", HALF)
         weigh(0, g_a0[0][:], sig_a0[:, :, block(0)])
-        y_q.append(quantise_turn(3, turned3))
-        quantise_into(h_a0, block(0), g_a0[0][:])
         weigh(0, g_a0[1][:], sig_a0[:, :, block(1)])
+        quantise_into(h_a0, block(0), g_a0[0][:])
+        y_q.append(quantise_turn(3, turned3))
+        quantise_into(h_a0, block(1), g_a0[1][:])
         scaled_b2 = turned_scores(1, 2, 0)
         sig_b0 = direct_sigmoid(1, direct_b)
         scaled_b3 = turned_scores(1, 3, 3)
-        warm_up(3, "idle_middle", y_q[0], 1)
         sig_a1 = turned_sigmoid(0, 2, scaled_a, (1, 6))
         g_b0 = [h_tile("g_b%d" % j, P) for j in range(2)]
         h_b0 = mx_tiles("hb0", HALF)
         weigh(1, g_b0[0][:], sig_b0[:, :, block(0)])
-        quantise_into(h_a0, block(1), g_a0[1][:])
         weigh(1, g_b0[1][:], sig_b0[:, :, block(1)])
         for j in range(2):
             quantise_into(h_b0, block(j), g_b0[j][:])
@@ -344,6 +343,7 @@ def tile_attend_grbm_kernel(tc, vT, W, cf, tv, offs, foffs, out):
         for s, h in enumerate((h_a0, h_b0)):
             for j in range(2):
                 flipped_passes(flipped, s, j, h)
+        warm_up(6, "idle_late", h_b0, 1)
         g_a1 = [h_tile("g_a%d" % (2 + j), P, 50 + j) for j in range(2)]
         h_a1 = mx_tiles("ha1", HALF)
         g_b1 = [h_tile("g_b%d" % (2 + j), P, 56 + j) for j in range(2)]

from contextlib import ExitStack

import concourse.mybir as mybir
from concourse.masks import make_identity

F32 = mybir.dt.float32
BF16 = mybir.dt.bfloat16
U32 = mybir.dt.uint32
U16 = mybir.dt.uint16
U8 = mybir.dt.uint8
FP8X4 = mybir.dt.float8_e4m3fn_x4
MULT = mybir.AluOpType.mult
ADD = mybir.AluOpType.add
COPY = mybir.ActivationFunctionType.Copy
SIGMOID = mybir.ActivationFunctionType.Sigmoid

P = 128
PACK = 4
D = 512
F = 512
SLOTS = 512
T = 2048
HALF = F // 2
T_STEP = 1
FLOPS = 4 * 2 * D * F * SLOTS


def tile_attend_grbm_kernel(tc, vT, W, cf, tv, offs, foffs, out):
    nc = tc.nc
    with ExitStack() as ctx:
        keep = ctx.enter_context(tc.tile_pool(name="keep", bufs=1))
        psum = ctx.enter_context(tc.psum_pool(name="psum", bufs=1))
        shared = ctx.enter_context(tc.tile_pool(name="shared", bufs=1))

        def placed(kib, name, shape, dtype):
            return shared.tile(shape, dtype, name=name, offset=int(kib * 1024), align_bytes=64)

        def bank(b, name, shape):
            return psum.tile(shape, F32, name=name, tag="bank%d" % b)

        def block(j):
            return slice(j * P, (j + 1) * P)

        def mx_tiles(name, width, codes=None):
            if codes is None:
                codes = keep.tile([P, width], U32, name=name + "_codes", align_bytes=64)
            return codes, keep.tile([P, width], U8, name=name + "_scales", align_bytes=64)

        def quantise_into(operand, cols, grouped):
            nc.vector.quantize_mx(out=operand[0][:, cols].bitcast(FP8X4), scales=operand[1][:, cols], in_=grouped)

        def quantise(name, grouped, width, codes=None):
            operand = mx_tiles(name, width, codes)
            quantise_into(operand, slice(0, width), grouped)
            return operand

        def product(acc, stationary, s_cols, moving, m_cols, start=True, stop=True):
            nc.tensor.matmul_mx(
                out=acc,
                lhsT=stationary[0][:, s_cols].bitcast(FP8X4),
                lhsT_scale=stationary[1][:, s_cols],
                rhs=moving[0][:, m_cols].bitcast(FP8X4),
                rhs_scale=moving[1][:, m_cols],
                start=start,
                stop=stop,
            )

        def weave(ap):
            return ap.rearrange("p (c i t) -> p c t i", i=2, t=PACK)

        def planar(ap):
            return ap.rearrange("p t (c i) -> p c t i", i=2)

        tv_sb = keep.tile([P, T], F32, name="tv_sb")
        nc.scalar.dma_start(tv_sb[P - 1 :, :], tv[0:1, :])
        lists = []
        for name, src in (("offs", offs), ("foffs", foffs)):
            tile = keep.tile([P, SLOTS // 16], U16, name=name + "_sb")
            nc.sync.dma_start(tile[:], src)
            lists.append(tile)
        cf_row = keep.tile([P, F], F32, name="cf_row")
        nc.scalar.dma_start(cf_row[P - 1 :, :], cf[0:1, :])
        nc.vector.memset(tv_sb[: P - 1, :], 0.0)
        ident = keep.tile([P, P], F32, name="ident")
        make_identity(nc, ident[:])
        nc.gpsimd.memset(cf_row[: P - 1, :], 0.0)
        warm = keep.tile([P, 1], F32, name="warm")
        nc.scalar.activation(warm[:64, :], tv_sb[:64, 0:1], SIGMOID)
        vT_planes = vT.rearrange("(p t) x -> t p x", t=PACK)
        planes = []
        for t in range(PACK):
            plane = placed(8 * t, "plane%d" % t, [P, T], F32)
            nc.sync.dma_start(plane[:], vT_planes[t])
            planes.append(plane)
        w_rows = W.rearrange("(p t) f -> p t f", t=PACK)
        w_raw = []
        for n, (f0, width) in enumerate(((0, HALF), (HALF, P), (HALF + P, P))):
            raw = placed(32 + f0 // 64, "w_raw%d" % n, [P, PACK, width], F32)
            nc.sync.dma_start(raw[:], w_rows[:, :, f0 : f0 + width])
            w_raw.append(raw)
        cf_sb = keep.tile([P, F], F32, name="cf_sb")
        nc.sync.dma_start(cf_sb[:], cf)

        cf_bank = bank(0, "cf_bank", [P, PACK, P])
        for j in range(PACK):
            nc.tensor.transpose(cf_bank[:, j, :], cf_row[:, block(j)], ident[:])

        tv_picked = [keep.tile([P, SLOTS], F32, name="tv_picked%d" % s) for s in range(2)]
        nc.scalar.activation(tv_picked[0][:], tv_sb[:].indirect(lists[0][:]), COPY)
        nc.vector.tensor_scalar(tv_picked[1][:], tv_sb[:].indirect(lists[1][:]), -1.0, 0.0, MULT, ADD)
        t_bank = bank(7, "t_bank", [P, SLOTS])
        for k in reversed(range(2 * PACK)):
            nc.tensor.transpose(t_bank[:, T_STEP * k : T_STEP * k + P], tv_picked[k // PACK][:, k % PACK :: PACK], ident[:])
        t_columns = t_bank[:, P - 1 : P - 1 + 2 * PACK * T_STEP : T_STEP]
        t_psum = [t_columns[:, s * PACK : (s + 1) * PACK] for s in range(2)]

        picked = [placed(44 - 4 * s, "picked%d" % s, [P, (PACK - 1 + s) * SLOTS], BF16) for s in range(2)]
        grouped_x = [keep.tile([P, PACK * SLOTS], BF16, name="x_grouped0", align_bytes=64)]
        ident_bf = keep.tile([P, P], BF16, name="ident_bf")
        nc.gpsimd.tensor_copy(ident_bf[:], ident[:])

        def picked_plane(s, t):
            return picked[s][:, t * SLOTS : (t + 1) * SLOTS]

        def gather(t):
            if t == PACK - 2:
                for half in range(2):
                    to = picked_plane(0, t)[:, half * HALF : (half + 1) * HALF]
                    nc.vector.tensor_copy(to, planes[t][:].indirect(lists[0][:, half * 16 : (half + 1) * 16]))
                nc.scalar.activation(picked_plane(1, t), planes[t][:].indirect(lists[1][:]), COPY)
                return
            if t < PACK - 1:
                to = picked_plane(0, t)
            else:
                to = grouped_x[0][:].rearrange("p (r c t) -> p c r t", r=PACK, t=PACK)[:, :, :, t]
            nc.vector.tensor_copy(to, planes[t][:].indirect(lists[0][:]))
            nc.scalar.activation(picked_plane(1, t), planes[t][:].indirect(lists[1][:]), COPY)

        def weave_planes(s, count, grouped, r0=0, places=PACK, runs=slice(0, SLOTS // 8)):
            nc.vector.tensor_copy(
                grouped[:].rearrange("p (r k m t) -> p k r t m", r=places, m=2, t=PACK)[:, runs, :, :count],
                picked[s][:].rearrange("p (t k m r) -> p k r t m", t=count, m=2, r=PACK)[:, runs, r0 : r0 + places],
            )

        def turn(t, b, order=(0, 1)):
            y_bank = bank(b, "y_bank%d" % t, [P, 2, 2, P])
            for s in order:
                pairs = picked_plane(s, t).bitcast(F32)
                for u in range(2):
                    nc.tensor.transpose(y_bank[:, s, u, :], pairs[:, u::2], ident[:])
            return y_bank

        def empty_turn(y_bank, turned):
            nc.scalar.copy(
                turned[:].rearrange("p (s c i u) -> p s c u i", s=2, i=2, u=2),
                y_bank[:].rearrange("p s u (c i) -> p s c u i", i=2),
            )
            return turned

        def turn_last(b, turned):
            y_bank = bank(b, "y_bank3", [P, 2, 2 * P])
            halves = y_bank[:, 0, :].bitcast(BF16).rearrange("p (r x) -> p r x", r=PACK)
            last = grouped_x[0][:].rearrange("p (r c t) -> p r c t", r=PACK, t=PACK)
            for r in range(PACK):
                nc.tensor.transpose(halves[:, r, :], last[:, r, :, PACK - 1], ident_bf[:])
            pairs = picked_plane(1, PACK - 1).bitcast(F32)
            for u in range(2):
                nc.tensor.transpose(y_bank[:, 1, block(u)], pairs[:, u::2], ident[:])
            nc.scalar.copy(
                turned[:, : 2 * P].bitcast(BF16).rearrange("p (c i r) -> p c r i", i=2, r=PACK),
                halves.rearrange("p r (c i) -> p c r i", i=2),
            )
            nc.scalar.copy(
                turned[:, 2 * P :].rearrange("p (c i u) -> p c u i", i=2, u=2),
                y_bank[:, 1, :].rearrange("p (u c i) -> p c u i", u=2, i=2),
            )
            return turned

        def quantise_turn(t, turned, codes=None):
            return quantise("y%d" % t, turned[:].bitcast(BF16), 2 * P, codes)

        def w_group(copy, h, grouped):
            copy(weave(grouped[:]), planar(w_raw[h][:]))
            return grouped

        words = [P, 2 * 2 * P]
        y_q = []
        gather(0)
        t_all = placed(0, "t_all", [P, 4, PACK], F32)
        nc.vector.tensor_copy(t_all[:, :2, :].rearrange("p s r -> p (s r)"), t_columns)
        nc.vector.tensor_scalar(t_all[:, 2, :], t_psum[1], -1.0, None, MULT)
        nc.vector.tensor_copy(t_all[:, 3, :], cf_bank[:, :, P - 1])
        cf_col = t_all[:, 3, :]
        t_plain = [t_all[:, 0, :], t_all[:, 2, :]]
        y_bank0 = turn(0, 3)
        gather(1)
        y_bank1 = turn(1, 4)
        turned0 = empty_turn(y_bank0, placed(8, "turned0", words, F32))
        gather(2)
        y_bank2 = turn(2, 5, (1, 0))
        turned1 = empty_turn(y_bank1, placed(16, "turned1", words, F32))
        for half in range(2):
            weave_planes(0, PACK - 1, grouped_x[0], runs=slice(32 * half, 32 * (half + 1)))
        gather(3)

        def turned_scores(s, j, b, scaled=None):
            score = bank(b, "score%d%d" % (s, j), [P, SLOTS])
            product(score[:], w_q[j // 2], block(j % 2), x_q[s], slice(0, SLOTS))
            if scaled is None:
                scaled = keep.tile([P, SLOTS], F32, name="scaled%d%d" % (s, j))
            nc.scalar.activation(scaled[:], score[:], COPY, scale=cf_col[:, j : j + 1])
            return scaled

        def turned_sigmoid(s, j0, scaled, homes, between=None):
            nj = len(scaled)
            width = nj * P
            per_bank = PACK // nj
            logits = [bank(b, "logit%d%d%d" % (s, j0, b), [P, per_bank, width]) for b in homes]
            for jj in range(nj):
                for r in range(PACK):
                    nc.tensor.transpose(logits[r // per_bank][:, r % per_bank, block(jj)], scaled[jj][:, block(r)], ident[:])
            if between is not None:
                between()
            sig = keep.tile([P, PACK, width], F32, name="sig%d%d" % (s, j0))
            for r in range(PACK):
                nc.scalar.activation(sig[:, r, :], logits[r // per_bank][:, r % per_bank, :], SIGMOID, scale=t_plain[s][:, r : r + 1])
            return sig

        def cf_rows(j0, width, count):
            return cf_sb[:, j0 * P : j0 * P + width].rearrange("p (e f) -> p e f", e=1).to_broadcast([P, count, width])

        def direct_scores(s, i, b, kib):
            score = bank(b, "dscore%d%d" % (s, i), [P, 2, HALF])
            for e in range(2):
                product(score[:, e, :], x_q[s], block(2 * i + e), w_q[0], slice(0, HALF))
            scaled = placed(kib, "direct%d%d" % (s, i), [P, 2, HALF], F32)
            nc.vector.tensor_tensor(scaled[:], score[:], cf_rows(0, HALF, 2), MULT)
            return scaled

        def direct_sigmoid(s, scaled):
            sig = keep.tile([P, PACK, HALF], F32, name="sig%d0" % s)
            for r in range(PACK):
                nc.scalar.activation(sig[:, r, :], scaled[r // 2][:, r % 2, :], SIGMOID, scale=t_plain[s][:, r : r + 1])
            return sig

        def weigh(s, grouped, sig):
            factor = t_psum[s].rearrange("p (c t i) -> p c t i", c=1, i=1).to_broadcast([P, sig.shape[2] // 2, PACK, 2])
            nc.vector.tensor_tensor(weave(grouped), planar(sig), factor, MULT)

        def warm_up(b, name, operand, count):
            idle = bank(b, name, [P, 2, 2 * P])
            for e in range(count):
                product(idle[:, e % 2, :], operand, block(0), operand, slice(0, 2 * P))

        def passes(acc, planes_of, s, h, h_cols, opens):
            for e, t in enumerate(planes_of):
                first = opens and e == 0
                last = not opens and e == len(planes_of) - 1
                product(acc[:, e, :], y_q[t], block(s), h, h_cols, first, last)

        out_rows = out.rearrange("(p t) f -> p t f", t=PACK)

        def emit(acc, t0, j0, kib):
            rows, width = acc.shape[1], acc.shape[2]
            result = placed(kib, "result%d%d" % (t0, j0), [P, rows, width], F32)
            nc.vector.tensor_tensor(result[:], acc, cf_rows(j0, width, rows), MULT)
            nc.sync.dma_start(out_rows[:, t0 : t0 + rows, j0 * P : j0 * P + width], result[:])

        def flipped_passes(flipped, s, j, h):
            for i in range(2):
                for e in range(2):
                    first = s == 0 and j == 0 and e == 0
                    last = s == 1 and j == 1 and e == 1
                    product(flipped[i][:, j, e, :], h, block(j), y_q[2 * i + e], block(s), first, last)

        def scale_flipped(flipped, i, b):
            flipped_sb = keep.tile([P, 2, 2, P], F32, name="flipped_sb%d" % i)
            for j in range(2):
                nc.scalar.activation(flipped_sb[:, j], flipped[:, j], COPY, scale=cf_col[:, j : j + 1])
            back = bank(b, "back%d" % i, [P, 2, 2, P])
            for n in range(PACK):
                j, e = divmod(n, 2)
                nc.tensor.transpose(back[:, e, j, :], flipped_sb[:, j, e, :], ident[:])
            return back

        def emit_back(back, i):
            rows = back[:].rearrange("p t j f -> p t (j f)")
            for t0, count, queue in ((0, 1, (nc.sync, nc.scalar)[i]), (1, 1, (nc.sync, nc.scalar)[i])):
                result = keep.tile([P, count, HALF], F32, name="result_back%d%d" % (i, t0))
                nc.scalar.copy(result[:], rows[:, t0 : t0 + count, :])
                queue.dma_start(out_rows[:, 2 * i + t0 : 2 * i + t0 + count, 0:HALF], result[:])

        def h_tile(name, width, kib=None):
            if kib is None:
                return keep.tile([P, PACK * width], BF16, name=name, align_bytes=64)
            return placed(kib, name, [P, PACK * width], BF16)

        x_first = keep.tile([P, PACK * P], BF16, name="x_grouped1_first", align_bytes=64)
        weave_planes(1, PACK, x_first, 0, 1)
        w_grouped0 = w_group(nc.scalar.copy, 0, placed(10, "w_grouped0", [P, PACK * HALF], BF16))
        w_q = [quantise("w0", w_grouped0[:], HALF)]
        y_q.append(quantise_turn(0, turned0, placed(24, "y0_codes", [P, 2 * P], U32)))
        x_q = [quantise("x0", grouped_x[0][:], SLOTS, placed(26, "x0_codes", [P, SLOTS], U32))]
        y_q.append(quantise_turn(1, turned1, placed(31.5, "y1_codes", [P, 2 * P], U32)))
        grouped_x.append(placed(10, "x_grouped1", [P, (PACK - 1) * SLOTS], BF16))
        weave_planes(1, PACK, grouped_x[1], 1, PACK - 1)
        w_grouped1 = keep.tile([P, PACK * HALF], BF16, name="w_grouped1", align_bytes=64)
        for j in range(2):
            nc.scalar.copy(weave(w_grouped1[:, j * PACK * P : (j + 1) * PACK * P]), planar(w_raw[1 + j][:]))
        turned2 = empty_turn(y_bank2, placed(32.5, "turned2", words, F32))
        turned3 = turn_last(6, placed(34.5, "turned3", words, F32))
        direct_a = [direct_scores(0, 0, 0, 52)]
        warm_up(6, "idle_early", y_q[0], 2)
        w_q.append(quantise("w1", w_grouped1[:], HALF))
        direct_a.append(direct_scores(0, 1, 1, 54))
        x_q.append(mx_tiles("x1", SLOTS))
        quantise_into(x_q[1], block(0), x_first[:])
        quantise_into(x_q[1], slice(P, SLOTS), grouped_x[1][:])
        y_q.append(quantise_turn(2, turned2))
        sig_a0 = direct_sigmoid(0, direct_a)
        scaled_a = [turned_scores(0, 2, 4), turned_scores(0, 3, 5)]
        direct_b = [direct_scores(1, i, 2 + i, 48 + 2 * i) for i in range(2)]
        g_a0 = [h_tile("g_a%d" % j, P) for j in range(2)]
        h_a0 = mx_tiles("ha0", HALF)
        weigh(0, g_a0[0][:], sig_a0[:, :, block(0)])
        weigh(0, g_a0[1][:], sig_a0[:, :, block(1)])
        quantise_into(h_a0, block(0), g_a0[0][:])
        y_q.append(quantise_turn(3, turned3))
        quantise_into(h_a0, block(1), g_a0[1][:])
        scaled_b2 = turned_scores(1, 2, 0)
        sig_b0 = direct_sigmoid(1, direct_b)
        scaled_b3 = turned_scores(1, 3, 3)
        sig_a1 = turned_sigmoid(0, 2, scaled_a, (1, 6))
        g_b0 = [h_tile("g_b%d" % j, P) for j in range(2)]
        h_b0 = mx_tiles("hb0", HALF)
        weigh(1, g_b0[0][:], sig_b0[:, :, block(0)])
        weigh(1, g_b0[1][:], sig_b0[:, :, block(1)])
        for j in range(2):
            quantise_into(h_b0, block(j), g_b0[j][:])
        sig_b2 = turned_sigmoid(1, 2, [scaled_b2], (0,))
        sig_b3 = turned_sigmoid(1, 3, [scaled_b3], (3,))
        flipped = [bank(4 + i, "flipped%d" % i, [P, 2, 2, P]) for i in range(2)]
        for s, h in enumerate((h_a0, h_b0)):
            for j in range(2):
                flipped_passes(flipped, s, j, h)
        warm_up(6, "idle_late", h_b0, 1)
        g_a1 = [h_tile("g_a%d" % (2 + j), P, 50 + j) for j in range(2)]
        h_a1 = mx_tiles("ha1", HALF)
        g_b1 = [h_tile("g_b%d" % (2 + j), P, 56 + j) for j in range(2)]
        weigh(0, g_a1[0][:], sig_a1[:, :, block(0)])
        weigh(1, g_b1[0][:], sig_b2[:])
        quantise_into(h_a1, block(0), g_a1[0][:])
        weigh(0, g_a1[1][:], sig_a1[:, :, block(1)])
        h_b2 = quantise("hb2", g_b1[0][:], P)
        backs = [scale_flipped(flipped[0], 0, 2)]
        third = bank(1, "third", [P, PACK, P])
        passes(third, range(PACK), 0, h_a1, block(0), True)
        passes(third, range(PACK), 1, h_b2, block(0), False)
        backs.append(scale_flipped(flipped[1], 1, 3))
        for i in range(2):
            emit_back(backs[i], i)
        weigh(1, g_b1[1][:], sig_b3[:])
        quantise_into(h_a1, block(1), g_a1[1][:])
        h_b3 = quantise("hb3", g_b1[1][:], P)
        last = [bank(b, "last%d" % b, [P, 2, P]) for b in (6, 4)]
        for i in range(2):
            passes(last[i], (2 * i, 2 * i + 1), 0, h_a1, block(1), True)
            passes(last[i], (2 * i, 2 * i + 1), 1, h_b3, block(0), False)
        for i in range(2):
            emit(third[:, 2 * i : 2 * i + 2, :], 2 * i, 2, (51, 57)[i])
        for i in range(2):
            emit(last[i][:], 2 * i, 3, 58 + i)
